import numpy as np
import ml_dtypes


def mxq(x, axis, fmt="e4m3"):
    dtype, down = {"e4m3": (ml_dtypes.float8_e4m3fn, 7), "e5m2": (ml_dtypes.float8_e5m2, 14)}[fmt]
    v = np.moveaxis(np.asarray(x, np.float32).astype(ml_dtypes.bfloat16).astype(np.float64), axis, -1)
    blocks = v.reshape(v.shape[:-1] + (-1, 32))
    amax = np.abs(blocks).max(-1, keepdims=True)
    byte = np.maximum(np.where(amax > 0, np.frexp(amax)[1] - 1 + 127, 0) - down, 1)
    scale = np.exp2(byte - 127.0)
    codes = (blocks / scale).astype(np.float32).astype(dtype).astype(np.float64)
    return np.moveaxis((codes * scale).reshape(v.shape), -1, axis)


WIDE = False


def mx_kscale(k):
    if not WIDE:
        return np.ones(k)
    levels = np.array([10, -10, 5, -5, 0])
    if k % 512:
        return np.exp2(np.random.permutation(np.resize(levels, k // 32))).repeat(32)
    a = np.empty((k // 512, 16))
    for p in range(k // 512):
        a[p, :8] = np.random.permutation(np.resize(levels, 8))
        for g in range(8):
            far = levels[np.abs(levels - a[p, g]) >= 10]
            a[p, g + 8] = far[np.random.randint(len(far))]
    return np.exp2(a.ravel()).repeat(32)


def f64(x):
    return np.asarray(x).astype(np.float64)


def striped(idx):
    return np.tile(idx.reshape(-1, 16).T, (8, 1)).astype(np.uint16)


def unstriped(offs):
    return offs[:16].T.reshape(-1).astype(np.int64)


E2M1 = np.array([0.0, 0.5, 1.0, 1.5, 2.0, 3.0, 4.0, 6.0, -0.0, -0.5, -1.0, -1.5, -2.0, -3.0, -4.0, -6.0])


def pack_weight(w, fmt):
    k, n = w.shape
    w = f64(np.asarray(w, np.float32).astype(ml_dtypes.bfloat16)).reshape(k // 32, 32, n)
    amax = np.abs(w).max(1)
    if fmt == "e4m3":
        byte = np.frexp(amax)[1] - 1 + 127 - 7
    else:
        mant, ex = np.frexp(amax / 6.0)
        byte = np.where(mant > 0.5, ex, ex - 1) + 127
    byte = np.clip(np.where(amax > 0, byte, 1), 1, 254)
    scaled = (w * np.exp2(127.0 - byte)[:, None, :]).reshape(k, n).astype(np.float32)
    by_word = np.ascontiguousarray(scaled.reshape(k // 512, 128, 4, n).transpose(0, 1, 3, 2))
    if fmt == "e4m3":
        words = by_word.astype(ml_dtypes.float8_e4m3fn).view(np.uint8)
    else:
        c = by_word.astype(ml_dtypes.float4_e2m1fn).view(np.uint8) & 0xF
        words = (c[..., 0::2] | (c[..., 1::2] << 4)).reshape(k // 512, 128, 2 * n)
    return np.ascontiguousarray(words), np.ascontiguousarray(byte.astype(np.uint8).reshape(k // 512, 16, n))


def unpack_weight(words, scales, fmt):
    g, _, n = scales.shape
    words = np.ascontiguousarray(words).reshape(g, 128, n, -1)
    if fmt == "e4m3":
        vals = words.view(ml_dtypes.float8_e4m3fn).astype(np.float64)
    else:
        nib = np.empty((g, 128, n, 4), np.uint8)
        nib[..., 0::2] = words & 0xF
        nib[..., 1::2] = words >> 4
        vals = E2M1[nib]
    vals = vals * np.repeat(np.exp2(scales.astype(np.float64) - 127.0), 8, axis=1)[..., None]
    return vals.transpose(0, 1, 3, 2).reshape(g * 512, n)


def gelu(v):
    return 0.5 * v * (1.0 + np.tanh(np.sqrt(2.0 / np.pi) * (v + 0.044715 * v**3)))


K, T, S, T2, P, H, N = 1024, 4096, 1024, 2048, 1024, 1024, 512

def setup_inputs():
    n = np.random.standard_normal
    s = mx_kscale(K)[:, None]
    u = mx_kscale(H)[:, None]
    tab_words, tab_scales = pack_weight(n((K, T)) * s, "e4m3")
    w2_words, w2_scales = pack_weight(n((H, N)) / np.sqrt(H) / u, "e2m1")
    return {
        "tab_words": tab_words, "tab_scales": tab_scales,
        "offs": striped(np.random.permutation(T)[:S]),
        "w1": (n((K, H)) / np.sqrt(K) / s * u.T).astype(np.float32),
        "b1": (0.5 * n(H) * u[:, 0]).astype(np.float32),
        "wgs": np.exp(0.3 * n((128, S))).astype(np.float32),
        "offs2": striped(np.random.permutation(T2)[:S]),
        "offs3": striped(np.random.permutation(T2)[:P]),
        "offs4": striped(np.random.permutation(T2)[:P]),
        "bstep": (0.8 * n((H, P)) * u).astype(np.float32),
        "w2_words": w2_words, "w2_scales": w2_scales,
        "le": np.exp(0.3 * n(P)).astype(np.float32),
    }

def reference(tab_words, tab_scales, offs, w1, b1, wgs, offs2, offs3, offs4, bstep, w2_words, w2_scales, le):
    v = unpack_weight(tab_words, tab_scales, "e4m3")[:, unstriped(offs)]
    h = (mxq(f64(w1), 0, "e4m3").T @ v) + f64(b1)[:, None]
    page = np.zeros((H, T2))
    page[:, unstriped(offs2)] = np.tile(f64(wgs), (H // 128, 1)) * h
    x1 = page[:, unstriped(offs3)]
    x2 = page[:, unstriped(offs4)]
    z = x2 - x1 + f64(bstep)
    w2 = unpack_weight(w2_words, w2_scales, "e2m1")
    y = w2.T @ mxq(z, 0, "e4m3")
    return y * f64(le)[None, :]

@@ -1,0 +1,246 @@
+from contextlib import ExitStack
+
+import concourse.mybir as mybir
+
+K, T, S, T2, E, H, N = 1024, 4096, 1024, 2048, 1024, 1024, 512
+FLOPS = 2 * K * H * S + 2 * H * N * E
+
+F32 = mybir.dt.float32
+BF16 = mybir.dt.bfloat16
+I32 = mybir.dt.int32
+U32 = mybir.dt.uint32
+U16 = mybir.dt.uint16
+U8 = mybir.dt.uint8
+FP8X4 = mybir.dt.float8_e4m3fn_x4
+FP4X4 = mybir.dt.float4_e2m1fn_x4
+MULT = mybir.AluOpType.mult
+SUB = mybir.AluOpType.subtract
+IDENT = mybir.ActivationFunctionType.Identity
+
+P = 128
+KIB = 1024
+HALF = 512
+CHUNKS = (512, 256, 128, 128)
+
+
+def tile_list_tsunami_edge_fluxes_kernel(
+    tc, tab_words, tab_scales, offs, w1, b1, wgs, offs2, offs3, offs4, bstep, w2_words, w2_scales, le, out
+):
+    nc = tc.nc
+    with ExitStack() as ctx:
+        lists = ctx.enter_context(tc.tile_pool(name="lists", bufs=1))
+        keep = ctx.enter_context(tc.tile_pool(name="keep", bufs=1))
+        shared = ctx.enter_context(tc.tile_pool(name="shared", bufs=1))
+        ring = ctx.enter_context(tc.tile_pool(name="ring", bufs=2))
+        psum = ctx.enter_context(tc.psum_pool(name="psum", bufs=4))
+
+        idx = lists.tile([P, S // 16], U16, name="idx")
+        idx2 = lists.tile([P, S // 16], U16, name="idx2")
+        idx3 = lists.tile([P, E // 16], U16, name="idx3")
+        idx4 = lists.tile([P, E // 16], U16, name="idx4")
+
+        tab = [shared.tile([P, T], I32, name="tab%d" % a, offset=16 * KIB * a) for a in range(2)]
+        w1_nat = [shared.tile([P, 2, 4, P], F32, name="w1_nat%d" % i, offset=(32 + 4 * i) * KIB) for i in range(4)]
+        w1_hi = shared.tile([P, 2, 4, HALF], F32, name="w1_hi", offset=48 * KIB)
+
+        tab_sc = shared.tile([P, T], U8, name="tab_sc", offset=64 * KIB)
+        v_words = [
+            shared.tile([P, S], U32, name="v_words%d" % a, align_bytes=64, offset=place * KIB)
+            for a, place in enumerate((68, 64))
+        ]
+        v_sc = keep.tile([P, S], U8, name="v_sc", align_bytes=64)
+        pages = [
+            shared.tile([P, T2], F32, name="page%d" % i, offset=place * KIB) for i, place in enumerate((72, 80, 0, 8))
+        ]
+        bias_lo = keep.tile([P, 4], F32, name="bias_lo")
+        bias_hi = keep.tile([P, 4], F32, name="bias_hi")
+        wgs_lo = keep.tile([P, S], F32, name="wgs_lo")
+        bstep_lo = [keep.tile([P, E], F32, name="bstep_lo%d" % i) for i in range(4)]
+        w2_w = keep.tile([P, 2, 2 * N], U8, name="w2_w", align_bytes=64)
+        w2_sc = keep.tile([P, 2, N], U8, name="w2_sc", align_bytes=64)
+        le_all = keep.tile([P, E], F32, name="le_all")
+
+        def load_w1_nat(i):
+            for a in range(2):
+                rows = w1[HALF * a : HALF * (a + 1), P * i : P * (i + 1)]
+                nc.sync.dma_start(out=w1_nat[i][:, a], in_=rows.rearrange("(p j) c -> p j c", j=4))
+
+        def load_tab(a):
+            nc.sync.dma_start(out=tab[a][:], in_=tab_words[a].rearrange("p t i -> p (t i)").bitcast(I32))
+
+        nc.vector.memset(tab_sc[:].bitcast(I32), 0)
+        for q in range(4):
+            nc.gpsimd.dma_start(
+                out=tab_sc[32 * q : 32 * q + 8, :].bitcast(I32),
+                in_=tab_scales[:, 4 * q : 4 * q + 4, :].bitcast(I32),
+            )
+        for i in range(2):
+            nc.vector.memset(pages[i][:], 0.0)
+        nc.vector.memset(w2_sc[:].rearrange("p a c -> p (a c)").bitcast(I32), 0)
+
+        load_tab(0)
+        nc.sync.dma_start(idx[:], offs)
+        load_w1_nat(0)
+        load_tab(1)
+        nc.sync.dma_start(out=wgs_lo[:], in_=wgs)
+        nc.sync.dma_start(idx2[:], offs2)
+        with nc.allow_non_contiguous_dma(reason="one bias value a partition"):
+            nc.sync.dma_start(out=bias_lo[:], in_=b1[0:HALF].rearrange("(i p) -> p i", p=P))
+        load_w1_nat(1)
+        nc.sync.dma_start(idx3[:], offs3)
+        nc.sync.dma_start(idx4[:], offs4)
+        nc.sync.dma_start(out=bstep_lo[0][:], in_=bstep[0:P, :])
+        load_w1_nat(2)
+        nc.sync.dma_start(out=bstep_lo[1][:], in_=bstep[P : 2 * P, :])
+        load_w1_nat(3)
+        for i in (2, 3):
+            nc.sync.dma_start(out=bstep_lo[i][:], in_=bstep[P * i : P * (i + 1), :])
+        for a in range(2):
+            rows = w1[HALF * a : HALF * (a + 1), HALF:H]
+            nc.sync.dma_start(out=w1_hi[:, a], in_=rows.rearrange("(p j) c -> p j c", j=4))
+        nc.sync.dma_start(out=bias_hi[:], in_=b1[HALF:H].rearrange("(p t) -> p t", t=4))
+
+        nc.vector.tensor_copy(out=v_sc[:], in_=tab_sc[:].indirect(idx[:]))
+        nc.vector.tensor_copy(out=v_words[0][:], in_=tab[0][:].bitcast(U32).indirect(idx[:]))
+
+        for i in range(2, 4):
+            nc.gpsimd.memset(pages[i][:], 0.0)
+
+        def quantise_w1(src):
+            grouped = ring.tile([P, 2, P, 4], BF16, name="w1_grouped", align_bytes=64)
+            nc.scalar.activation(out=grouped[:], in_=src, func=IDENT)
+            codes = ring.tile([P, 2 * P], U32, name="w1_codes", align_bytes=64, bufs=4)
+            scales = ring.tile([P, 2 * P], U8, name="w1_scales", align_bytes=64, bufs=4)
+            nc.vector.quantize_mx(
+                out=codes[:].bitcast(FP8X4), scales=scales[:], in_=grouped[:].rearrange("p a c j -> p (a c j)")
+            )
+            return codes, scales
+
+        def make_h(codes, scales, bias):
+            h = ring.tile([P, S], F32, name="h", bufs=4)
+            for s0 in range(0, S, HALF):
+                cols = slice(s0, s0 + HALF)
+                acc = psum.tile([P, HALF], F32, name="acc_h")
+                for a in range(2):
+                    nc.tensor.matmul_mx(
+                        out=acc[:],
+                        lhsT=codes[:, P * a : P * (a + 1)].bitcast(FP8X4),
+                        lhsT_scale=scales[:, P * a : P * (a + 1)],
+                        rhs=v_words[a][:, cols].bitcast(FP8X4),
+                        rhs_scale=v_sc[4 * a : P, cols],
+                        start=(a == 0),
+                        stop=(a == 1),
+                    )
+                nc.scalar.activation(out=h[:, cols], in_=acc[:], func=IDENT, bias=bias)
+            return h
+
+        def list_cols(m0, width):
+            return slice(m0 // 16, (m0 + width) // 16)
+
+        quantised = quantise_w1(w1_nat[0][:].rearrange("p a j c -> p a c j"))
+        for s0 in range(0, S, HALF):
+            nc.vector.tensor_copy(
+                out=v_words[1][:, s0 : s0 + HALF],
+                in_=tab[1][:].bitcast(U32).indirect(idx[:, list_cols(s0, HALF)]),
+            )
+        h = make_h(quantised[0], quantised[1], bias_lo[:, 0:1])
+        for s0 in range(0, S, HALF):
+            cols = slice(s0, s0 + HALF)
+            nc.vector.tensor_tensor(
+                out=pages[0][:].indirect(idx2[:, list_cols(s0, HALF)]), in0=h[:, cols], in1=wgs_lo[:, cols], op=MULT
+            )
+        for i in range(1, 4):
+            quantised = quantise_w1(w1_nat[i][:].rearrange("p a j c -> p a c j"))
+            h = make_h(quantised[0], quantised[1], bias_lo[:, i : i + 1])
+            nc.vector.tensor_tensor(out=pages[i][:].indirect(idx2[:]), in0=h[:], in1=wgs_lo[:], op=MULT)
+
+        wgs_hi = keep.tile([P, 4, S], F32, name="wgs_hi")
+        for q in range(4):
+            nc.sync.dma_start(out=wgs_hi[32 * q : 32 * (q + 1)], in_=wgs.rearrange("(p t) j -> p t j", t=4))
+        bstep_hi = shared.tile([P, 4, E], F32, name="bstep_hi", offset=32 * KIB)
+        nc.sync.dma_start(out=bstep_hi[:], in_=bstep[HALF:H, :].rearrange("(p t) m -> p t m", t=4))
+        nc.sync.dma_start(
+            out=w2_w[:].bitcast(I32), in_=w2_words.rearrange("a p c -> p a c").bitcast(I32)
+        )
+        for q in range(4):
+            nc.sync.dma_start(
+                out=w2_sc[32 * q : 32 * q + 4].bitcast(I32),
+                in_=w2_scales[:, 4 * q : 4 * q + 4, :].rearrange("a r c -> r a c").bitcast(I32),
+            )
+        nc.sync.dma_start(out=le_all[:], in_=le.partition_broadcast(P))
+
+        h_hi = []
+        for t in range(4):
+            quantised = quantise_w1(w1_hi[:].rearrange("p a j (c t) -> p t a c j", t=4)[:, t])
+            h_hi.append(make_h(quantised[0], quantised[1], bias_hi[:, t : t + 1]))
+
+        z_lo = shared.tile([P, 4, E], F32, name="z_lo", offset=16 * KIB)
+        for i in range(4):
+            y = ring.tile([P, E], F32, name="y_lo")
+            z_nat = ring.tile([P, E], F32, name="z_nat")
+            for m0 in range(0, E, HALF):
+                cols = slice(m0, m0 + HALF)
+                nc.vector.tensor_tensor(
+                    out=y[:, cols], in0=pages[i][:].indirect(idx3[:, list_cols(m0, HALF)]), in1=bstep_lo[i][:, cols], op=SUB
+                )
+            for m0 in range(0, E, HALF):
+                cols = slice(m0, m0 + HALF)
+                nc.vector.tensor_tensor(
+                    out=z_nat[:, cols], in0=pages[i][:].indirect(idx4[:, list_cols(m0, HALF)]), in1=y[:, cols], op=SUB
+                )
+            for t in range(4):
+                nc.sync.dma_start(out=z_lo[32 * i : 32 * (i + 1), t, :], in_=z_nat[t:P:4, :])
+
+        def quantise_z(src, width, name):
+            grouped = keep.tile([P, width, 4], BF16, name="zg_" + name, align_bytes=64)
+            nc.scalar.activation(out=grouped[:], in_=src.rearrange("p t m -> p m t"), func=IDENT)
+            codes = keep.tile([P, width], U32, name="zc_" + name, align_bytes=64)
+            scales = keep.tile([P, width], U8, name="zs_" + name, align_bytes=64)
+            nc.vector.quantize_mx(
+                out=codes[:].bitcast(FP8X4), scales=scales[:], in_=grouped[:].rearrange("p m t -> p (m t)")
+            )
+            return codes, scales
+
+        for t in range(4):
+            nc.vector.tensor_tensor(out=pages[t][:].indirect(idx2[:]), in0=h_hi[t][:], in1=wgs_hi[:, t, :], op=MULT)
+        zq_lo = [quantise_z(z_lo[:, :, m0 : m0 + HALF], HALF, "lo%d" % m0) for m0 in range(0, E, HALF)]
+
+        out_v = out.rearrange("(b p) m -> p b m", p=P)
+        m0 = 0
+        for width in CHUNKS:
+            cols = slice(m0, m0 + width)
+            y = ring.tile([P, 4, width], F32, name="y_hi")
+            z_hi = shared.tile([P, 4, width], F32, name="z_hi%d" % m0, offset=48 * KIB + 16 * m0)
+            for t in range(4):
+                nc.vector.tensor_tensor(
+                    out=y[:, t, :], in0=pages[t][:].indirect(idx3[:, list_cols(m0, width)]), in1=bstep_hi[:, t, cols], op=SUB
+                )
+            for t in range(4):
+                nc.vector.tensor_tensor(
+                    out=z_hi[:, t, :], in0=pages[t][:].indirect(idx4[:, list_cols(m0, width)]), in1=y[:, t, :], op=SUB
+                )
+            zq_hi = quantise_z(z_hi[:], width, "hi%d" % m0)
+            for mb in range(m0, m0 + width, P):
+                acc = psum.tile([P, 4, P], F32, name="acc_out")
+                lo_codes, lo_scales = zq_lo[mb // HALF]
+                lo_cols = slice(mb % HALF, mb % HALF + P)
+                hi_cols = slice(mb - m0, mb - m0 + P)
+                passes = ((lo_codes, lo_scales, lo_cols), (zq_hi[0], zq_hi[1], hi_cols))
+                for b in range(4):
+                    for a in range(2):
+                        codes, scales, zcols = passes[a]
+                        nc.tensor.matmul_mx(
+                            out=acc[:, b, :],
+                            lhsT=w2_w[:, a, 2 * P * b : 2 * P * (b + 1)].bitcast(FP4X4),
+                            lhsT_scale=w2_sc[:, a, P * b : P * (b + 1)],
+                            rhs=codes[:, zcols].bitcast(FP8X4),
+                            rhs_scale=scales[:, zcols],
+                            start=(a == 0),
+                            stop=(a == 1),
+                        )
+                res = ring.tile([P, 4, P], F32, name="res", bufs=4)
+                nc.vector.tensor_tensor(
+                    out=res[:], in0=acc[:], in1=le_all[:, mb : mb + P].unsqueeze(1).to_broadcast([P, 4, P]), op=MULT
+                )
+                nc.sync.dma_start(out=out_v[:, :, mb : mb + P], in_=res[:])
+            m0 = m0 + width

@@ -20,7 +20,7 @@ IDENT = mybir.ActivationFunctionType.Identity
 P = 128
 KIB = 1024
 HALF = 512
-CHUNKS = (512, 256, 128, 128)
+CHUNKS = (512, 256, 256)
 
 
 def tile_list_tsunami_edge_fluxes_kernel(
@@ -32,7 +32,7 @@ def tile_list_tsunami_edge_fluxes_kernel(
         keep = ctx.enter_context(tc.tile_pool(name="keep", bufs=1))
         shared = ctx.enter_context(tc.tile_pool(name="shared", bufs=1))
         ring = ctx.enter_context(tc.tile_pool(name="ring", bufs=2))
-        psum = ctx.enter_context(tc.psum_pool(name="psum", bufs=4))
+        psum = ctx.enter_context(tc.psum_pool(name="psum", bufs=8))
 
         idx = lists.tile([P, S // 16], U16, name="idx")
         idx2 = lists.tile([P, S // 16], U16, name="idx2")
@@ -50,7 +50,7 @@ def tile_list_tsunami_edge_fluxes_kernel(
         ]
         v_sc = keep.tile([P, S], U8, name="v_sc", align_bytes=64)
         pages = [
-            shared.tile([P, T2], F32, name="page%d" % i, offset=place * KIB) for i, place in enumerate((72, 80, 0, 8))
+            shared.tile([P, T2], F32, name="page%d" % i, offset=place * KIB) for i, place in enumerate((72, 80, 16, 24))
         ]
         bias_lo = keep.tile([P, 4], F32, name="bias_lo")
         bias_hi = keep.tile([P, 4], F32, name="bias_hi")
@@ -95,16 +95,9 @@ def tile_list_tsunami_edge_fluxes_kernel(
         load_w1_nat(3)
         for i in (2, 3):
             nc.sync.dma_start(out=bstep_lo[i][:], in_=bstep[P * i : P * (i + 1), :])
-        for a in range(2):
-            rows = w1[HALF * a : HALF * (a + 1), HALF:H]
-            nc.sync.dma_start(out=w1_hi[:, a], in_=rows.rearrange("(p j) c -> p j c", j=4))
-        nc.sync.dma_start(out=bias_hi[:], in_=b1[HALF:H].rearrange("(p t) -> p t", t=4))
 
         nc.vector.tensor_copy(out=v_sc[:], in_=tab_sc[:].indirect(idx[:]))
         nc.vector.tensor_copy(out=v_words[0][:], in_=tab[0][:].bitcast(U32).indirect(idx[:]))
-
-        for i in range(2, 4):
-            nc.gpsimd.memset(pages[i][:], 0.0)
 
         def quantise_w1(src):
             grouped = ring.tile([P, 2, P, 4], BF16, name="w1_grouped", align_bytes=64)
@@ -120,7 +113,7 @@ def tile_list_tsunami_edge_fluxes_kernel(
             h = ring.tile([P, S], F32, name="h", bufs=4)
             for s0 in range(0, S, HALF):
                 cols = slice(s0, s0 + HALF)
-                acc = psum.tile([P, HALF], F32, name="acc_h")
+                acc = psum.tile([P, HALF], F32, name="acc_h", tag="bank")
                 for a in range(2):
                     nc.tensor.matmul_mx(
                         out=acc[:],
@@ -143,6 +136,9 @@ def tile_list_tsunami_edge_fluxes_kernel(
                 out=v_words[1][:, s0 : s0 + HALF],
                 in_=tab[1][:].bitcast(U32).indirect(idx[:, list_cols(s0, HALF)]),
             )
+        for i in range(2, 4):
+            for c0 in range(0, T2, HALF):
+                nc.gpsimd.memset(pages[i][:, c0 : c0 + HALF], 0.0)
         h = make_h(quantised[0], quantised[1], bias_lo[:, 0:1])
         for s0 in range(0, S, HALF):
             cols = slice(s0, s0 + HALF)
@@ -154,29 +150,9 @@ def tile_list_tsunami_edge_fluxes_kernel(
             h = make_h(quantised[0], quantised[1], bias_lo[:, i : i + 1])
             nc.vector.tensor_tensor(out=pages[i][:].indirect(idx2[:]), in0=h[:], in1=wgs_lo[:], op=MULT)
 
-        wgs_hi = keep.tile([P, 4, S], F32, name="wgs_hi")
-        for q in range(4):
-            nc.sync.dma_start(out=wgs_hi[32 * q : 32 * (q + 1)], in_=wgs.rearrange("(p t) j -> p t j", t=4))
-        bstep_hi = shared.tile([P, 4, E], F32, name="bstep_hi", offset=32 * KIB)
-        nc.sync.dma_start(out=bstep_hi[:], in_=bstep[HALF:H, :].rearrange("(p t) m -> p t m", t=4))
-        nc.sync.dma_start(
-            out=w2_w[:].bitcast(I32), in_=w2_words.rearrange("a p c -> p a c").bitcast(I32)
-        )
-        for q in range(4):
-            nc.sync.dma_start(
-                out=w2_sc[32 * q : 32 * q + 4].bitcast(I32),
-                in_=w2_scales[:, 4 * q : 4 * q + 4, :].rearrange("a r c -> r a c").bitcast(I32),
-            )
-        nc.sync.dma_start(out=le_all[:], in_=le.partition_broadcast(P))
+        z_lo = shared.tile([P, 4, E], F32, name="z_lo", offset=0)
 
-        h_hi = []
-        for t in range(4):
-            quantised = quantise_w1(w1_hi[:].rearrange("p a j (c t) -> p t a c j", t=4)[:, t])
-            h_hi.append(make_h(quantised[0], quantised[1], bias_hi[:, t : t + 1]))
-
-        z_lo = shared.tile([P, 4, E], F32, name="z_lo", offset=16 * KIB)
-        for i in range(4):
-            y = ring.tile([P, E], F32, name="y_lo")
+        def gather_lo(i, y):
             z_nat = ring.tile([P, E], F32, name="z_nat")
             for m0 in range(0, E, HALF):
                 cols = slice(m0, m0 + HALF)
@@ -191,8 +167,44 @@ def tile_list_tsunami_edge_fluxes_kernel(
             for t in range(4):
                 nc.sync.dma_start(out=z_lo[32 * i : 32 * (i + 1), t, :], in_=z_nat[t:P:4, :])
 
-        def quantise_z(src, width, name):
-            grouped = keep.tile([P, width, 4], BF16, name="zg_" + name, align_bytes=64)
+        for i in range(2):
+            gather_lo(i, ring.tile([P, E], F32, name="y_lo"))
+
+        for a in range(2):
+            rows = w1[HALF * a : HALF * (a + 1), HALF:H]
+            nc.sync.dma_start(out=w1_hi[:, a], in_=rows.rearrange("(p j) c -> p j c", j=4))
+        nc.sync.dma_start(out=bias_hi[:], in_=b1[HALF:H].rearrange("(p t) -> p t", t=4))
+        grouped_hi = shared.tile([P, 4, 2, P, 4], BF16, name="grouped_hi", align_bytes=64, offset=88 * KIB)
+        for t in range(4):
+            src = w1_hi[:].rearrange("p a j (c t) -> p t a c j", t=4)[:, t]
+            nc.scalar.activation(out=grouped_hi[:, t], in_=src, func=IDENT)
+        codes_hi = keep.tile([P, 4, 2 * P], U32, name="codes_hi", align_bytes=64)
+        scales_hi = keep.tile([P, 4, 2 * P], U8, name="scales_hi", align_bytes=64)
+        nc.vector.quantize_mx(
+            out=codes_hi[:].rearrange("p t c -> p (t c)").bitcast(FP8X4),
+            scales=scales_hi[:].rearrange("p t c -> p (t c)"),
+            in_=grouped_hi[:].rearrange("p t a c j -> p (t a c j)"),
+        )
+        h_hi = [make_h(codes_hi[:, t], scales_hi[:, t], bias_hi[:, t : t + 1]) for t in range(4)]
+
+        gather_lo(2, shared.tile([P, E], F32, name="y_lo2", offset=88 * KIB))
+        gather_lo(3, ring.tile([P, E], F32, name="y_lo"))
+
+        wgs_hi = keep.tile([P, 4, S], F32, name="wgs_hi")
+        for q in range(4):
+            nc.sync.dma_start(out=wgs_hi[32 * q : 32 * (q + 1)], in_=wgs.rearrange("(p t) j -> p t j", t=4))
+        nc.sync.dma_start(out=w2_w[:].bitcast(I32), in_=w2_words.rearrange("a p c -> p a c").bitcast(I32))
+        for q in range(4):
+            nc.sync.dma_start(
+                out=w2_sc[32 * q : 32 * q + 4].bitcast(I32),
+                in_=w2_scales[:, 4 * q : 4 * q + 4, :].rearrange("a r c -> r a c").bitcast(I32),
+            )
+        bstep_hi = shared.tile([P, 4, E], F32, name="bstep_hi", offset=32 * KIB)
+        nc.sync.dma_start(out=bstep_hi[:], in_=bstep[HALF:H, :].rearrange("(p t) m -> p t m", t=4))
+        nc.sync.dma_start(out=le_all[:], in_=le.partition_broadcast(P))
+
+        def quantise_z(src, grouped, name):
+            width = src.shape[2]
             nc.scalar.activation(out=grouped[:], in_=src.rearrange("p t m -> p m t"), func=IDENT)
             codes = keep.tile([P, width], U32, name="zc_" + name, align_bytes=64)
             scales = keep.tile([P, width], U8, name="zs_" + name, align_bytes=64)
@@ -203,13 +215,44 @@ def tile_list_tsunami_edge_fluxes_kernel(
 
         for t in range(4):
             nc.vector.tensor_tensor(out=pages[t][:].indirect(idx2[:]), in0=h_hi[t][:], in1=wgs_hi[:, t, :], op=MULT)
-        zq_lo = [quantise_z(z_lo[:, :, m0 : m0 + HALF], HALF, "lo%d" % m0) for m0 in range(0, E, HALF)]
+        zq_lo = []
+        for m0 in range(0, E, HALF):
+            grouped = shared.tile([P, HALF, 4], BF16, name="zg_lo%d" % m0, align_bytes=64, offset=88 * KIB + 8 * m0)
+            zq_lo.append(quantise_z(z_lo[:, :, m0 : m0 + HALF], grouped, "lo%d" % m0))
+
+        def out_pass(acc, a, width, blocks, codes, scales, z0):
+            step = HALF if width == HALF else P
+            pieces = [(k, c0) for k in range(len(blocks)) for c0 in range(0, width, step)]
+            for k, c0 in pieces:
+                b = blocks[k]
+                zcols = slice(z0 + c0, z0 + c0 + step)
+                nc.tensor.matmul_mx(
+                    out=acc[:, k, c0 : c0 + step],
+                    lhsT=w2_w[:, a, 2 * P * b : 2 * P * (b + 1)].bitcast(FP4X4),
+                    lhsT_scale=w2_sc[:, a, P * b : P * (b + 1)],
+                    rhs=codes[:, zcols].bitcast(FP8X4),
+                    rhs_scale=scales[:, zcols],
+                    start=(a == 0 and (k, c0) == pieces[0]),
+                    stop=(a == 1 and (k, c0) == pieces[-1]),
+                )
+
+        starts = [sum(CHUNKS[:c]) for c in range(len(CHUNKS))]
+        banks = []
+        for m0, width in zip(starts, CHUNKS):
+            per_bank = HALF // width
+            chunk_banks = []
+            for b0 in range(0, 4, per_bank):
+                blocks = list(range(b0, b0 + per_bank))
+                acc = psum.tile([P, per_bank, width], F32, name="acc_out", tag="bank")
+                lo_codes, lo_scales = zq_lo[m0 // HALF]
+                out_pass(acc, 0, width, blocks, lo_codes, lo_scales, m0 % HALF)
+                chunk_banks.append((acc, blocks))
+            banks.append(chunk_banks)
 
         out_v = out.rearrange("(b p) m -> p b m", p=P)
-        m0 = 0
-        for width in CHUNKS:
+        for m0, width, chunk_banks in zip(starts, CHUNKS, banks):
             cols = slice(m0, m0 + width)
-            y = ring.tile([P, 4, width], F32, name="y_hi")
+            y = shared.tile([P, 4, width], F32, name="y_hi%d" % m0, offset=88 * KIB + 16 * m0)
             z_hi = shared.tile([P, 4, width], F32, name="z_hi%d" % m0, offset=48 * KIB + 16 * m0)
             for t in range(4):
                 nc.vector.tensor_tensor(
@@ -219,28 +262,11 @@ def tile_list_tsunami_edge_fluxes_kernel(
                 nc.vector.tensor_tensor(
                     out=z_hi[:, t, :], in0=pages[t][:].indirect(idx4[:, list_cols(m0, width)]), in1=y[:, t, :], op=SUB
                 )
-            zq_hi = quantise_z(z_hi[:], width, "hi%d" % m0)
-            for mb in range(m0, m0 + width, P):
-                acc = psum.tile([P, 4, P], F32, name="acc_out")
-                lo_codes, lo_scales = zq_lo[mb // HALF]
-                lo_cols = slice(mb % HALF, mb % HALF + P)
-                hi_cols = slice(mb - m0, mb - m0 + P)
-                passes = ((lo_codes, lo_scales, lo_cols), (zq_hi[0], zq_hi[1], hi_cols))
-                for b in range(4):
-                    for a in range(2):
-                        codes, scales, zcols = passes[a]
-                        nc.tensor.matmul_mx(
-                            out=acc[:, b, :],
-                            lhsT=w2_w[:, a, 2 * P * b : 2 * P * (b + 1)].bitcast(FP4X4),
-                            lhsT_scale=w2_sc[:, a, P * b : P * (b + 1)],
-                            rhs=codes[:, zcols].bitcast(FP8X4),
-                            rhs_scale=scales[:, zcols],
-                            start=(a == 0),
-                            stop=(a == 1),
-                        )
-                res = ring.tile([P, 4, P], F32, name="res", bufs=4)
-                nc.vector.tensor_tensor(
-                    out=res[:], in0=acc[:], in1=le_all[:, mb : mb + P].unsqueeze(1).to_broadcast([P, 4, P]), op=MULT
-                )
-                nc.sync.dma_start(out=out_v[:, :, mb : mb + P], in_=res[:])
-            m0 = m0 + width
+            grouped = keep.tile([P, width, 4], BF16, name="zg_hi%d" % m0, align_bytes=64)
+            hi_codes, hi_scales = quantise_z(z_hi[:], grouped, "hi%d" % m0)
+            for acc, blocks in chunk_banks:
+                out_pass(acc, 1, width, blocks, hi_codes, hi_scales, 0)
+                res = ring.tile([P, len(blocks), width], F32, name="res", bufs=4)
+                factors = le_all[:, cols].unsqueeze(1).to_broadcast([P, len(blocks), width])
+                nc.vector.tensor_tensor(out=res[:], in0=acc[:], in1=factors, op=MULT)
+                nc.sync.dma_start(out=out_v[:, blocks[0] : blocks[-1] + 1, cols], in_=res[:])

@@ -93,24 +93,33 @@ def tile_list_tsunami_edge_fluxes_kernel(
         load_w1_nat(2)
         nc.sync.dma_start(out=bstep_lo[1][:], in_=bstep[P : 2 * P, :])
         load_w1_nat(3)
+        for a in range(2):
+            rows = w1[HALF * a : HALF * (a + 1), HALF:H]
+            nc.sync.dma_start(out=w1_hi[:, a], in_=rows.rearrange("(p j) c -> p j c", j=4))
+        nc.sync.dma_start(out=bias_hi[:], in_=b1[HALF:H].rearrange("(p t) -> p t", t=4))
         for i in (2, 3):
             nc.sync.dma_start(out=bstep_lo[i][:], in_=bstep[P * i : P * (i + 1), :])
 
         nc.vector.tensor_copy(out=v_sc[:], in_=tab_sc[:].indirect(idx[:]))
         nc.vector.tensor_copy(out=v_words[0][:], in_=tab[0][:].bitcast(U32).indirect(idx[:]))
 
-        def quantise_w1(src):
-            grouped = ring.tile([P, 2, P, 4], BF16, name="w1_grouped", align_bytes=64)
-            nc.scalar.activation(out=grouped[:], in_=src, func=IDENT)
-            codes = ring.tile([P, 2 * P], U32, name="w1_codes", align_bytes=64, bufs=4)
+        def quantise_w1(i, grouped_at, codes_at):
+            src = w1_nat[i]
+            grouped = shared.tile([P, 2, P, 4], BF16, name="w1_grouped%d" % i, align_bytes=64, offset=grouped_at * KIB)
+            for a in range(2):
+                nc.scalar.activation(
+                    out=grouped[:, a].rearrange("p (c i) j -> p c j i", i=4),
+                    in_=src[:, a].rearrange("p j (c i) -> p c j i", i=4),
+                    func=IDENT,
+                )
+            codes = shared.tile([P, 2 * P], U32, name="w1_codes%d" % i, align_bytes=64, offset=codes_at * KIB)
             scales = ring.tile([P, 2 * P], U8, name="w1_scales", align_bytes=64, bufs=4)
             nc.vector.quantize_mx(
                 out=codes[:].bitcast(FP8X4), scales=scales[:], in_=grouped[:].rearrange("p a c j -> p (a c j)")
             )
             return codes, scales
 
-        def make_h(codes, scales, bias):
-            h = ring.tile([P, S], F32, name="h", bufs=4)
+        def make_h(codes, scales, bias, h):
             for s0 in range(0, S, HALF):
                 cols = slice(s0, s0 + HALF)
                 acc = psum.tile([P, HALF], F32, name="acc_h", tag="bank")
@@ -130,7 +139,7 @@ def tile_list_tsunami_edge_fluxes_kernel(
         def list_cols(m0, width):
             return slice(m0 // 16, (m0 + width) // 16)
 
-        quantised = quantise_w1(w1_nat[0][:].rearrange("p a j c -> p a c j"))
+        quantised = quantise_w1(0, 106, 104)
         for s0 in range(0, S, HALF):
             nc.vector.tensor_copy(
                 out=v_words[1][:, s0 : s0 + HALF],
@@ -139,15 +148,15 @@ def tile_list_tsunami_edge_fluxes_kernel(
         for i in range(2, 4):
             for c0 in range(0, T2, HALF):
                 nc.gpsimd.memset(pages[i][:, c0 : c0 + HALF], 0.0)
-        h = make_h(quantised[0], quantised[1], bias_lo[:, 0:1])
+        h = make_h(quantised[0], quantised[1], bias_lo[:, 0:1], ring.tile([P, S], F32, name="h", bufs=4))
         for s0 in range(0, S, HALF):
             cols = slice(s0, s0 + HALF)
             nc.vector.tensor_tensor(
                 out=pages[0][:].indirect(idx2[:, list_cols(s0, HALF)]), in0=h[:, cols], in1=wgs_lo[:, cols], op=MULT
             )
         for i in range(1, 4):
-            quantised = quantise_w1(w1_nat[i][:].rearrange("p a j c -> p a c j"))
-            h = make_h(quantised[0], quantised[1], bias_lo[:, i : i + 1])
+            quantised = quantise_w1(i, 104, 105 + i)
+            h = make_h(quantised[0], quantised[1], bias_lo[:, i : i + 1], ring.tile([P, S], F32, name="h", bufs=4))
             nc.vector.tensor_tensor(out=pages[i][:].indirect(idx2[:]), in0=h[:], in1=wgs_lo[:], op=MULT)
 
         z_lo = shared.tile([P, 4, E], F32, name="z_lo", offset=0)
@@ -165,19 +174,18 @@ def tile_list_tsunami_edge_fluxes_kernel(
                     out=z_nat[:, cols], in0=pages[i][:].indirect(idx4[:, list_cols(m0, HALF)]), in1=y[:, cols], op=SUB
                 )
             for t in range(4):
-                nc.sync.dma_start(out=z_lo[32 * i : 32 * (i + 1), t, :], in_=z_nat[t:P:4, :])
+                nc.gpsimd.dma_start(out=z_lo[32 * i : 32 * (i + 1), t, :], in_=z_nat[t:P:4, :])
 
         for i in range(2):
             gather_lo(i, ring.tile([P, E], F32, name="y_lo"))
 
-        for a in range(2):
-            rows = w1[HALF * a : HALF * (a + 1), HALF:H]
-            nc.sync.dma_start(out=w1_hi[:, a], in_=rows.rearrange("(p j) c -> p j c", j=4))
-        nc.sync.dma_start(out=bias_hi[:], in_=b1[HALF:H].rearrange("(p t) -> p t", t=4))
         grouped_hi = shared.tile([P, 4, 2, P, 4], BF16, name="grouped_hi", align_bytes=64, offset=88 * KIB)
-        for t in range(4):
-            src = w1_hi[:].rearrange("p a j (c t) -> p t a c j", t=4)[:, t]
-            nc.scalar.activation(out=grouped_hi[:, t], in_=src, func=IDENT)
+        for a in range(2):
+            nc.scalar.activation(
+                out=grouped_hi[:].rearrange("p t a c j -> p a c t j")[:, a],
+                in_=w1_hi[:, a].rearrange("p j (c t) -> p c t j", t=4),
+                func=IDENT,
+            )
         codes_hi = keep.tile([P, 4, 2 * P], U32, name="codes_hi", align_bytes=64)
         scales_hi = keep.tile([P, 4, 2 * P], U8, name="scales_hi", align_bytes=64)
         nc.vector.quantize_mx(
@@ -185,9 +193,11 @@ def tile_list_tsunami_edge_fluxes_kernel(
             scales=scales_hi[:].rearrange("p t c -> p (t c)"),
             in_=grouped_hi[:].rearrange("p t a c j -> p (t a c j)"),
         )
-        h_hi = [make_h(codes_hi[:, t], scales_hi[:, t], bias_hi[:, t : t + 1]) for t in range(4)]
-
         gather_lo(2, shared.tile([P, E], F32, name="y_lo2", offset=88 * KIB))
+        h_hi = [shared.tile([P, S], F32, name="h_hi%d" % t, offset=(88 + 4 * t) * KIB) for t in range(2)]
+        h_hi = h_hi + [ring.tile([P, S], F32, name="h", bufs=4) for t in range(2)]
+        for t in range(4):
+            make_h(codes_hi[:, t], scales_hi[:, t], bias_hi[:, t : t + 1], h_hi[t])
         gather_lo(3, ring.tile([P, E], F32, name="y_lo"))
 
         wgs_hi = keep.tile([P, 4, S], F32, name="wgs_hi")
@@ -205,7 +215,11 @@ def tile_list_tsunami_edge_fluxes_kernel(
 
         def quantise_z(src, grouped, name):
             width = src.shape[2]
-            nc.scalar.activation(out=grouped[:], in_=src.rearrange("p t m -> p m t"), func=IDENT)
+            nc.scalar.activation(
+                out=grouped[:].rearrange("p (c i) t -> p c t i", i=4),
+                in_=src.rearrange("p t (c i) -> p c t i", i=4),
+                func=IDENT,
+            )
             codes = keep.tile([P, width], U32, name="zc_" + name, align_bytes=64)
             scales = keep.tile([P, width], U8, name="zs_" + name, align_bytes=64)
             nc.vector.quantize_mx(

@@ -20,7 +20,7 @@ IDENT = mybir.ActivationFunctionType.Identity
 P = 128
 KIB = 1024
 HALF = 512
-CHUNKS = (512, 256, 256)
+QUARTER = 256
 
 
 def tile_list_tsunami_edge_fluxes_kernel(
@@ -34,28 +34,27 @@ def tile_list_tsunami_edge_fluxes_kernel(
         ring = ctx.enter_context(tc.tile_pool(name="ring", bufs=2))
         psum = ctx.enter_context(tc.psum_pool(name="psum", bufs=8))
 
+        def placed(name, shape, dtype, kib):
+            return shared.tile(shape, dtype, name=name, align_bytes=64, offset=int(kib * KIB))
+
         idx = lists.tile([P, S // 16], U16, name="idx")
         idx2 = lists.tile([P, S // 16], U16, name="idx2")
         idx3 = lists.tile([P, E // 16], U16, name="idx3")
         idx4 = lists.tile([P, E // 16], U16, name="idx4")
 
-        tab = [shared.tile([P, T], I32, name="tab%d" % a, offset=16 * KIB * a) for a in range(2)]
-        w1_nat = [shared.tile([P, 2, 4, P], F32, name="w1_nat%d" % i, offset=(32 + 4 * i) * KIB) for i in range(4)]
-        w1_hi = shared.tile([P, 2, 4, HALF], F32, name="w1_hi", offset=48 * KIB)
-
-        tab_sc = shared.tile([P, T], U8, name="tab_sc", offset=64 * KIB)
-        v_words = [
-            shared.tile([P, S], U32, name="v_words%d" % a, align_bytes=64, offset=place * KIB)
-            for a, place in enumerate((68, 64))
-        ]
+        tab = [placed("tab%d" % a, [P, T], I32, 16 * a) for a in range(2)]
+        w1_nat = [placed("w1_nat%d" % i, [P, 2, 4, P], F32, 32 + 4 * i) for i in range(4)]
+        w1_hi = placed("w1_hi", [P, 2, 4, HALF], F32, 48)
+        tab_sc = placed("tab_sc", [P, T], U8, 64)
+        v_words = [placed("v_words%d" % a, [P, S], U32, kib) for a, kib in enumerate((68, 64))]
         v_sc = keep.tile([P, S], U8, name="v_sc", align_bytes=64)
-        pages = [
-            shared.tile([P, T2], F32, name="page%d" % i, offset=place * KIB) for i, place in enumerate((72, 80, 16, 24))
-        ]
+        pages = [keep.tile([P, T2], F32, name="page%d" % i) for i in range(4)]
         bias_lo = keep.tile([P, 4], F32, name="bias_lo")
         bias_hi = keep.tile([P, 4], F32, name="bias_hi")
         wgs_lo = keep.tile([P, S], F32, name="wgs_lo")
-        bstep_lo = [keep.tile([P, E], F32, name="bstep_lo%d" % i) for i in range(4)]
+        wgs_hi = keep.tile([P, 4, S], F32, name="wgs_hi")
+        bstep_lo = keep.tile([P, 4, E], F32, name="bstep_lo")
+        bstep_hi = keep.tile([P, 4, E], F32, name="bstep_hi")
         w2_w = keep.tile([P, 2, 2 * N], U8, name="w2_w", align_bytes=64)
         w2_sc = keep.tile([P, 2, N], U8, name="w2_sc", align_bytes=64)
         le_all = keep.tile([P, E], F32, name="le_all")
@@ -77,109 +76,134 @@ def tile_list_tsunami_edge_fluxes_kernel(
         for i in range(2):
             nc.vector.memset(pages[i][:], 0.0)
         nc.vector.memset(w2_sc[:].rearrange("p a c -> p (a c)").bitcast(I32), 0)
+        for i in range(2, 4):
+            for c0 in range(0, T2, HALF):
+                nc.gpsimd.memset(pages[i][:, c0 : c0 + HALF], 0.0)
 
         load_tab(0)
         nc.sync.dma_start(idx[:], offs)
         load_w1_nat(0)
         load_tab(1)
-        nc.sync.dma_start(out=wgs_lo[:], in_=wgs)
-        nc.sync.dma_start(idx2[:], offs2)
         with nc.allow_non_contiguous_dma(reason="one bias value a partition"):
             nc.sync.dma_start(out=bias_lo[:], in_=b1[0:HALF].rearrange("(i p) -> p i", p=P))
+        nc.sync.dma_start(idx2[:], offs2)
+        for s0 in range(0, S, HALF):
+            nc.sync.dma_start(out=wgs_lo[:, s0 : s0 + HALF], in_=wgs[:, s0 : s0 + HALF])
         load_w1_nat(1)
+        load_w1_nat(2)
+        load_w1_nat(3)
         nc.sync.dma_start(idx3[:], offs3)
         nc.sync.dma_start(idx4[:], offs4)
-        nc.sync.dma_start(out=bstep_lo[0][:], in_=bstep[0:P, :])
-        load_w1_nat(2)
-        nc.sync.dma_start(out=bstep_lo[1][:], in_=bstep[P : 2 * P, :])
-        load_w1_nat(3)
         for a in range(2):
             rows = w1[HALF * a : HALF * (a + 1), HALF:H]
             nc.sync.dma_start(out=w1_hi[:, a], in_=rows.rearrange("(p j) c -> p j c", j=4))
         nc.sync.dma_start(out=bias_hi[:], in_=b1[HALF:H].rearrange("(p t) -> p t", t=4))
-        for i in (2, 3):
-            nc.sync.dma_start(out=bstep_lo[i][:], in_=bstep[P * i : P * (i + 1), :])
-
-        nc.vector.tensor_copy(out=v_sc[:], in_=tab_sc[:].indirect(idx[:]))
-        nc.vector.tensor_copy(out=v_words[0][:], in_=tab[0][:].bitcast(U32).indirect(idx[:]))
-
-        def quantise_w1(i, grouped_at, codes_at):
-            src = w1_nat[i]
-            grouped = shared.tile([P, 2, P, 4], BF16, name="w1_grouped%d" % i, align_bytes=64, offset=grouped_at * KIB)
-            for a in range(2):
-                nc.scalar.activation(
-                    out=grouped[:, a].rearrange("p (c i) j -> p c j i", i=4),
-                    in_=src[:, a].rearrange("p j (c i) -> p c j i", i=4),
-                    func=IDENT,
-                )
-            codes = shared.tile([P, 2 * P], U32, name="w1_codes%d" % i, align_bytes=64, offset=codes_at * KIB)
-            scales = ring.tile([P, 2 * P], U8, name="w1_scales", align_bytes=64, bufs=4)
-            nc.vector.quantize_mx(
-                out=codes[:].bitcast(FP8X4), scales=scales[:], in_=grouped[:].rearrange("p a c j -> p (a c j)")
+        for q in range(4):
+            nc.sync.dma_start(out=wgs_hi[32 * q : 32 * (q + 1)], in_=wgs.rearrange("(p t) j -> p t j", t=4))
+        nc.sync.dma_start(out=bstep_lo[:], in_=bstep[0:HALF, :].rearrange("(i p) m -> p i m", p=P))
+        nc.sync.dma_start(out=w2_w[:].bitcast(I32), in_=w2_words.rearrange("a p c -> p a c").bitcast(I32))
+        for q in range(4):
+            nc.sync.dma_start(
+                out=w2_sc[32 * q : 32 * q + 4].bitcast(I32),
+                in_=w2_scales[:, 4 * q : 4 * q + 4, :].rearrange("a r c -> r a c").bitcast(I32),
             )
-            return codes, scales
-
-        def make_h(codes, scales, bias, h):
-            for s0 in range(0, S, HALF):
-                cols = slice(s0, s0 + HALF)
-                acc = psum.tile([P, HALF], F32, name="acc_h", tag="bank")
-                for a in range(2):
-                    nc.tensor.matmul_mx(
-                        out=acc[:],
-                        lhsT=codes[:, P * a : P * (a + 1)].bitcast(FP8X4),
-                        lhsT_scale=scales[:, P * a : P * (a + 1)],
-                        rhs=v_words[a][:, cols].bitcast(FP8X4),
-                        rhs_scale=v_sc[4 * a : P, cols],
-                        start=(a == 0),
-                        stop=(a == 1),
-                    )
-                nc.scalar.activation(out=h[:, cols], in_=acc[:], func=IDENT, bias=bias)
-            return h
+        nc.sync.dma_start(out=bstep_hi[:], in_=bstep[HALF:H, :].rearrange("(p t) m -> p t m", t=4))
+        nc.sync.dma_start(out=le_all[:], in_=le.partition_broadcast(P))
 
         def list_cols(m0, width):
             return slice(m0 // 16, (m0 + width) // 16)
 
-        quantised = quantise_w1(0, 106, 104)
+        def cast_w1(first, count, grouped_at):
+            grouped = placed("w1_grouped%d" % first, [P, count, 2, P, 4], BF16, grouped_at)
+            for i in range(count):
+                for a in range(2):
+                    nc.scalar.activation(
+                        out=grouped[:, i, a].rearrange("p (c i) j -> p c j i", i=4),
+                        in_=w1_nat[first + i][:, a].rearrange("p j (c i) -> p c j i", i=4),
+                        func=IDENT,
+                    )
+            return grouped
+
+        def quantise_w1(first, grouped, codes_at, scales_at):
+            count = grouped.shape[1]
+            codes = placed("w1_codes%d" % first, [P, count, 2 * P], U32, codes_at)
+            scales = placed("w1_scales%d" % first, [P, count, 2 * P], U8, scales_at)
+            nc.vector.quantize_mx(
+                out=codes[:].rearrange("p i c -> p (i c)").bitcast(FP8X4),
+                scales=scales[:].rearrange("p i c -> p (i c)"),
+                in_=grouped[:].rearrange("p i a c j -> p (i a c j)"),
+            )
+            return [(codes[:, i], scales[:, i]) for i in range(count)]
+
+        def multiply_h(quantised, s0):
+            codes, scales = quantised
+            cols = slice(s0, s0 + HALF)
+            acc = psum.tile([P, HALF], F32, name="acc_h", tag="bank")
+            for a in range(2):
+                nc.tensor.matmul_mx(
+                    out=acc[:],
+                    lhsT=codes[:, P * a : P * (a + 1)].bitcast(FP8X4),
+                    lhsT_scale=scales[:, P * a : P * (a + 1)],
+                    rhs=v_words[a][:, cols].bitcast(FP8X4),
+                    rhs_scale=v_sc[4 * a : P, cols],
+                    start=(a == 0),
+                    stop=(a == 1),
+                )
+            return acc
+
+        def add_bias(dst, acc, bias):
+            nc.scalar.activation(out=dst, in_=acc[:], func=IDENT, bias=bias)
+
+        def make_h(h, quantised, bias):
+            for s0 in range(0, S, HALF):
+                add_bias(h[:, s0 : s0 + HALF], multiply_h(quantised, s0), bias)
+            return h
+
+        def h_tile(i):
+            return placed("h%d" % i, [P, S], F32, 88 + 4 * (i % 4))
+
+        def scatter(page, h, weights, s0, width):
+            nc.vector.tensor_tensor(
+                out=page[:].indirect(idx2[:, list_cols(s0, width)]), in0=h[:], in1=weights[:, s0 : s0 + width], op=MULT
+            )
+
+        def gather_minus(dst, page, which, m0, width, other):
+            nc.vector.tensor_tensor(out=dst, in0=page[:].indirect(which[:, list_cols(m0, width)]), in1=other, op=SUB)
+
+        nc.vector.tensor_copy(out=v_words[0][:], in_=tab[0][:].bitcast(U32).indirect(idx[:]))
+        nc.vector.tensor_copy(out=v_sc[:], in_=tab_sc[:].indirect(idx[:]))
+        w1_q = quantise_w1(0, cast_w1(0, 1, 76), 79, 72)
         for s0 in range(0, S, HALF):
             nc.vector.tensor_copy(
                 out=v_words[1][:, s0 : s0 + HALF],
                 in_=tab[1][:].bitcast(U32).indirect(idx[:, list_cols(s0, HALF)]),
             )
-        for i in range(2, 4):
-            for c0 in range(0, T2, HALF):
-                nc.gpsimd.memset(pages[i][:, c0 : c0 + HALF], 0.0)
-        h = make_h(quantised[0], quantised[1], bias_lo[:, 0:1], ring.tile([P, S], F32, name="h", bufs=4))
-        for s0 in range(0, S, HALF):
-            cols = slice(s0, s0 + HALF)
-            nc.vector.tensor_tensor(
-                out=pages[0][:].indirect(idx2[:, list_cols(s0, HALF)]), in0=h[:, cols], in1=wgs_lo[:, cols], op=MULT
-            )
-        for i in range(1, 4):
-            quantised = quantise_w1(i, 104, 105 + i)
-            h = make_h(quantised[0], quantised[1], bias_lo[:, i : i + 1], ring.tile([P, S], F32, name="h", bufs=4))
-            nc.vector.tensor_tensor(out=pages[i][:].indirect(idx2[:]), in0=h[:], in1=wgs_lo[:], op=MULT)
+        h_first = [placed("h_first%d" % c, [P, HALF], F32, kib) for c, kib in enumerate((84, 88))]
+        acc_first = [multiply_h(w1_q[0], HALF * c) for c in range(2)]
+        add_bias(h_first[0][:], acc_first[0], bias_lo[:, 0:1])
+        grouped_second = cast_w1(1, 1, 72)
+        add_bias(h_first[1][:], acc_first[1], bias_lo[:, 0:1])
+        scatter(pages[0], h_first[0], wgs_lo, 0, HALF)
+        w1_q = w1_q + quantise_w1(1, grouped_second, 74, 75)
+        scatter(pages[0], h_first[1], wgs_lo, HALF, HALF)
 
-        z_lo = shared.tile([P, 4, E], F32, name="z_lo", offset=0)
+        z_lo = placed("z_lo", [P, 4, E], F32, 0)
 
-        def gather_lo(i, y):
-            z_nat = ring.tile([P, E], F32, name="z_nat")
-            for m0 in range(0, E, HALF):
-                cols = slice(m0, m0 + HALF)
-                nc.vector.tensor_tensor(
-                    out=y[:, cols], in0=pages[i][:].indirect(idx3[:, list_cols(m0, HALF)]), in1=bstep_lo[i][:, cols], op=SUB
-                )
-            for m0 in range(0, E, HALF):
-                cols = slice(m0, m0 + HALF)
-                nc.vector.tensor_tensor(
-                    out=z_nat[:, cols], in0=pages[i][:].indirect(idx4[:, list_cols(m0, HALF)]), in1=y[:, cols], op=SUB
-                )
+        def left_lo(i):
+            y = ring.tile([P, E], F32, name="y_lo", bufs=3)
+            gather_minus(y[:], pages[i], idx3, 0, E, bstep_lo[:, i, :])
+            return y
+
+        def right_lo(i, y):
+            z_nat = placed("z_nat%d" % i, [P, E], F32, (104, 108, 48, 52)[i])
+            gather_minus(z_nat[:], pages[i], idx4, 0, E, y[:])
             for t in range(4):
-                nc.gpsimd.dma_start(out=z_lo[32 * i : 32 * (i + 1), t, :], in_=z_nat[t:P:4, :])
+                nc.sync.dma_start(out=z_lo[32 * i : 32 * (i + 1), t, :], in_=z_nat[t:P:4, :])
 
-        for i in range(2):
-            gather_lo(i, ring.tile([P, E], F32, name="y_lo"))
+        w1_q = w1_q + quantise_w1(2, cast_w1(2, 2, 84), 76, 78)
+        h = {i: make_h(h_tile(i), w1_q[i], bias_lo[:, i : i + 1]) for i in range(1, 4)}
 
-        grouped_hi = shared.tile([P, 4, 2, P, 4], BF16, name="grouped_hi", align_bytes=64, offset=88 * KIB)
+        grouped_hi = placed("grouped_hi", [P, 4, 2, P, 4], BF16, 76)
         for a in range(2):
             nc.scalar.activation(
                 out=grouped_hi[:].rearrange("p t a c j -> p a c t j")[:, a],
@@ -193,33 +217,33 @@ def tile_list_tsunami_edge_fluxes_kernel(
             scales=scales_hi[:].rearrange("p t c -> p (t c)"),
             in_=grouped_hi[:].rearrange("p t a c j -> p (t a c j)"),
         )
-        gather_lo(2, shared.tile([P, E], F32, name="y_lo2", offset=88 * KIB))
-        h_hi = [shared.tile([P, S], F32, name="h_hi%d" % t, offset=(88 + 4 * t) * KIB) for t in range(2)]
-        h_hi = h_hi + [ring.tile([P, S], F32, name="h", bufs=4) for t in range(2)]
-        for t in range(4):
-            make_h(codes_hi[:, t], scales_hi[:, t], bias_hi[:, t : t + 1], h_hi[t])
-        gather_lo(3, ring.tile([P, E], F32, name="y_lo"))
 
-        wgs_hi = keep.tile([P, 4, S], F32, name="wgs_hi")
-        for q in range(4):
-            nc.sync.dma_start(out=wgs_hi[32 * q : 32 * (q + 1)], in_=wgs.rearrange("(p t) j -> p t j", t=4))
-        nc.sync.dma_start(out=w2_w[:].bitcast(I32), in_=w2_words.rearrange("a p c -> p a c").bitcast(I32))
-        for q in range(4):
-            nc.sync.dma_start(
-                out=w2_sc[32 * q : 32 * q + 4].bitcast(I32),
-                in_=w2_scales[:, 4 * q : 4 * q + 4, :].rearrange("a r c -> r a c").bitcast(I32),
-            )
-        bstep_hi = shared.tile([P, 4, E], F32, name="bstep_hi", offset=32 * KIB)
-        nc.sync.dma_start(out=bstep_hi[:], in_=bstep[HALF:H, :].rearrange("(p t) m -> p t m", t=4))
-        nc.sync.dma_start(out=le_all[:], in_=le.partition_broadcast(P))
+        def scatter_tile(i):
+            if i < 4:
+                scatter(pages[i], h[i], wgs_lo, 0, S)
+            else:
+                t = i - 4
+                h_hi = make_h(h_tile(i), (codes_hi[:, t], scales_hi[:, t]), bias_hi[:, t : t + 1])
+                scatter(pages[t], h_hi, wgs_hi[:, t, :], 0, S)
 
-        def quantise_z(src, grouped, name):
-            width = src.shape[2]
+        for i in range(1, 4):
+            scatter_tile(i)
+        y = {0: left_lo(0)}
+        for i in range(3):
+            y[i + 1] = left_lo(i + 1)
+            right_lo(i, y[i])
+        right_lo(3, y[3])
+        for i in range(4, 8):
+            scatter_tile(i)
+
+        def interleave_z(src, grouped):
             nc.scalar.activation(
                 out=grouped[:].rearrange("p (c i) t -> p c t i", i=4),
                 in_=src.rearrange("p t (c i) -> p c t i", i=4),
                 func=IDENT,
             )
+
+        def quantise_z(grouped, width, name):
             codes = keep.tile([P, width], U32, name="zc_" + name, align_bytes=64)
             scales = keep.tile([P, width], U8, name="zs_" + name, align_bytes=64)
             nc.vector.quantize_mx(
@@ -227,12 +251,11 @@ def tile_list_tsunami_edge_fluxes_kernel(
             )
             return codes, scales
 
-        for t in range(4):
-            nc.vector.tensor_tensor(out=pages[t][:].indirect(idx2[:]), in0=h_hi[t][:], in1=wgs_hi[:, t, :], op=MULT)
         zq_lo = []
-        for m0 in range(0, E, HALF):
-            grouped = shared.tile([P, HALF, 4], BF16, name="zg_lo%d" % m0, align_bytes=64, offset=88 * KIB + 8 * m0)
-            zq_lo.append(quantise_z(z_lo[:, :, m0 : m0 + HALF], grouped, "lo%d" % m0))
+        for c, m0 in enumerate(range(0, E, HALF)):
+            grouped = placed("zg_lo%d" % c, [P, HALF, 4], BF16, 88 + 4 * c)
+            interleave_z(z_lo[:, :, m0 : m0 + HALF], grouped)
+            zq_lo.append(quantise_z(grouped, HALF, "lo%d" % c))
 
         def out_pass(acc, a, width, blocks, codes, scales, z0):
             step = HALF if width == HALF else P
@@ -250,37 +273,56 @@ def tile_list_tsunami_edge_fluxes_kernel(
                     stop=(a == 1 and (k, c0) == pieces[-1]),
                 )
 
-        starts = [sum(CHUNKS[:c]) for c in range(len(CHUNKS))]
-        banks = []
-        for m0, width in zip(starts, CHUNKS):
+        def open_banks(m0, width):
             per_bank = HALF // width
-            chunk_banks = []
+            opened = []
             for b0 in range(0, 4, per_bank):
                 blocks = list(range(b0, b0 + per_bank))
                 acc = psum.tile([P, per_bank, width], F32, name="acc_out", tag="bank")
                 lo_codes, lo_scales = zq_lo[m0 // HALF]
                 out_pass(acc, 0, width, blocks, lo_codes, lo_scales, m0 % HALF)
-                chunk_banks.append((acc, blocks))
-            banks.append(chunk_banks)
+                opened.append((acc, blocks))
+            return opened
 
+        banks = {0: open_banks(0, HALF), HALF: open_banks(HALF, QUARTER), HALF + QUARTER: open_banks(HALF + QUARTER, QUARTER)}
         out_v = out.rearrange("(b p) m -> p b m", p=P)
-        for m0, width, chunk_banks in zip(starts, CHUNKS, banks):
+
+        def gather_hi(m0, y_at):
+            cols = slice(m0, m0 + HALF)
+            y = [placed("y_hi%d_%d" % (m0, t), [P, HALF], F32, y_at + 2 * t) for t in range(4)]
+            z_hi = placed("z_hi%d" % m0, [P, 4, HALF], F32, 0)
+            for t in range(4):
+                gather_minus(y[t][:], pages[t], idx3, m0, HALF, bstep_hi[:, t, cols])
+            for t in range(4):
+                gather_minus(z_hi[:, t, :], pages[t], idx4, m0, HALF, y[t][:])
+            return z_hi
+
+        def close_banks(m0, width, quantised):
+            for acc, blocks in banks[m0]:
+                out_pass(acc, 1, width, blocks, quantised[0], quantised[1], 0)
+
+        def finish(m0, width, k, res_at):
+            acc, blocks = banks[m0][k]
             cols = slice(m0, m0 + width)
-            y = shared.tile([P, 4, width], F32, name="y_hi%d" % m0, offset=88 * KIB + 16 * m0)
-            z_hi = shared.tile([P, 4, width], F32, name="z_hi%d" % m0, offset=48 * KIB + 16 * m0)
-            for t in range(4):
-                nc.vector.tensor_tensor(
-                    out=y[:, t, :], in0=pages[t][:].indirect(idx3[:, list_cols(m0, width)]), in1=bstep_hi[:, t, cols], op=SUB
-                )
-            for t in range(4):
-                nc.vector.tensor_tensor(
-                    out=z_hi[:, t, :], in0=pages[t][:].indirect(idx4[:, list_cols(m0, width)]), in1=y[:, t, :], op=SUB
-                )
-            grouped = keep.tile([P, width, 4], BF16, name="zg_hi%d" % m0, align_bytes=64)
-            hi_codes, hi_scales = quantise_z(z_hi[:], grouped, "hi%d" % m0)
-            for acc, blocks in chunk_banks:
-                out_pass(acc, 1, width, blocks, hi_codes, hi_scales, 0)
-                res = ring.tile([P, len(blocks), width], F32, name="res", bufs=4)
-                factors = le_all[:, cols].unsqueeze(1).to_broadcast([P, len(blocks), width])
-                nc.vector.tensor_tensor(out=res[:], in0=acc[:], in1=factors, op=MULT)
-                nc.sync.dma_start(out=out_v[:, blocks[0] : blocks[-1] + 1, cols], in_=res[:])
+            res = placed("res%d_%d" % (m0, k), [P, len(blocks), width], F32, res_at)
+            factors = le_all[:, cols].unsqueeze(1).to_broadcast([P, len(blocks), width])
+            nc.vector.tensor_tensor(out=res[:], in0=acc[:], in1=factors, op=MULT)
+            nc.sync.dma_start(out=out_v[:, blocks[0] : blocks[-1] + 1, cols], in_=res[:])
+
+        z_first = gather_hi(0, 32)
+        grouped = placed("zg_hi0", [P, HALF, 4], BF16, 48)
+        interleave_z(z_first[:], grouped)
+        close_banks(0, HALF, quantise_z(grouped, HALF, "hi0"))
+
+        z_last = gather_hi(HALF, 32)
+        grouped_last = [placed("zg_hi%d" % (1 + c), [P, QUARTER, 4], BF16, 52 + 2 * c) for c in range(2)]
+        for c in range(2):
+            interleave_z(z_last[:, :, QUARTER * c : QUARTER * (c + 1)], grouped_last[c])
+        for k in range(3):
+            finish(0, HALF, k, 32 + 2 * k)
+        close_banks(HALF, QUARTER, quantise_z(grouped_last[0], QUARTER, "hi1"))
+        finish(0, HALF, 3, 38)
+        close_banks(HALF + QUARTER, QUARTER, quantise_z(grouped_last[1], QUARTER, "hi2"))
+        for c in range(2):
+            for k in range(2):
+                finish(HALF + QUARTER * c, QUARTER, k, 56 + 4 * c + 2 * k)

@@ -43,21 +43,22 @@ def tile_list_tsunami_edge_fluxes_kernel(
         idx4 = lists.tile([P, E // 16], U16, name="idx4")
 
         tab = [placed("tab%d" % a, [P, T], I32, 16 * a) for a in range(2)]
-        w1_nat = [placed("w1_nat%d" % i, [P, 2, 4, P], F32, 32 + 4 * i) for i in range(4)]
-        w1_hi = placed("w1_hi", [P, 2, 4, HALF], F32, 48)
-        tab_sc = placed("tab_sc", [P, T], U8, 64)
-        v_words = [placed("v_words%d" % a, [P, S], U32, kib) for a, kib in enumerate((68, 64))]
+        wgs_hi = placed("wgs_hi", [P, 4, S], F32, 0.25)
+        w1_nat = [placed("w1_nat%d" % i, [P, 2, 4, P], F32, kib) for i, kib in enumerate((44.25, 148, 20.25, 24.25))]
+        w1_hi = placed("w1_hi", [P, 2, 4, HALF], F32, 28.25)
+        tab_sc = placed("tab_sc", [P, T], U8, 159.9375)
+        v_words = [placed("v_words%d" % a, [P, S], U32, kib) for a, kib in enumerate((52.25, 48.25))]
+        bstep_lo = placed("bstep_lo", [P, 4, E], F32, 90)
+        bstep_hi = placed("bstep_hi", [P, 4, E], F32, 106.875)
+        w2_w = placed("w2_w", [P, 2, 2 * N], U8, 123)
+        le_all = placed("le_all", [P, E], F32, 126.875)
+        picked_sc = placed("picked_sc", [P, S], U8, 171.9375)
+        w2_sc = placed("w2_sc", [P, 2, N], U8, 131)
         v_sc = keep.tile([P, S], U8, name="v_sc", align_bytes=64)
-        pages = [keep.tile([P, T2], F32, name="page%d" % i) for i in range(4)]
+        pages = [placed("page%d" % i, [P, T2], F32, kib) for i, kib in enumerate((181, 152, 164, 172.875))]
         bias_lo = keep.tile([P, 4], F32, name="bias_lo")
         bias_hi = keep.tile([P, 4], F32, name="bias_hi")
         wgs_lo = keep.tile([P, S], F32, name="wgs_lo")
-        wgs_hi = keep.tile([P, 4, S], F32, name="wgs_hi")
-        bstep_lo = keep.tile([P, 4, E], F32, name="bstep_lo")
-        bstep_hi = keep.tile([P, 4, E], F32, name="bstep_hi")
-        w2_w = keep.tile([P, 2, 2 * N], U8, name="w2_w", align_bytes=64)
-        w2_sc = keep.tile([P, 2, N], U8, name="w2_sc", align_bytes=64)
-        le_all = keep.tile([P, E], F32, name="le_all")
 
         def load_w1_nat(i):
             for a in range(2):
@@ -67,21 +68,28 @@ def tile_list_tsunami_edge_fluxes_kernel(
         def load_tab(a):
             nc.sync.dma_start(out=tab[a][:], in_=tab_words[a].rearrange("p t i -> p (t i)").bitcast(I32))
 
-        nc.vector.memset(tab_sc[:].bitcast(I32), 0)
+        for rows in (slice(32, 64), slice(64, P)):
+            nc.vector.memset(tab_sc[rows, :].bitcast(I32), 0)
+        for r in range(4):
+            nc.sync.dma_start(
+                out=tab_sc[r:32:4, :].bitcast(I32),
+                in_=tab_scales.rearrange("a (q r) t -> r q a t", r=4)[r].bitcast(I32),
+            )
+        nc.sync.dma_start(idx[:], offs)
+        nc.vector.memset(v_sc[:].bitcast(I32), 0)
+        nc.vector.tensor_copy(out=picked_sc[:], in_=tab_sc[:].indirect(idx[:]))
         for q in range(4):
             nc.gpsimd.dma_start(
-                out=tab_sc[32 * q : 32 * q + 8, :].bitcast(I32),
-                in_=tab_scales[:, 4 * q : 4 * q + 4, :].bitcast(I32),
+                out=v_sc[32 * q : 32 * q + 8, :].bitcast(I32), in_=picked_sc[8 * q : 8 * q + 8, :].bitcast(I32)
             )
         for i in range(2):
             nc.vector.memset(pages[i][:], 0.0)
-        nc.vector.memset(w2_sc[:].rearrange("p a c -> p (a c)").bitcast(I32), 0)
         for i in range(2, 4):
             for c0 in range(0, T2, HALF):
                 nc.gpsimd.memset(pages[i][:, c0 : c0 + HALF], 0.0)
+        nc.vector.memset(w2_sc[:].rearrange("p a c -> p (a c)").bitcast(I32), 0)
 
         load_tab(0)
-        nc.sync.dma_start(idx[:], offs)
         load_w1_nat(0)
         load_tab(1)
         with nc.allow_non_contiguous_dma(reason="one bias value a partition"):
@@ -89,26 +97,10 @@ def tile_list_tsunami_edge_fluxes_kernel(
         nc.sync.dma_start(idx2[:], offs2)
         for s0 in range(0, S, HALF):
             nc.sync.dma_start(out=wgs_lo[:, s0 : s0 + HALF], in_=wgs[:, s0 : s0 + HALF])
-        load_w1_nat(1)
-        load_w1_nat(2)
-        load_w1_nat(3)
         nc.sync.dma_start(idx3[:], offs3)
         nc.sync.dma_start(idx4[:], offs4)
-        for a in range(2):
-            rows = w1[HALF * a : HALF * (a + 1), HALF:H]
-            nc.sync.dma_start(out=w1_hi[:, a], in_=rows.rearrange("(p j) c -> p j c", j=4))
         nc.sync.dma_start(out=bias_hi[:], in_=b1[HALF:H].rearrange("(p t) -> p t", t=4))
-        for q in range(4):
-            nc.sync.dma_start(out=wgs_hi[32 * q : 32 * (q + 1)], in_=wgs.rearrange("(p t) j -> p t j", t=4))
-        nc.sync.dma_start(out=bstep_lo[:], in_=bstep[0:HALF, :].rearrange("(i p) m -> p i m", p=P))
-        nc.sync.dma_start(out=w2_w[:].bitcast(I32), in_=w2_words.rearrange("a p c -> p a c").bitcast(I32))
-        for q in range(4):
-            nc.sync.dma_start(
-                out=w2_sc[32 * q : 32 * q + 4].bitcast(I32),
-                in_=w2_scales[:, 4 * q : 4 * q + 4, :].rearrange("a r c -> r a c").bitcast(I32),
-            )
-        nc.sync.dma_start(out=bstep_hi[:], in_=bstep[HALF:H, :].rearrange("(p t) m -> p t m", t=4))
-        nc.sync.dma_start(out=le_all[:], in_=le.partition_broadcast(P))
+        load_w1_nat(1)
 
         def list_cols(m0, width):
             return slice(m0 // 16, (m0 + width) // 16)
@@ -160,7 +152,7 @@ def tile_list_tsunami_edge_fluxes_kernel(
             return h
 
         def h_tile(i):
-            return placed("h%d" % i, [P, S], F32, 88 + 4 * (i % 4))
+            return placed("h%d" % i, [P, S], F32, 72.25 + 4 * (i % 4))
 
         def scatter(page, h, weights, s0, width):
             nc.vector.tensor_tensor(
@@ -171,23 +163,39 @@ def tile_list_tsunami_edge_fluxes_kernel(
             nc.vector.tensor_tensor(out=dst, in0=page[:].indirect(which[:, list_cols(m0, width)]), in1=other, op=SUB)
 
         nc.vector.tensor_copy(out=v_words[0][:], in_=tab[0][:].bitcast(U32).indirect(idx[:]))
-        nc.vector.tensor_copy(out=v_sc[:], in_=tab_sc[:].indirect(idx[:]))
-        w1_q = quantise_w1(0, cast_w1(0, 1, 76), 79, 72)
+        w1_q = quantise_w1(0, cast_w1(0, 1, 60.25), 105.9375, 56.25)
         for s0 in range(0, S, HALF):
             nc.vector.tensor_copy(
                 out=v_words[1][:, s0 : s0 + HALF],
                 in_=tab[1][:].bitcast(U32).indirect(idx[:, list_cols(s0, HALF)]),
             )
-        h_first = [placed("h_first%d" % c, [P, HALF], F32, kib) for c, kib in enumerate((84, 88))]
+        h_first = [placed("h_first%d" % c, [P, HALF], F32, kib) for c, kib in enumerate((68.25, 124.9375))]
         acc_first = [multiply_h(w1_q[0], HALF * c) for c in range(2)]
+        load_w1_nat(2)
+        load_w1_nat(3)
+        for a in range(2):
+            rows = w1[HALF * a : HALF * (a + 1), HALF:H]
+            nc.sync.dma_start(out=w1_hi[:, a], in_=rows.rearrange("(p j) c -> p j c", j=4))
+        for q in range(4):
+            nc.sync.dma_start(out=wgs_hi[32 * q : 32 * (q + 1)], in_=wgs.rearrange("(p t) j -> p t j", t=4))
+        nc.sync.dma_start(out=bstep_lo[:], in_=bstep[0:HALF, :].rearrange("(i p) m -> p i m", p=P))
+        for q in range(4):
+            nc.sync.dma_start(
+                out=w2_sc[32 * q : 32 * q + 4].bitcast(I32),
+                in_=w2_scales[:, 4 * q : 4 * q + 4, :].rearrange("a r c -> r a c").bitcast(I32),
+            )
+        nc.sync.dma_start(out=bstep_hi[:], in_=bstep[HALF:H, :].rearrange("(p t) m -> p t m", t=4))
+
         add_bias(h_first[0][:], acc_first[0], bias_lo[:, 0:1])
-        grouped_second = cast_w1(1, 1, 72)
+        grouped_second = cast_w1(1, 1, 56.25)
         add_bias(h_first[1][:], acc_first[1], bias_lo[:, 0:1])
         scatter(pages[0], h_first[0], wgs_lo, 0, HALF)
-        w1_q = w1_q + quantise_w1(1, grouped_second, 74, 75)
+        w1_q = w1_q + quantise_w1(1, grouped_second, 58.25, 59.25)
         scatter(pages[0], h_first[1], wgs_lo, HALF, HALF)
+        nc.sync.dma_start(out=w2_w[:].bitcast(I32), in_=w2_words.rearrange("a p c -> p a c").bitcast(I32))
+        nc.sync.dma_start(out=le_all[:], in_=le.partition_broadcast(P))
 
-        z_lo = placed("z_lo", [P, 4, E], F32, 0)
+        z_lo = placed("z_lo", [P, 4, E], F32, 132)
 
         def left_lo(i):
             y = ring.tile([P, E], F32, name="y_lo", bufs=3)
@@ -195,15 +203,15 @@ def tile_list_tsunami_edge_fluxes_kernel(
             return y
 
         def right_lo(i, y):
-            z_nat = placed("z_nat%d" % i, [P, E], F32, (104, 108, 48, 52)[i])
+            z_nat = placed("z_nat%d" % i, [P, E], F32, (16.25, 20.25, 28.25, 32.25)[i])
             gather_minus(z_nat[:], pages[i], idx4, 0, E, y[:])
             for t in range(4):
                 nc.sync.dma_start(out=z_lo[32 * i : 32 * (i + 1), t, :], in_=z_nat[t:P:4, :])
 
-        w1_q = w1_q + quantise_w1(2, cast_w1(2, 2, 84), 76, 78)
+        w1_q = w1_q + quantise_w1(2, cast_w1(2, 2, 68.25), 60.25, 62.25)
         h = {i: make_h(h_tile(i), w1_q[i], bias_lo[:, i : i + 1]) for i in range(1, 4)}
 
-        grouped_hi = placed("grouped_hi", [P, 4, 2, P, 4], BF16, 76)
+        grouped_hi = placed("grouped_hi", [P, 4, 2, P, 4], BF16, 60.25)
         for a in range(2):
             nc.scalar.activation(
                 out=grouped_hi[:].rearrange("p t a c j -> p a c t j")[:, a],
@@ -253,7 +261,7 @@ def tile_list_tsunami_edge_fluxes_kernel(
 
         zq_lo = []
         for c, m0 in enumerate(range(0, E, HALF)):
-            grouped = placed("zg_lo%d" % c, [P, HALF, 4], BF16, 88 + 4 * c)
+            grouped = placed("zg_lo%d" % c, [P, HALF, 4], BF16, 72.25 + 4 * c)
             interleave_z(z_lo[:, :, m0 : m0 + HALF], grouped)
             zq_lo.append(quantise_z(grouped, HALF, "lo%d" % c))
 
@@ -290,7 +298,7 @@ def tile_list_tsunami_edge_fluxes_kernel(
         def gather_hi(m0, y_at):
             cols = slice(m0, m0 + HALF)
             y = [placed("y_hi%d_%d" % (m0, t), [P, HALF], F32, y_at + 2 * t) for t in range(4)]
-            z_hi = placed("z_hi%d" % m0, [P, 4, HALF], F32, 0)
+            z_hi = placed("z_hi%d" % m0, [P, 4, HALF], F32, 132)
             for t in range(4):
                 gather_minus(y[t][:], pages[t], idx3, m0, HALF, bstep_hi[:, t, cols])
             for t in range(4):
@@ -309,20 +317,20 @@ def tile_list_tsunami_edge_fluxes_kernel(
             nc.vector.tensor_tensor(out=res[:], in0=acc[:], in1=factors, op=MULT)
             nc.sync.dma_start(out=out_v[:, blocks[0] : blocks[-1] + 1, cols], in_=res[:])
 
-        z_first = gather_hi(0, 32)
-        grouped = placed("zg_hi0", [P, HALF, 4], BF16, 48)
+        z_first = gather_hi(0, 44.25)
+        grouped = placed("zg_hi0", [P, HALF, 4], BF16, 36.25)
         interleave_z(z_first[:], grouped)
         close_banks(0, HALF, quantise_z(grouped, HALF, "hi0"))
 
-        z_last = gather_hi(HALF, 32)
-        grouped_last = [placed("zg_hi%d" % (1 + c), [P, QUARTER, 4], BF16, 52 + 2 * c) for c in range(2)]
+        z_last = gather_hi(HALF, 44.25)
+        grouped_last = [placed("zg_hi%d" % (1 + c), [P, QUARTER, 4], BF16, 40.25 + 2 * c) for c in range(2)]
         for c in range(2):
             interleave_z(z_last[:, :, QUARTER * c : QUARTER * (c + 1)], grouped_last[c])
         for k in range(3):
-            finish(0, HALF, k, 32 + 2 * k)
+            finish(0, HALF, k, 44.25 + 2 * k)
         close_banks(HALF, QUARTER, quantise_z(grouped_last[0], QUARTER, "hi1"))
-        finish(0, HALF, 3, 38)
+        finish(0, HALF, 3, 50.25)
         close_banks(HALF + QUARTER, QUARTER, quantise_z(grouped_last[1], QUARTER, "hi2"))
         for c in range(2):
             for k in range(2):
-                finish(HALF + QUARTER * c, QUARTER, k, 56 + 4 * c + 2 * k)
+                finish(HALF + QUARTER * c, QUARTER, k, 16.25 + 4 * c + 2 * k)

@@ -1,6 +1,7 @@
 from contextlib import ExitStack
 
 import concourse.mybir as mybir
+from concourse.masks import make_identity
 
 K, T, S, T2, E, H, N = 1024, 4096, 1024, 2048, 1024, 1024, 512
 FLOPS = 2 * K * H * S + 2 * H * N * E
@@ -21,6 +22,11 @@ P = 128
 KIB = 1024
 HALF = 512
 QUARTER = 256
+STAGED = 96
+LAP = 0.0625
+FIRST_PIECES = ((0, QUARTER), (QUARTER, QUARTER), (HALF, HALF))
+TURNED = ((0, QUARTER), (QUARTER, QUARTER), (HALF, QUARTER))
+DIRECT = ((HALF + QUARTER, P), (HALF + QUARTER + P, P))
 
 
 def tile_list_tsunami_edge_fluxes_kernel(
@@ -31,7 +37,6 @@ def tile_list_tsunami_edge_fluxes_kernel(
         lists = ctx.enter_context(tc.tile_pool(name="lists", bufs=1))
         keep = ctx.enter_context(tc.tile_pool(name="keep", bufs=1))
         shared = ctx.enter_context(tc.tile_pool(name="shared", bufs=1))
-        ring = ctx.enter_context(tc.tile_pool(name="ring", bufs=2))
         psum = ctx.enter_context(tc.psum_pool(name="psum", bufs=8))
 
         def placed(name, shape, dtype, kib):
@@ -43,22 +48,26 @@ def tile_list_tsunami_edge_fluxes_kernel(
         idx4 = lists.tile([P, E // 16], U16, name="idx4")
 
         tab = [placed("tab%d" % a, [P, T], I32, 16 * a) for a in range(2)]
-        wgs_hi = placed("wgs_hi", [P, 4, S], F32, 0.25)
-        w1_nat = [placed("w1_nat%d" % i, [P, 2, 4, P], F32, kib) for i, kib in enumerate((44.25, 148, 20.25, 24.25))]
-        w1_hi = placed("w1_hi", [P, 2, 4, HALF], F32, 28.25)
-        tab_sc = placed("tab_sc", [P, T], U8, 159.9375)
-        v_words = [placed("v_words%d" % a, [P, S], U32, kib) for a, kib in enumerate((52.25, 48.25))]
-        bstep_lo = placed("bstep_lo", [P, 4, E], F32, 90)
-        bstep_hi = placed("bstep_hi", [P, 4, E], F32, 106.875)
-        w2_w = placed("w2_w", [P, 2, 2 * N], U8, 123)
-        le_all = placed("le_all", [P, E], F32, 126.875)
-        picked_sc = placed("picked_sc", [P, S], U8, 171.9375)
-        w2_sc = placed("w2_sc", [P, 2, N], U8, 131)
+        bstep_lo = [placed("bstep_lo%d" % c, [P, 2, E], F32, kib) for c, kib in enumerate((8 + LAP, 67 + 3 * LAP))]
+        w1_nat = [
+            placed("w1_nat%d" % i, [P, 2, 4, P], F32, kib) for i, kib in enumerate((57.125, 122, 16 + LAP, 20 + LAP))
+        ]
+        w1_hi = placed("w1_hi", [P, 2, 4, HALF], F32, 24 + LAP)
+        wgs_lo = placed("wgs_lo", [P, S], F32, 40.125)
+        v_words = [placed("v_words%d" % a, [P, S], U32, 44.125 + 4 * a) for a in range(2)]
+        tab_sc = placed("tab_sc", [P, T], U8, 52.125)
+        picked_sc = placed("picked_sc", [P, S], U8, 56.125)
+        wgs_hi = placed("wgs_hi", [P, 4, S], F32, 76 + LAP)
+        bstep_hi = placed("bstep_hi", [P, 4, E], F32, 94 + LAP)
+        w2_w = placed("w2_w", [P, 2, 2 * N], U8, 112 - LAP)
+        pages = [placed("page%d" % i, [P, T2], F32, kib) for i, kib in enumerate((132, 0, 114 + LAP, 124 - LAP))]
+        le_tail = placed("le_tail", [P, QUARTER], F32, 140 + LAP)
+        w2_sc = placed("w2_sc", [P, 2, N], U8, 146 + LAP)
+        le_col = placed("le_col", [P, 6], F32, 147 + 3 * LAP)
         v_sc = keep.tile([P, S], U8, name="v_sc", align_bytes=64)
-        pages = [placed("page%d" % i, [P, T2], F32, kib) for i, kib in enumerate((181, 152, 164, 172.875))]
         bias_lo = keep.tile([P, 4], F32, name="bias_lo")
         bias_hi = keep.tile([P, 4], F32, name="bias_hi")
-        wgs_lo = keep.tile([P, S], F32, name="wgs_lo")
+        ident = keep.tile([P, P], F32, name="ident")
 
         def load_w1_nat(i):
             for a in range(2):
@@ -68,26 +77,29 @@ def tile_list_tsunami_edge_fluxes_kernel(
         def load_tab(a):
             nc.sync.dma_start(out=tab[a][:], in_=tab_words[a].rearrange("p t i -> p (t i)").bitcast(I32))
 
-        for rows in (slice(32, 64), slice(64, P)):
-            nc.vector.memset(tab_sc[rows, :].bitcast(I32), 0)
+        def load_bstep_lo(c):
+            rows = bstep[QUARTER * c : QUARTER * (c + 1), :]
+            nc.sync.dma_start(out=bstep_lo[c][:], in_=rows.rearrange("(i p) m -> p i m", p=P))
+
+        def list_cols(m0, width):
+            return slice(m0 // 16, (m0 + width) // 16)
+
+        nc.vector.memset(tab_sc[0:STAGED, :].bitcast(I32), 0)
         for r in range(4):
             nc.sync.dma_start(
-                out=tab_sc[r:32:4, :].bitcast(I32),
+                out=tab_sc[STAGED + r : P : 4, :].bitcast(I32),
                 in_=tab_scales.rearrange("a (q r) t -> r q a t", r=4)[r].bitcast(I32),
             )
         nc.sync.dma_start(idx[:], offs)
         nc.vector.memset(v_sc[:].bitcast(I32), 0)
+        nc.vector.memset(pages[0][:], 0.0)
         nc.vector.tensor_copy(out=picked_sc[:], in_=tab_sc[:].indirect(idx[:]))
         for q in range(4):
             nc.gpsimd.dma_start(
-                out=v_sc[32 * q : 32 * q + 8, :].bitcast(I32), in_=picked_sc[8 * q : 8 * q + 8, :].bitcast(I32)
+                out=v_sc[32 * q : 32 * q + 8, :].bitcast(I32),
+                in_=picked_sc[STAGED + 8 * q : STAGED + 8 * q + 8, :].bitcast(I32),
             )
-        for i in range(2):
-            nc.vector.memset(pages[i][:], 0.0)
-        for i in range(2, 4):
-            for c0 in range(0, T2, HALF):
-                nc.gpsimd.memset(pages[i][:, c0 : c0 + HALF], 0.0)
-        nc.vector.memset(w2_sc[:].rearrange("p a c -> p (a c)").bitcast(I32), 0)
+        make_identity(nc, ident[:])
 
         load_tab(0)
         load_w1_nat(0)
@@ -97,13 +109,10 @@ def tile_list_tsunami_edge_fluxes_kernel(
         nc.sync.dma_start(idx2[:], offs2)
         for s0 in range(0, S, HALF):
             nc.sync.dma_start(out=wgs_lo[:, s0 : s0 + HALF], in_=wgs[:, s0 : s0 + HALF])
+        load_w1_nat(1)
         nc.sync.dma_start(idx3[:], offs3)
         nc.sync.dma_start(idx4[:], offs4)
         nc.sync.dma_start(out=bias_hi[:], in_=b1[HALF:H].rearrange("(p t) -> p t", t=4))
-        load_w1_nat(1)
-
-        def list_cols(m0, width):
-            return slice(m0 // 16, (m0 + width) // 16)
 
         def cast_w1(first, count, grouped_at):
             grouped = placed("w1_grouped%d" % first, [P, count, 2, P, 4], BF16, grouped_at)
@@ -127,122 +136,131 @@ def tile_list_tsunami_edge_fluxes_kernel(
             )
             return [(codes[:, i], scales[:, i]) for i in range(count)]
 
-        def multiply_h(quantised, s0):
+        def h_pass(acc, quantised, a, s0, width):
             codes, scales = quantised
-            cols = slice(s0, s0 + HALF)
-            acc = psum.tile([P, HALF], F32, name="acc_h", tag="bank")
-            for a in range(2):
-                nc.tensor.matmul_mx(
-                    out=acc[:],
-                    lhsT=codes[:, P * a : P * (a + 1)].bitcast(FP8X4),
-                    lhsT_scale=scales[:, P * a : P * (a + 1)],
-                    rhs=v_words[a][:, cols].bitcast(FP8X4),
-                    rhs_scale=v_sc[4 * a : P, cols],
-                    start=(a == 0),
-                    stop=(a == 1),
-                )
-            return acc
+            cols = slice(s0, s0 + width)
+            nc.tensor.matmul_mx(
+                out=acc[:],
+                lhsT=codes[:, P * a : P * (a + 1)].bitcast(FP8X4),
+                lhsT_scale=scales[:, P * a : P * (a + 1)],
+                rhs=v_words[a][:, cols].bitcast(FP8X4),
+                rhs_scale=v_sc[4 * a : P, cols],
+                start=(a == 0),
+                stop=(a == 1),
+            )
 
         def add_bias(dst, acc, bias):
             nc.scalar.activation(out=dst, in_=acc[:], func=IDENT, bias=bias)
 
-        def make_h(h, quantised, bias):
+        def make_h(i, quantised, bias):
+            h = placed("h%d" % i, [P, S], F32, (204.5, 52.125, 57.125, 61.125)[i % 4])
             for s0 in range(0, S, HALF):
-                add_bias(h[:, s0 : s0 + HALF], multiply_h(quantised, s0), bias)
+                acc = psum.tile([P, HALF], F32, name="acc_h", tag="bank")
+                for a in range(2):
+                    h_pass(acc, quantised, a, s0, HALF)
+                add_bias(h[:, s0 : s0 + HALF], acc, bias)
             return h
-
-        def h_tile(i):
-            return placed("h%d" % i, [P, S], F32, 72.25 + 4 * (i % 4))
 
         def scatter(page, h, weights, s0, width):
             nc.vector.tensor_tensor(
-                out=page[:].indirect(idx2[:, list_cols(s0, width)]), in0=h[:], in1=weights[:, s0 : s0 + width], op=MULT
+                out=page[:].indirect(idx2[:, list_cols(s0, width)]), in0=h, in1=weights[:, s0 : s0 + width], op=MULT
             )
 
         def gather_minus(dst, page, which, m0, width, other):
             nc.vector.tensor_tensor(out=dst, in0=page[:].indirect(which[:, list_cols(m0, width)]), in1=other, op=SUB)
 
         nc.vector.tensor_copy(out=v_words[0][:], in_=tab[0][:].bitcast(U32).indirect(idx[:]))
-        w1_q = quantise_w1(0, cast_w1(0, 1, 60.25), 105.9375, 56.25)
-        for s0 in range(0, S, HALF):
-            nc.vector.tensor_copy(
-                out=v_words[1][:, s0 : s0 + HALF],
-                in_=tab[1][:].bitcast(U32).indirect(idx[:, list_cols(s0, HALF)]),
-            )
-        h_first = [placed("h_first%d" % c, [P, HALF], F32, kib) for c, kib in enumerate((68.25, 124.9375))]
-        acc_first = [multiply_h(w1_q[0], HALF * c) for c in range(2)]
+        nc.vector.memset(pages[1][:], 0.0)
+        w1_q = quantise_w1(0, cast_w1(0, 1, 65.125), 75.125, 92 + LAP)
+        acc_first = []
+        for s0, width in FIRST_PIECES:
+            acc = psum.tile([P, width], F32, name="acc_first", tag="bank")
+            h_pass(acc, w1_q[0], 0, s0, width)
+            acc_first.append(acc)
+        h_first = [placed("h_first%d" % c, [P, HALF], F32, kib) for c, kib in enumerate((110, 122))]
+        for (s0, width), acc in zip(FIRST_PIECES, acc_first):
+            if s0 % HALF == 0:
+                nc.vector.tensor_copy(
+                    out=v_words[1][:, s0 : s0 + HALF],
+                    in_=tab[1][:].bitcast(U32).indirect(idx[:, list_cols(s0, HALF)]),
+                )
+            h_pass(acc, w1_q[0], 1, s0, width)
+            if s0 < HALF:
+                add_bias(h_first[0][:, s0 : s0 + width], acc, bias_lo[:, 0:1])
+
         load_w1_nat(2)
         load_w1_nat(3)
+        load_bstep_lo(0)
         for a in range(2):
             rows = w1[HALF * a : HALF * (a + 1), HALF:H]
             nc.sync.dma_start(out=w1_hi[:, a], in_=rows.rearrange("(p j) c -> p j c", j=4))
+        load_bstep_lo(1)
         for q in range(4):
             nc.sync.dma_start(out=wgs_hi[32 * q : 32 * (q + 1)], in_=wgs.rearrange("(p t) j -> p t j", t=4))
-        nc.sync.dma_start(out=bstep_lo[:], in_=bstep[0:HALF, :].rearrange("(i p) m -> p i m", p=P))
+
+        grouped_second = cast_w1(1, 1, 92 + LAP)
+        add_bias(h_first[1][:], acc_first[-1], bias_lo[:, 0:1])
+        scatter(pages[0], h_first[0][:], wgs_lo, 0, HALF)
+        w1_q = w1_q + quantise_w1(1, grouped_second, 141, 147)
+        scatter(pages[0], h_first[1][:], wgs_lo, HALF, HALF)
+        nc.sync.dma_start(out=bstep_hi[:], in_=bstep[HALF:H, :].rearrange("(p t) m -> p t m", t=4))
+        nc.sync.dma_start(out=w2_w[:].bitcast(I32), in_=w2_words.rearrange("a p c -> p a c").bitcast(I32))
+        h = {1: make_h(1, w1_q[1], bias_lo[:, 1:2])}
+        scatter(pages[1], h[1][:], wgs_lo, 0, S)
+
+        for i in range(2, 4):
+            for c0 in range(0, T2, HALF):
+                nc.gpsimd.memset(pages[i][:, c0 : c0 + HALF], 0.0)
+        nc.gpsimd.memset(w2_sc[:].rearrange("p a c -> p (a c)").bitcast(I32), 0)
+        nc.sync.dma_start(out=le_tail[:], in_=le[E - QUARTER : E].partition_broadcast(P))
+        with nc.allow_non_contiguous_dma(reason="one length factor a partition"):
+            nc.sync.dma_start(out=le_col[:], in_=le[0 : E - QUARTER].rearrange("(c p) -> p c", p=P))
         for q in range(4):
             nc.sync.dma_start(
                 out=w2_sc[32 * q : 32 * q + 4].bitcast(I32),
                 in_=w2_scales[:, 4 * q : 4 * q + 4, :].rearrange("a r c -> r a c").bitcast(I32),
             )
-        nc.sync.dma_start(out=bstep_hi[:], in_=bstep[HALF:H, :].rearrange("(p t) m -> p t m", t=4))
 
-        add_bias(h_first[0][:], acc_first[0], bias_lo[:, 0:1])
-        grouped_second = cast_w1(1, 1, 56.25)
-        add_bias(h_first[1][:], acc_first[1], bias_lo[:, 0:1])
-        scatter(pages[0], h_first[0], wgs_lo, 0, HALF)
-        w1_q = w1_q + quantise_w1(1, grouped_second, 58.25, 59.25)
-        scatter(pages[0], h_first[1], wgs_lo, HALF, HALF)
-        nc.sync.dma_start(out=w2_w[:].bitcast(I32), in_=w2_words.rearrange("a p c -> p a c").bitcast(I32))
-        nc.sync.dma_start(out=le_all[:], in_=le.partition_broadcast(P))
+        w1_q = w1_q + quantise_w1(2, cast_w1(2, 2, 142 - LAP), 147.5, 149.5)
+        for i in range(2, 4):
+            h[i] = make_h(i, w1_q[i], bias_lo[:, i : i + 1])
 
-        z_lo = placed("z_lo", [P, 4, E], F32, 132)
+        z_lo = placed("z_lo", [P, 4, E], F32, 179)
 
-        def left_lo(i):
-            y = ring.tile([P, E], F32, name="y_lo", bufs=3)
-            gather_minus(y[:], pages[i], idx3, 0, E, bstep_lo[:, i, :])
-            return y
+        def gather_lo(first):
+            y = [placed("y_lo%d" % (first + c), [P, E], F32, 171 + 4 * c) for c in range(2)]
+            for c in range(2):
+                gather_minus(y[c][:], pages[c], idx3, 0, E, bstep_lo[first // 2][:, c, :])
+            for c in range(2):
+                i = first + c
+                z_nat = placed("z_nat%d" % i, [P, E], F32, (142 - LAP, 158, 150, 162)[i])
+                gather_minus(z_nat[:], pages[c], idx4, 0, E, y[c][:])
+                for t in range(4):
+                    nc.sync.dma_start(out=z_lo[32 * i : 32 * (i + 1), t, :], in_=z_nat[t:P:4, :])
 
-        def right_lo(i, y):
-            z_nat = placed("z_nat%d" % i, [P, E], F32, (16.25, 20.25, 28.25, 32.25)[i])
-            gather_minus(z_nat[:], pages[i], idx4, 0, E, y[:])
-            for t in range(4):
-                nc.sync.dma_start(out=z_lo[32 * i : 32 * (i + 1), t, :], in_=z_nat[t:P:4, :])
+        gather_lo(0)
 
-        w1_q = w1_q + quantise_w1(2, cast_w1(2, 2, 68.25), 60.25, 62.25)
-        h = {i: make_h(h_tile(i), w1_q[i], bias_lo[:, i : i + 1]) for i in range(1, 4)}
-
-        grouped_hi = placed("grouped_hi", [P, 4, 2, P, 4], BF16, 60.25)
+        grouped_hi = placed("grouped_hi", [P, 4, 2, P, 4], BF16, 150)
         for a in range(2):
             nc.scalar.activation(
                 out=grouped_hi[:].rearrange("p t a c j -> p a c t j")[:, a],
                 in_=w1_hi[:, a].rearrange("p j (c t) -> p c t j", t=4),
                 func=IDENT,
             )
-        codes_hi = keep.tile([P, 4, 2 * P], U32, name="codes_hi", align_bytes=64)
-        scales_hi = keep.tile([P, 4, 2 * P], U8, name="scales_hi", align_bytes=64)
+        for c in range(2):
+            scatter(pages[c], h[2 + c][:], wgs_lo, 0, S)
+        codes_hi = placed("codes_hi", [P, 4, 2 * P], U32, 166)
+        scales_hi = placed("scales_hi", [P, 4, 2 * P], U8, 170)
         nc.vector.quantize_mx(
             out=codes_hi[:].rearrange("p t c -> p (t c)").bitcast(FP8X4),
             scales=scales_hi[:].rearrange("p t c -> p (t c)"),
             in_=grouped_hi[:].rearrange("p t a c j -> p (t a c j)"),
         )
-
-        def scatter_tile(i):
-            if i < 4:
-                scatter(pages[i], h[i], wgs_lo, 0, S)
-            else:
-                t = i - 4
-                h_hi = make_h(h_tile(i), (codes_hi[:, t], scales_hi[:, t]), bias_hi[:, t : t + 1])
-                scatter(pages[t], h_hi, wgs_hi[:, t, :], 0, S)
-
-        for i in range(1, 4):
-            scatter_tile(i)
-        y = {0: left_lo(0)}
-        for i in range(3):
-            y[i + 1] = left_lo(i + 1)
-            right_lo(i, y[i])
-        right_lo(3, y[3])
-        for i in range(4, 8):
-            scatter_tile(i)
+        h_hi = [make_h(4 + t, (codes_hi[:, t], scales_hi[:, t]), bias_hi[:, t : t + 1]) for t in range(4)]
+        gather_lo(2)
+        pages_hi = pages[2:] + pages[:2]
+        for t in range(4):
+            scatter(pages_hi[t], h_hi[t][:], wgs_hi[:, t, :], 0, S)
 
         def interleave_z(src, grouped):
             nc.scalar.activation(
@@ -251,86 +269,124 @@ def tile_list_tsunami_edge_fluxes_kernel(
                 func=IDENT,
             )
 
-        def quantise_z(grouped, width, name):
-            codes = keep.tile([P, width], U32, name="zc_" + name, align_bytes=64)
-            scales = keep.tile([P, width], U8, name="zs_" + name, align_bytes=64)
-            nc.vector.quantize_mx(
-                out=codes[:].bitcast(FP8X4), scales=scales[:], in_=grouped[:].rearrange("p m t -> p (m t)")
-            )
-            return codes, scales
+        z_codes = [placed("z_codes%d" % a, [P, E], U32, 195) for a in range(1)]
+        z_scales = [placed("z_scales%d" % a, [P, E], U8, 199) for a in range(1)]
 
-        zq_lo = []
+        def quantise_z(grouped, codes, scales):
+            nc.vector.quantize_mx(out=codes.bitcast(FP8X4), scales=scales, in_=grouped[:].rearrange("p m t -> p (m t)"))
+
         for c, m0 in enumerate(range(0, E, HALF)):
-            grouped = placed("zg_lo%d" % c, [P, HALF, 4], BF16, 72.25 + 4 * c)
+            grouped = placed("zg_lo%d" % c, [P, HALF, 4], BF16, 24 + LAP + 4 * c)
             interleave_z(z_lo[:, :, m0 : m0 + HALF], grouped)
-            zq_lo.append(quantise_z(grouped, HALF, "lo%d" % c))
+            quantise_z(grouped, z_codes[0][:, m0 : m0 + HALF], z_scales[0][:, m0 : m0 + HALF])
 
-        def out_pass(acc, a, width, blocks, codes, scales, z0):
-            step = HALF if width == HALF else P
-            pieces = [(k, c0) for k in range(len(blocks)) for c0 in range(0, width, step)]
-            for k, c0 in pieces:
-                b = blocks[k]
-                zcols = slice(z0 + c0, z0 + c0 + step)
-                nc.tensor.matmul_mx(
-                    out=acc[:, k, c0 : c0 + step],
-                    lhsT=w2_w[:, a, 2 * P * b : 2 * P * (b + 1)].bitcast(FP4X4),
-                    lhsT_scale=w2_sc[:, a, P * b : P * (b + 1)],
-                    rhs=codes[:, zcols].bitcast(FP8X4),
-                    rhs_scale=scales[:, zcols],
-                    start=(a == 0 and (k, c0) == pieces[0]),
-                    stop=(a == 1 and (k, c0) == pieces[-1]),
-                )
-
-        def open_banks(m0, width):
-            per_bank = HALF // width
-            opened = []
-            for b0 in range(0, 4, per_bank):
-                blocks = list(range(b0, b0 + per_bank))
-                acc = psum.tile([P, per_bank, width], F32, name="acc_out", tag="bank")
-                lo_codes, lo_scales = zq_lo[m0 // HALF]
-                out_pass(acc, 0, width, blocks, lo_codes, lo_scales, m0 % HALF)
-                opened.append((acc, blocks))
-            return opened
-
-        banks = {0: open_banks(0, HALF), HALF: open_banks(HALF, QUARTER), HALF + QUARTER: open_banks(HALF + QUARTER, QUARTER)}
         out_v = out.rearrange("(b p) m -> p b m", p=P)
 
-        def gather_hi(m0, y_at):
-            cols = slice(m0, m0 + HALF)
-            y = [placed("y_hi%d_%d" % (m0, t), [P, HALF], F32, y_at + 2 * t) for t in range(4)]
-            z_hi = placed("z_hi%d" % m0, [P, 4, HALF], F32, 132)
+        def direct_pass(acc, a, codes, scales):
+            for b in range(4):
+                nc.tensor.matmul_mx(
+                    out=acc[:, b, :],
+                    lhsT=w2_w[:, a, 2 * P * b : 2 * P * (b + 1)].bitcast(FP4X4),
+                    lhsT_scale=w2_sc[:, a, P * b : P * (b + 1)],
+                    rhs=codes.bitcast(FP8X4),
+                    rhs_scale=scales,
+                    start=(a == 0 and b == 0),
+                    stop=(a == 1 and b == 3),
+                )
+
+        direct_acc = {}
+        for m0, width in DIRECT:
+            acc = psum.tile([P, 4, width], F32, name="acc_direct", tag="bank")
+            direct_pass(acc, 0, z_codes[0][:, m0 : m0 + width], z_scales[0][:, m0 : m0 + width])
+            direct_acc[m0] = acc
+
+        def gather_left(m0, width):
+            y = [placed("y_hi%d_%d" % (m0, t), [P, width], F32, 16 + LAP + t) for t in range(4)]
             for t in range(4):
-                gather_minus(y[t][:], pages[t], idx3, m0, HALF, bstep_hi[:, t, cols])
+                gather_minus(y[t][:], pages_hi[t], idx3, m0, width, bstep_hi[:, t, m0 : m0 + width])
+            return y
+
+        def gather_right(m0, width, y):
+            z_hi = placed("z_hi%d" % m0, [P, 4, width], F32, 179)
             for t in range(4):
-                gather_minus(z_hi[:, t, :], pages[t], idx4, m0, HALF, y[t][:])
+                gather_minus(z_hi[:, t, :], pages_hi[t], idx4, m0, width, y[t][:])
             return z_hi
 
-        def close_banks(m0, width, quantised):
-            for acc, blocks in banks[m0]:
-                out_pass(acc, 1, width, blocks, quantised[0], quantised[1], 0)
+        def group_hi(c, width, z_hi):
+            grouped = placed("zg_hi%d" % c, [P, width, 4], BF16, 209 + 2 * (c % 2))
+            interleave_z(z_hi[:], grouped)
+            return grouped
 
-        def finish(m0, width, k, res_at):
-            acc, blocks = banks[m0][k]
-            cols = slice(m0, m0 + width)
-            res = placed("res%d_%d" % (m0, k), [P, len(blocks), width], F32, res_at)
-            factors = le_all[:, cols].unsqueeze(1).to_broadcast([P, len(blocks), width])
-            nc.vector.tensor_tensor(out=res[:], in0=acc[:], in1=factors, op=MULT)
-            nc.sync.dma_start(out=out_v[:, blocks[0] : blocks[-1] + 1, cols], in_=res[:])
+        def quantise_hi(m0, width, grouped):
+            codes = placed("zc_hi%d" % m0, [P, width], U32, 200 + m0 / 256)
+            scales = placed("zs_hi%d" % m0, [P, width], U8, 221 + m0 / 1024)
+            quantise_z(grouped, codes[:], scales[:])
+            return codes, scales
 
-        z_first = gather_hi(0, 44.25)
-        grouped = placed("zg_hi0", [P, HALF, 4], BF16, 36.25)
-        interleave_z(z_first[:], grouped)
-        close_banks(0, HALF, quantise_z(grouped, HALF, "hi0"))
+        def multiply_turned(m0, width, quantised):
+            banks = []
+            for j in range(width // P):
+                acc = psum.tile([P, N], F32, name="acc_turned", tag="bank")
+                lo = slice(m0 + P * j, m0 + P * (j + 1))
+                hi = slice(P * j, P * (j + 1))
+                sides = ((z_codes[0][:, lo], z_scales[0][:, lo]), (quantised[0][:, hi], quantised[1][:, hi]))
+                for a, (codes, scales) in enumerate(sides):
+                    nc.tensor.matmul_mx(
+                        out=acc[:],
+                        lhsT=codes.bitcast(FP8X4),
+                        lhsT_scale=scales,
+                        rhs=w2_w[:, a, :].bitcast(FP4X4),
+                        rhs_scale=w2_sc[:, a, :],
+                        start=(a == 0),
+                        stop=(a == 1),
+                    )
+                banks.append(acc)
+            return banks
 
-        z_last = gather_hi(HALF, 44.25)
-        grouped_last = [placed("zg_hi%d" % (1 + c), [P, QUARTER, 4], BF16, 40.25 + 2 * c) for c in range(2)]
-        for c in range(2):
-            interleave_z(z_last[:, :, QUARTER * c : QUARTER * (c + 1)], grouped_last[c])
-        for k in range(3):
-            finish(0, HALF, k, 44.25 + 2 * k)
-        close_banks(HALF, QUARTER, quantise_z(grouped_last[0], QUARTER, "hi1"))
-        finish(0, HALF, 3, 50.25)
-        close_banks(HALF + QUARTER, QUARTER, quantise_z(grouped_last[1], QUARTER, "hi2"))
-        for c in range(2):
-            for k in range(2):
-                finish(HALF + QUARTER * c, QUARTER, k, 16.25 + 4 * c + 2 * k)
+        def scale_and_turn(m0, banks):
+            turned = []
+            for j, acc in enumerate(banks):
+                block = m0 // P + j
+                scaled = placed("scaled%d" % block, [P, N], F32, 213 + 2 * (block % 4))
+                nc.scalar.activation(out=scaled[:], in_=acc[:], func=IDENT, scale=le_col[:, block : block + 1])
+                back = psum.tile([P, 4, P], F32, name="acc_back", tag="bank")
+                for b in range(4):
+                    nc.tensor.transpose(back[:, b, :], scaled[:, P * b : P * (b + 1)], ident[:])
+                turned.append(back)
+            return turned
+
+        def store_turned(m0, width, turned):
+            res = placed("res%d" % m0, [P, 4, width], F32, (8 + LAP, 12 + LAP, 32 + LAP)[m0 // QUARTER])
+            for j, back in enumerate(turned):
+                nc.scalar.copy(out=res[:, :, P * j : P * (j + 1)], in_=back[:])
+            nc.sync.dma_start(out=out_v[:, :, m0 : m0 + width], in_=res[:])
+
+        def store_direct(m0, width):
+            res = placed("res%d" % m0, [P, 4, width], F32, 36 + LAP + (m0 - DIRECT[0][0]) / 64)
+            cols = slice(m0 - DIRECT[0][0], m0 - DIRECT[0][0] + width)
+            factors = le_tail[:, cols].unsqueeze(1).to_broadcast([P, 4, width])
+            nc.vector.tensor_tensor(out=res[:], in0=direct_acc[m0][:], in1=factors, op=MULT)
+            nc.sync.dma_start(out=out_v[:, :, m0 : m0 + width], in_=res[:])
+
+        chunks = TURNED + DIRECT
+        grouped = {}
+        turned = {}
+        for c in range(len(chunks) + 1):
+            if c < len(chunks):
+                y = gather_left(*chunks[c])
+            if c == len(chunks):
+                store_direct(*chunks[c - 2])
+            if c >= 1:
+                m0, width = chunks[c - 1]
+                quantised = quantise_hi(m0, width, grouped[c - 1])
+                if c - 1 < len(TURNED):
+                    banks = multiply_turned(m0, width, quantised)
+                else:
+                    direct_pass(direct_acc[m0], 1, quantised[0][:], quantised[1][:])
+            if 0 <= c - 2 < len(TURNED):
+                store_turned(*chunks[c - 2], turned[c - 2])
+            if 0 <= c - 1 < len(TURNED):
+                turned[c - 1] = scale_and_turn(chunks[c - 1][0], banks)
+            if c < len(chunks):
+                grouped[c] = group_hi(c, chunks[c][1], gather_right(*chunks[c], y))
+        store_direct(*chunks[-1])

@@ -25,8 +25,9 @@ QUARTER = 256
 STAGED = 96
 LAP = 0.0625
 FIRST_PIECES = ((0, QUARTER), (QUARTER, QUARTER), (HALF, HALF))
-TURNED = ((0, QUARTER), (QUARTER, QUARTER), (HALF, QUARTER))
-DIRECT = ((HALF + QUARTER, P), (HALF + QUARTER + P, P))
+TURNED = ((0, QUARTER), (QUARTER, QUARTER), (HALF, P))
+DIRECT = ((HALF + P, P), (HALF + 2 * P, P), (HALF + 3 * P, P))
+TURNED_EDGES = HALF + P
 
 
 def tile_list_tsunami_edge_fluxes_kernel(
@@ -47,23 +48,23 @@ def tile_list_tsunami_edge_fluxes_kernel(
         idx3 = lists.tile([P, E // 16], U16, name="idx3")
         idx4 = lists.tile([P, E // 16], U16, name="idx4")
 
-        tab = [placed("tab%d" % a, [P, T], I32, 16 * a) for a in range(2)]
-        bstep_lo = [placed("bstep_lo%d" % c, [P, 2, E], F32, kib) for c, kib in enumerate((8 + LAP, 67 + 3 * LAP))]
+        tab = [placed("tab%d" % a, [P, T], I32, 16 * a + LAP) for a in range(2)]
+        bstep_lo = [placed("bstep_lo%d" % c, [P, 2, E], F32, kib) for c, kib in enumerate((24, 67 + 3 * LAP))]
         w1_nat = [
-            placed("w1_nat%d" % i, [P, 2, 4, P], F32, kib) for i, kib in enumerate((57.125, 122, 16 + LAP, 20 + LAP))
+            placed("w1_nat%d" % i, [P, 2, 4, P], F32, kib) for i, kib in enumerate((57.125, 12, 16, 20))
         ]
-        w1_hi = placed("w1_hi", [P, 2, 4, HALF], F32, 24 + LAP)
-        wgs_lo = placed("wgs_lo", [P, S], F32, 40.125)
-        v_words = [placed("v_words%d" % a, [P, S], U32, 44.125 + 4 * a) for a in range(2)]
+        w1_hi = placed("w1_hi", [P, 2, 4, HALF], F32, 32)
+        wgs_lo = placed("wgs_lo", [P, S], F32, 8)
+        v_words = [placed("v_words%d" % a, [P, S], U32, kib) for a, kib in enumerate((132, 48))]
         tab_sc = placed("tab_sc", [P, T], U8, 52.125)
         picked_sc = placed("picked_sc", [P, S], U8, 56.125)
         wgs_hi = placed("wgs_hi", [P, 4, S], F32, 76 + LAP)
         bstep_hi = placed("bstep_hi", [P, 4, E], F32, 94 + LAP)
         w2_w = placed("w2_w", [P, 2, 2 * N], U8, 112 - LAP)
-        pages = [placed("page%d" % i, [P, T2], F32, kib) for i, kib in enumerate((132, 0, 114 + LAP, 124 - LAP))]
-        le_tail = placed("le_tail", [P, QUARTER], F32, 140 + LAP)
+        pages = [placed("page%d" % i, [P, T2], F32, kib) for i, kib in enumerate((223, 0, 114 + LAP, 124 - LAP))]
+        le_tail = placed("le_tail", [P, E - TURNED_EDGES], F32, 139.5 + LAP)
         w2_sc = placed("w2_sc", [P, 2, N], U8, 146 + LAP)
-        le_col = placed("le_col", [P, 6], F32, 147 + 3 * LAP)
+        le_col = placed("le_col", [P, TURNED_EDGES // P], F32, 147 + 3 * LAP)
         v_sc = keep.tile([P, S], U8, name="v_sc", align_bytes=64)
         bias_lo = keep.tile([P, 4], F32, name="bias_lo")
         bias_hi = keep.tile([P, 4], F32, name="bias_hi")
@@ -85,34 +86,32 @@ def tile_list_tsunami_edge_fluxes_kernel(
             return slice(m0 // 16, (m0 + width) // 16)
 
         nc.vector.memset(tab_sc[0:STAGED, :].bitcast(I32), 0)
-        for r in range(4):
-            nc.sync.dma_start(
-                out=tab_sc[STAGED + r : P : 4, :].bitcast(I32),
-                in_=tab_scales.rearrange("a (q r) t -> r q a t", r=4)[r].bitcast(I32),
-            )
+        nc.sync.dma_start(
+            out=tab_sc[STAGED:P, :].bitcast(I32), in_=tab_scales.rearrange("a q t -> (a q) t").bitcast(I32)
+        )
         nc.sync.dma_start(idx[:], offs)
+        nc.sync.dma_start(idx2[:], offs2)
+        with nc.allow_non_contiguous_dma(reason="one bias value a partition"):
+            nc.gpsimd.dma_start(out=bias_lo[:], in_=b1[0:HALF].rearrange("(i p) -> p i", p=P))
+        nc.gpsimd.dma_start(out=bias_hi[:], in_=b1[HALF:H].rearrange("(p t) -> p t", t=4))
         nc.vector.memset(v_sc[:].bitcast(I32), 0)
-        nc.vector.memset(pages[0][:], 0.0)
+        for c0 in range(0, T2, HALF):
+            nc.gpsimd.memset(pages[0][:, c0 : c0 + HALF], 0.0)
         nc.vector.tensor_copy(out=picked_sc[:], in_=tab_sc[:].indirect(idx[:]))
-        for q in range(4):
-            nc.gpsimd.dma_start(
-                out=v_sc[32 * q : 32 * q + 8, :].bitcast(I32),
-                in_=picked_sc[STAGED + 8 * q : STAGED + 8 * q + 8, :].bitcast(I32),
-            )
+        for a, queue in enumerate((nc.scalar, nc.gpsimd)):
+            for q in range(4):
+                row = STAGED + 16 * a + 4 * q
+                queue.dma_start(
+                    out=v_sc[32 * q + 4 * a : 32 * q + 4 * a + 4, :].bitcast(I32),
+                    in_=picked_sc[row : row + 4, :].bitcast(I32),
+                )
         make_identity(nc, ident[:])
 
         load_tab(0)
         load_w1_nat(0)
         load_tab(1)
-        with nc.allow_non_contiguous_dma(reason="one bias value a partition"):
-            nc.sync.dma_start(out=bias_lo[:], in_=b1[0:HALF].rearrange("(i p) -> p i", p=P))
-        nc.sync.dma_start(idx2[:], offs2)
-        for s0 in range(0, S, HALF):
-            nc.sync.dma_start(out=wgs_lo[:, s0 : s0 + HALF], in_=wgs[:, s0 : s0 + HALF])
-        load_w1_nat(1)
         nc.sync.dma_start(idx3[:], offs3)
         nc.sync.dma_start(idx4[:], offs4)
-        nc.sync.dma_start(out=bias_hi[:], in_=b1[HALF:H].rearrange("(p t) -> p t", t=4))
 
         def cast_w1(first, count, grouped_at):
             grouped = placed("w1_grouped%d" % first, [P, count, 2, P, 4], BF16, grouped_at)
@@ -170,14 +169,17 @@ def tile_list_tsunami_edge_fluxes_kernel(
             nc.vector.tensor_tensor(out=dst, in0=page[:].indirect(which[:, list_cols(m0, width)]), in1=other, op=SUB)
 
         nc.vector.tensor_copy(out=v_words[0][:], in_=tab[0][:].bitcast(U32).indirect(idx[:]))
+        for s0 in range(0, S, HALF):
+            nc.sync.dma_start(out=wgs_lo[:, s0 : s0 + HALF], in_=wgs[:, s0 : s0 + HALF])
+        load_w1_nat(1)
         nc.vector.memset(pages[1][:], 0.0)
-        w1_q = quantise_w1(0, cast_w1(0, 1, 65.125), 75.125, 92 + LAP)
+        w1_q = quantise_w1(0, cast_w1(0, 1, 65.125), 75.125, 123)
         acc_first = []
         for s0, width in FIRST_PIECES:
             acc = psum.tile([P, width], F32, name="acc_first", tag="bank")
             h_pass(acc, w1_q[0], 0, s0, width)
             acc_first.append(acc)
-        h_first = [placed("h_first%d" % c, [P, HALF], F32, kib) for c, kib in enumerate((110, 122))]
+        h_first = [placed("h_first%d" % c, [P, HALF], F32, kib) for c, kib in enumerate((110, 12))]
         for (s0, width), acc in zip(FIRST_PIECES, acc_first):
             if s0 % HALF == 0:
                 nc.vector.tensor_copy(
@@ -198,7 +200,7 @@ def tile_list_tsunami_edge_fluxes_kernel(
         for q in range(4):
             nc.sync.dma_start(out=wgs_hi[32 * q : 32 * (q + 1)], in_=wgs.rearrange("(p t) j -> p t j", t=4))
 
-        grouped_second = cast_w1(1, 1, 92 + LAP)
+        grouped_second = cast_w1(1, 1, 122)
         add_bias(h_first[1][:], acc_first[-1], bias_lo[:, 0:1])
         scatter(pages[0], h_first[0][:], wgs_lo, 0, HALF)
         w1_q = w1_q + quantise_w1(1, grouped_second, 141, 147)
@@ -212,9 +214,9 @@ def tile_list_tsunami_edge_fluxes_kernel(
             for c0 in range(0, T2, HALF):
                 nc.gpsimd.memset(pages[i][:, c0 : c0 + HALF], 0.0)
         nc.gpsimd.memset(w2_sc[:].rearrange("p a c -> p (a c)").bitcast(I32), 0)
-        nc.sync.dma_start(out=le_tail[:], in_=le[E - QUARTER : E].partition_broadcast(P))
+        nc.sync.dma_start(out=le_tail[:], in_=le[TURNED_EDGES:E].partition_broadcast(P))
         with nc.allow_non_contiguous_dma(reason="one length factor a partition"):
-            nc.sync.dma_start(out=le_col[:], in_=le[0 : E - QUARTER].rearrange("(c p) -> p c", p=P))
+            nc.sync.dma_start(out=le_col[:], in_=le[0:TURNED_EDGES].rearrange("(c p) -> p c", p=P))
         for q in range(4):
             nc.sync.dma_start(
                 out=w2_sc[32 * q : 32 * q + 4].bitcast(I32),
@@ -276,7 +278,7 @@ def tile_list_tsunami_edge_fluxes_kernel(
             nc.vector.quantize_mx(out=codes.bitcast(FP8X4), scales=scales, in_=grouped[:].rearrange("p m t -> p (m t)"))
 
         for c, m0 in enumerate(range(0, E, HALF)):
-            grouped = placed("zg_lo%d" % c, [P, HALF, 4], BF16, 24 + LAP + 4 * c)
+            grouped = placed("zg_lo%d" % c, [P, HALF, 4], BF16, 32 + 4 * c)
             interleave_z(z_lo[:, :, m0 : m0 + HALF], grouped)
             quantise_z(grouped, z_codes[0][:, m0 : m0 + HALF], z_scales[0][:, m0 : m0 + HALF])
 
@@ -301,15 +303,15 @@ def tile_list_tsunami_edge_fluxes_kernel(
             direct_acc[m0] = acc
 
         def gather_left(m0, width):
-            y = [placed("y_hi%d_%d" % (m0, t), [P, width], F32, 16 + LAP + t) for t in range(4)]
+            y = [placed("y_hi%d_%d" % (m0, t), [P, width], F32, 16 + t) for t in range(4)]
             for t in range(4):
                 gather_minus(y[t][:], pages_hi[t], idx3, m0, width, bstep_hi[:, t, m0 : m0 + width])
             return y
 
-        def gather_right(m0, width, y):
-            z_hi = placed("z_hi%d" % m0, [P, 4, width], F32, 179)
+        def gather_right(m0, width, y, z_at):
+            z_hi = placed("z_hi%d" % m0, [P, 4, width], F32, z_at)
             for t in range(4):
-                gather_minus(z_hi[:, t, :], pages_hi[t], idx4, m0, width, y[t][:])
+                gather_minus(z_hi[:, t, :], pages_hi[t], idx4, m0, width, y[t])
             return z_hi
 
         def group_hi(c, width, z_hi):
@@ -356,37 +358,43 @@ def tile_list_tsunami_edge_fluxes_kernel(
             return turned
 
         def store_turned(m0, width, turned):
-            res = placed("res%d" % m0, [P, 4, width], F32, (8 + LAP, 12 + LAP, 32 + LAP)[m0 // QUARTER])
+            res = placed("res%d" % m0, [P, 4, width], F32, (24, 28, 40)[m0 // QUARTER])
             for j, back in enumerate(turned):
                 nc.scalar.copy(out=res[:, :, P * j : P * (j + 1)], in_=back[:])
             nc.sync.dma_start(out=out_v[:, :, m0 : m0 + width], in_=res[:])
 
         def store_direct(m0, width):
-            res = placed("res%d" % m0, [P, 4, width], F32, 36 + LAP + (m0 - DIRECT[0][0]) / 64)
+            res = placed("res%d" % m0, [P, 4, width], F32, 42 + (m0 - DIRECT[0][0]) / 64)
             cols = slice(m0 - DIRECT[0][0], m0 - DIRECT[0][0] + width)
             factors = le_tail[:, cols].unsqueeze(1).to_broadcast([P, 4, width])
             nc.vector.tensor_tensor(out=res[:], in0=direct_acc[m0][:], in1=factors, op=MULT)
             nc.sync.dma_start(out=out_v[:, :, m0 : m0 + width], in_=res[:])
 
-        chunks = TURNED + DIRECT
         grouped = {}
         turned = {}
-        for c in range(len(chunks) + 1):
-            if c < len(chunks):
-                y = gather_left(*chunks[c])
-            if c == len(chunks):
-                store_direct(*chunks[c - 2])
+        for c in range(len(TURNED) + 1):
+            y = gather_left(QUARTER * c, QUARTER)
             if c >= 1:
-                m0, width = chunks[c - 1]
-                quantised = quantise_hi(m0, width, grouped[c - 1])
-                if c - 1 < len(TURNED):
-                    banks = multiply_turned(m0, width, quantised)
-                else:
-                    direct_pass(direct_acc[m0], 1, quantised[0][:], quantised[1][:])
-            if 0 <= c - 2 < len(TURNED):
-                store_turned(*chunks[c - 2], turned[c - 2])
-            if 0 <= c - 1 < len(TURNED):
-                turned[c - 1] = scale_and_turn(chunks[c - 1][0], banks)
-            if c < len(chunks):
-                grouped[c] = group_hi(c, chunks[c][1], gather_right(*chunks[c], y))
-        store_direct(*chunks[-1])
+                m0, width = TURNED[c - 1]
+                quantised = quantise_hi(m0, QUARTER, grouped[c - 1])
+                banks = multiply_turned(m0, width, quantised)
+                if width < QUARTER:
+                    direct_pass(direct_acc[m0 + width], 1, quantised[0][:, width:], quantised[1][:, width:])
+            if c >= 2:
+                store_turned(*TURNED[c - 2], turned[c - 2])
+            if c >= 1:
+                turned[c - 1] = scale_and_turn(m0, banks)
+            if c < len(TURNED):
+                grouped[c] = group_hi(c, QUARTER, gather_right(QUARTER * c, QUARTER, [part[:] for part in y], 179))
+        last = [
+            gather_right(m0, width, [part[:, P * j : P * (j + 1)] for part in y], 179 + 2 * j)
+            for j, (m0, width) in enumerate(DIRECT[1:])
+        ]
+        grouped_last = [group_hi(len(TURNED) + j, P, last[j]) for j in range(2)]
+        store_turned(*TURNED[-1], turned[len(TURNED) - 1])
+        store_direct(*DIRECT[0])
+        for j, (m0, width) in enumerate(DIRECT[1:]):
+            quantised = quantise_hi(m0, width, grouped_last[j])
+            direct_pass(direct_acc[m0], 1, quantised[0][:], quantised[1][:])
+        for m0, width in DIRECT[1:]:
+            store_direct(m0, width)

@@ -67,7 +67,8 @@ def tile_list_tsunami_edge_fluxes_kernel(
         le_col = placed("le_col", [P, TURNED_EDGES // P], F32, 147 + 3 * LAP)
         v_sc = keep.tile([P, S], U8, name="v_sc", align_bytes=64)
         bias_lo = keep.tile([P, 4], F32, name="bias_lo")
-        bias_hi = keep.tile([P, 4], F32, name="bias_hi")
+        bias_hi = placed("bias_hi", [P, 4], F32, 56.125)
+        bias_rows = keep.tile([P, P], F32, name="bias_rows")
         ident = keep.tile([P, P], F32, name="ident")
 
         def load_w1_nat(i):
@@ -91,9 +92,12 @@ def tile_list_tsunami_edge_fluxes_kernel(
         )
         nc.sync.dma_start(idx[:], offs)
         nc.sync.dma_start(idx2[:], offs2)
-        with nc.allow_non_contiguous_dma(reason="one bias value a partition"):
-            nc.gpsimd.dma_start(out=bias_lo[:], in_=b1[0:HALF].rearrange("(i p) -> p i", p=P))
-        nc.gpsimd.dma_start(out=bias_hi[:], in_=b1[HALF:H].rearrange("(p t) -> p t", t=4))
+        nc.gpsimd.memset(bias_rows[:], 0.0)
+        nc.gpsimd.dma_start(out=bias_rows[0:4, :], in_=b1[0:HALF].rearrange("(i p) -> i p", p=P))
+        make_identity(nc, ident[:])
+        bias_turned = psum.tile([P, P], F32, name="bias_turned", tag="bank")
+        nc.tensor.transpose(bias_turned[:], bias_rows[:], ident[:])
+        nc.scalar.activation(out=bias_lo[:], in_=bias_turned[:, 0:4], func=IDENT)
         nc.vector.memset(v_sc[:].bitcast(I32), 0)
         for c0 in range(0, T2, HALF):
             nc.gpsimd.memset(pages[0][:, c0 : c0 + HALF], 0.0)
@@ -105,7 +109,7 @@ def tile_list_tsunami_edge_fluxes_kernel(
                     out=v_sc[32 * q + 4 * a : 32 * q + 4 * a + 4, :].bitcast(I32),
                     in_=picked_sc[row : row + 4, :].bitcast(I32),
                 )
-        make_identity(nc, ident[:])
+        nc.gpsimd.dma_start(out=bias_hi[:], in_=b1[HALF:H].rearrange("(p t) -> p t", t=4))
 
         load_tab(0)
         load_w1_nat(0)

@@ -50,12 +50,12 @@ def tile_list_tsunami_edge_fluxes_kernel(
 
         tab = [placed("tab%d" % a, [P, T], I32, 16 * a + LAP) for a in range(2)]
         bstep_lo = [placed("bstep_lo%d" % c, [P, 2, E], F32, kib) for c, kib in enumerate((24, 67 + 3 * LAP))]
-        w1_nat = [
-            placed("w1_nat%d" % i, [P, 2, 4, P], F32, kib) for i, kib in enumerate((57.125, 12, 16, 20))
-        ]
+        w1_first = [placed("w1_first%d" % a, [P, 4, P], F32, kib) for a, kib in enumerate((57.125, 50))]
+        w1_nat = {i: placed("w1_nat%d" % i, [P, 2, 4, P], F32, kib) for i, kib in ((1, 12), (2, 16), (3, 20))}
         w1_hi = placed("w1_hi", [P, 2, 4, HALF], F32, 32)
         wgs_lo = placed("wgs_lo", [P, S], F32, 8)
-        v_words = [placed("v_words%d" % a, [P, S], U32, kib) for a, kib in enumerate((132, 48))]
+        v_words0 = placed("v_words0", [P, S], U32, 132)
+        v_words1 = [placed("v_words1_%d" % c, [P, HALF], U32, 48 + 2 * c) for c in range(2)]
         tab_sc = placed("tab_sc", [P, T], U8, 52.125)
         picked_sc = placed("picked_sc", [P, S], U8, 56.125)
         wgs_hi = placed("wgs_hi", [P, 4, S], F32, 76 + LAP)
@@ -75,6 +75,10 @@ def tile_list_tsunami_edge_fluxes_kernel(
             for a in range(2):
                 rows = w1[HALF * a : HALF * (a + 1), P * i : P * (i + 1)]
                 nc.sync.dma_start(out=w1_nat[i][:, a], in_=rows.rearrange("(p j) c -> p j c", j=4))
+
+        def load_w1_first(a):
+            rows = w1[HALF * a : HALF * (a + 1), 0:P]
+            nc.sync.dma_start(out=w1_first[a][:], in_=rows.rearrange("(p j) c -> p j c", j=4))
 
         def load_tab(a):
             nc.sync.dma_start(out=tab[a][:], in_=tab_words[a].rearrange("p t i -> p (t i)").bitcast(I32))
@@ -112,8 +116,9 @@ def tile_list_tsunami_edge_fluxes_kernel(
         nc.gpsimd.dma_start(out=bias_hi[:], in_=b1[HALF:H].rearrange("(p t) -> p t", t=4))
 
         load_tab(0)
-        load_w1_nat(0)
+        load_w1_first(0)
         load_tab(1)
+        load_w1_first(1)
         nc.sync.dma_start(idx3[:], offs3)
         nc.sync.dma_start(idx4[:], offs4)
 
@@ -128,6 +133,9 @@ def tile_list_tsunami_edge_fluxes_kernel(
                     )
             return grouped
 
+        def by_pass(codes, scales):
+            return [(codes[:, P * a : P * (a + 1)], scales[:, P * a : P * (a + 1)]) for a in range(2)]
+
         def quantise_w1(first, grouped, codes_at, scales_at):
             count = grouped.shape[1]
             codes = placed("w1_codes%d" % first, [P, count, 2 * P], U32, codes_at)
@@ -137,16 +145,31 @@ def tile_list_tsunami_edge_fluxes_kernel(
                 scales=scales[:].rearrange("p i c -> p (i c)"),
                 in_=grouped[:].rearrange("p i a c j -> p (i a c j)"),
             )
-            return [(codes[:, i], scales[:, i]) for i in range(count)]
+            return [by_pass(codes[:, i], scales[:, i]) for i in range(count)]
+
+        def quantise_first(a):
+            grouped = placed("first_grouped%d" % a, [P, P, 4], BF16, 65.125 + a)
+            nc.scalar.activation(
+                out=grouped[:].rearrange("p (c i) j -> p c j i", i=4),
+                in_=w1_first[a][:].rearrange("p j (c i) -> p c j i", i=4),
+                func=IDENT,
+            )
+            codes = placed("first_codes%d" % a, [P, P], U32, 75.625 - 0.5 * a)
+            scales = placed("first_scales%d" % a, [P, P], U8, 123 + 0.125 * a)
+            nc.vector.quantize_mx(
+                out=codes[:].bitcast(FP8X4), scales=scales[:], in_=grouped[:].rearrange("p c j -> p (c j)")
+            )
+            return codes[:], scales[:]
 
         def h_pass(acc, quantised, a, s0, width):
-            codes, scales = quantised
+            codes, scales = quantised[a]
             cols = slice(s0, s0 + width)
+            words = v_words0[:, cols] if a == 0 else v_words1[s0 // HALF][:, s0 % HALF : s0 % HALF + width]
             nc.tensor.matmul_mx(
                 out=acc[:],
-                lhsT=codes[:, P * a : P * (a + 1)].bitcast(FP8X4),
-                lhsT_scale=scales[:, P * a : P * (a + 1)],
-                rhs=v_words[a][:, cols].bitcast(FP8X4),
+                lhsT=codes.bitcast(FP8X4),
+                lhsT_scale=scales,
+                rhs=words.bitcast(FP8X4),
                 rhs_scale=v_sc[4 * a : P, cols],
                 start=(a == 0),
                 stop=(a == 1),
@@ -172,12 +195,12 @@ def tile_list_tsunami_edge_fluxes_kernel(
         def gather_minus(dst, page, which, m0, width, other):
             nc.vector.tensor_tensor(out=dst, in0=page[:].indirect(which[:, list_cols(m0, width)]), in1=other, op=SUB)
 
-        nc.vector.tensor_copy(out=v_words[0][:], in_=tab[0][:].bitcast(U32).indirect(idx[:]))
+        nc.vector.tensor_copy(out=v_words0[:], in_=tab[0][:].bitcast(U32).indirect(idx[:]))
         for s0 in range(0, S, HALF):
             nc.sync.dma_start(out=wgs_lo[:, s0 : s0 + HALF], in_=wgs[:, s0 : s0 + HALF])
         load_w1_nat(1)
         nc.vector.memset(pages[1][:], 0.0)
-        w1_q = quantise_w1(0, cast_w1(0, 1, 65.125), 75.125, 123)
+        w1_q = [[quantise_first(a) for a in range(2)]]
         acc_first = []
         for s0, width in FIRST_PIECES:
             acc = psum.tile([P, width], F32, name="acc_first", tag="bank")
@@ -187,7 +210,7 @@ def tile_list_tsunami_edge_fluxes_kernel(
         for (s0, width), acc in zip(FIRST_PIECES, acc_first):
             if s0 % HALF == 0:
                 nc.vector.tensor_copy(
-                    out=v_words[1][:, s0 : s0 + HALF],
+                    out=v_words1[s0 // HALF][:],
                     in_=tab[1][:].bitcast(U32).indirect(idx[:, list_cols(s0, HALF)]),
                 )
             h_pass(acc, w1_q[0], 1, s0, width)
@@ -262,7 +285,7 @@ def tile_list_tsunami_edge_fluxes_kernel(
             scales=scales_hi[:].rearrange("p t c -> p (t c)"),
             in_=grouped_hi[:].rearrange("p t a c j -> p (t a c j)"),
         )
-        h_hi = [make_h(4 + t, (codes_hi[:, t], scales_hi[:, t]), bias_hi[:, t : t + 1]) for t in range(4)]
+        h_hi = [make_h(4 + t, by_pass(codes_hi[:, t], scales_hi[:, t]), bias_hi[:, t : t + 1]) for t in range(4)]
         gather_lo(2)
         pages_hi = pages[2:] + pages[:2]
         for t in range(4):
@@ -306,10 +329,10 @@ def tile_list_tsunami_edge_fluxes_kernel(
             direct_pass(acc, 0, z_codes[0][:, m0 : m0 + width], z_scales[0][:, m0 : m0 + width])
             direct_acc[m0] = acc
 
-        def gather_left(m0, width):
-            y = [placed("y_hi%d_%d" % (m0, t), [P, width], F32, 16 + t) for t in range(4)]
-            for t in range(4):
-                gather_minus(y[t][:], pages_hi[t], idx3, m0, width, bstep_hi[:, t, m0 : m0 + width])
+        def gather_left(m0, width, planes=range(4), at=16):
+            y = [placed("y_hi%d_%d" % (m0, t), [P, width], F32, at + t) for t in planes]
+            for t, part in zip(planes, y):
+                gather_minus(part[:], pages_hi[t], idx3, m0, width, bstep_hi[:, t, m0 : m0 + width])
             return y
 
         def gather_right(m0, width, y, z_at):
@@ -318,8 +341,8 @@ def tile_list_tsunami_edge_fluxes_kernel(
                 gather_minus(z_hi[:, t, :], pages_hi[t], idx4, m0, width, y[t])
             return z_hi
 
-        def group_hi(c, width, z_hi):
-            grouped = placed("zg_hi%d" % c, [P, width, 4], BF16, 209 + 2 * (c % 2))
+        def group_hi(c, width, z_hi, at=None):
+            grouped = placed("zg_hi%d" % c, [P, width, 4], BF16, 209 + 2 * (c % 2) if at is None else at)
             interleave_z(z_hi[:], grouped)
             return grouped
 
@@ -329,23 +352,28 @@ def tile_list_tsunami_edge_fluxes_kernel(
             quantise_z(grouped, codes[:], scales[:])
             return codes, scales
 
-        def multiply_turned(m0, width, quantised):
+        def turned_pass(acc, a, codes, scales):
+            nc.tensor.matmul_mx(
+                out=acc[:],
+                lhsT=codes.bitcast(FP8X4),
+                lhsT_scale=scales,
+                rhs=w2_w[:, a, :].bitcast(FP4X4),
+                rhs_scale=w2_sc[:, a, :],
+                start=(a == 0),
+                stop=(a == 1),
+            )
+
+        def open_turned(m0):
+            acc = psum.tile([P, N], F32, name="acc_turned", tag="bank")
+            turned_pass(acc, 0, z_codes[0][:, m0 : m0 + P], z_scales[0][:, m0 : m0 + P])
+            return acc
+
+        def multiply_turned(m0, width, quantised, opened=None):
             banks = []
             for j in range(width // P):
-                acc = psum.tile([P, N], F32, name="acc_turned", tag="bank")
-                lo = slice(m0 + P * j, m0 + P * (j + 1))
+                acc = open_turned(m0 + P * j) if opened is None else opened
                 hi = slice(P * j, P * (j + 1))
-                sides = ((z_codes[0][:, lo], z_scales[0][:, lo]), (quantised[0][:, hi], quantised[1][:, hi]))
-                for a, (codes, scales) in enumerate(sides):
-                    nc.tensor.matmul_mx(
-                        out=acc[:],
-                        lhsT=codes.bitcast(FP8X4),
-                        lhsT_scale=scales,
-                        rhs=w2_w[:, a, :].bitcast(FP4X4),
-                        rhs_scale=w2_sc[:, a, :],
-                        start=(a == 0),
-                        stop=(a == 1),
-                    )
+                turned_pass(acc, 1, quantised[0][:, hi], quantised[1][:, hi])
                 banks.append(acc)
             return banks
 
@@ -367,21 +395,22 @@ def tile_list_tsunami_edge_fluxes_kernel(
                 nc.scalar.copy(out=res[:, :, P * j : P * (j + 1)], in_=back[:])
             nc.sync.dma_start(out=out_v[:, :, m0 : m0 + width], in_=res[:])
 
-        def store_direct(m0, width):
-            res = placed("res%d" % m0, [P, 4, width], F32, 42 + (m0 - DIRECT[0][0]) / 64)
+        def store_direct(m0, width, at):
+            res = placed("res%d" % m0, [P, 4, width], F32, at)
             cols = slice(m0 - DIRECT[0][0], m0 - DIRECT[0][0] + width)
             factors = le_tail[:, cols].unsqueeze(1).to_broadcast([P, 4, width])
             nc.vector.tensor_tensor(out=res[:], in0=direct_acc[m0][:], in1=factors, op=MULT)
             nc.sync.dma_start(out=out_v[:, :, m0 : m0 + width], in_=res[:])
 
+        opened = open_turned(HALF)
         grouped = {}
         turned = {}
         for c in range(len(TURNED) + 1):
-            y = gather_left(QUARTER * c, QUARTER)
+            y = gather_left(QUARTER * c, QUARTER, range(4) if c < len(TURNED) else range(3))
             if c >= 1:
                 m0, width = TURNED[c - 1]
                 quantised = quantise_hi(m0, QUARTER, grouped[c - 1])
-                banks = multiply_turned(m0, width, quantised)
+                banks = multiply_turned(m0, width, quantised, opened if width < QUARTER else None)
                 if width < QUARTER:
                     direct_pass(direct_acc[m0 + width], 1, quantised[0][:, width:], quantised[1][:, width:])
             if c >= 2:
@@ -390,15 +419,21 @@ def tile_list_tsunami_edge_fluxes_kernel(
                 turned[c - 1] = scale_and_turn(m0, banks)
             if c < len(TURNED):
                 grouped[c] = group_hi(c, QUARTER, gather_right(QUARTER * c, QUARTER, [part[:] for part in y], 179))
+        y = y + gather_left(HALF + QUARTER, QUARTER, range(3, 4), 178)
         last = [
-            gather_right(m0, width, [part[:, P * j : P * (j + 1)] for part in y], 179 + 2 * j)
+            gather_right(m0, width, [part[:, P * j : P * (j + 1)] for part in y], 179 + 3 * j)
             for j, (m0, width) in enumerate(DIRECT[1:])
         ]
-        grouped_last = [group_hi(len(TURNED) + j, P, last[j]) for j in range(2)]
-        store_turned(*TURNED[-1], turned[len(TURNED) - 1])
-        store_direct(*DIRECT[0])
-        for j, (m0, width) in enumerate(DIRECT[1:]):
-            quantised = quantise_hi(m0, width, grouped_last[j])
+
+        def finish_direct(j, grouped):
+            m0, width = DIRECT[j]
+            quantised = quantise_hi(m0, width, grouped)
             direct_pass(direct_acc[m0], 1, quantised[0][:], quantised[1][:])
-        for m0, width in DIRECT[1:]:
-            store_direct(m0, width)
+
+        finish_direct(1, group_hi(3, P, last[0], 147.125))
+        store_turned(*TURNED[-1], turned[len(TURNED) - 1])
+        grouped_last = group_hi(4, P, last[1], 213)
+        store_direct(*DIRECT[0], 179)
+        finish_direct(2, grouped_last)
+        store_direct(*DIRECT[1], 182)
+        store_direct(*DIRECT[2], 46)

@@ -311,23 +311,28 @@ def tile_list_tsunami_edge_fluxes_kernel(
 
         out_v = out.rearrange("(b p) m -> p b m", p=P)
 
-        def direct_pass(acc, a, codes, scales):
-            for b in range(4):
+        def direct_pass(acc, a, codes, scales, b0=0):
+            count = acc.shape[1]
+            for b in range(b0, b0 + count):
                 nc.tensor.matmul_mx(
-                    out=acc[:, b, :],
+                    out=acc[:, b - b0, :],
                     lhsT=w2_w[:, a, 2 * P * b : 2 * P * (b + 1)].bitcast(FP4X4),
                     lhsT_scale=w2_sc[:, a, P * b : P * (b + 1)],
                     rhs=codes.bitcast(FP8X4),
                     rhs_scale=scales,
-                    start=(a == 0 and b == 0),
-                    stop=(a == 1 and b == 3),
+                    start=(a == 0 and b == b0),
+                    stop=(a == 1 and b == b0 + count - 1),
                 )
 
         direct_acc = {}
-        for m0, width in DIRECT:
-            acc = psum.tile([P, 4, width], F32, name="acc_direct", tag="bank")
-            direct_pass(acc, 0, z_codes[0][:, m0 : m0 + width], z_scales[0][:, m0 : m0 + width])
-            direct_acc[m0] = acc
+
+        def open_direct(m0, b0, count):
+            acc = psum.tile([P, count, P], F32, name="acc_direct", tag="bank")
+            direct_pass(acc, 0, z_codes[0][:, m0 : m0 + P], z_scales[0][:, m0 : m0 + P], b0)
+            direct_acc[m0, b0] = acc
+
+        for (m0, width), count in zip(DIRECT, (4, 4, 2)):
+            open_direct(m0, 0, count)
 
         def gather_left(m0, width, planes=range(4), at=16):
             y = [placed("y_hi%d_%d" % (m0, t), [P, width], F32, at + t) for t in planes]
@@ -395,12 +400,12 @@ def tile_list_tsunami_edge_fluxes_kernel(
                 nc.scalar.copy(out=res[:, :, P * j : P * (j + 1)], in_=back[:])
             nc.sync.dma_start(out=out_v[:, :, m0 : m0 + width], in_=res[:])
 
-        def store_direct(m0, width, at):
-            res = placed("res%d" % m0, [P, 4, width], F32, at)
+        def store_direct(m0, width, at, b0=0, count=4):
+            res = placed("res%d_%d" % (m0, b0), [P, count, width], F32, at)
             cols = slice(m0 - DIRECT[0][0], m0 - DIRECT[0][0] + width)
-            factors = le_tail[:, cols].unsqueeze(1).to_broadcast([P, 4, width])
-            nc.vector.tensor_tensor(out=res[:], in0=direct_acc[m0][:], in1=factors, op=MULT)
-            nc.sync.dma_start(out=out_v[:, :, m0 : m0 + width], in_=res[:])
+            factors = le_tail[:, cols].unsqueeze(1).to_broadcast([P, count, width])
+            nc.vector.tensor_tensor(out=res[:], in0=direct_acc[m0, b0][:], in1=factors, op=MULT)
+            nc.sync.dma_start(out=out_v[:, b0 : b0 + count, m0 : m0 + width], in_=res[:])
 
         opened = open_turned(HALF)
         grouped = {}
@@ -412,13 +417,14 @@ def tile_list_tsunami_edge_fluxes_kernel(
                 quantised = quantise_hi(m0, QUARTER, grouped[c - 1])
                 banks = multiply_turned(m0, width, quantised, opened if width < QUARTER else None)
                 if width < QUARTER:
-                    direct_pass(direct_acc[m0 + width], 1, quantised[0][:, width:], quantised[1][:, width:])
+                    direct_pass(direct_acc[m0 + width, 0], 1, quantised[0][:, width:], quantised[1][:, width:])
             if c >= 2:
                 store_turned(*TURNED[c - 2], turned[c - 2])
             if c >= 1:
                 turned[c - 1] = scale_and_turn(m0, banks)
             if c < len(TURNED):
                 grouped[c] = group_hi(c, QUARTER, gather_right(QUARTER * c, QUARTER, [part[:] for part in y], 179))
+        open_direct(DIRECT[2][0], 2, 2)
         y = y + gather_left(HALF + QUARTER, QUARTER, range(3, 4), 178)
         last = [
             gather_right(m0, width, [part[:, P * j : P * (j + 1)] for part in y], 179 + 3 * j)
@@ -428,7 +434,9 @@ def tile_list_tsunami_edge_fluxes_kernel(
         def finish_direct(j, grouped):
             m0, width = DIRECT[j]
             quantised = quantise_hi(m0, width, grouped)
-            direct_pass(direct_acc[m0], 1, quantised[0][:], quantised[1][:])
+            for first, b0 in direct_acc:
+                if first == m0:
+                    direct_pass(direct_acc[m0, b0], 1, quantised[0][:], quantised[1][:], b0)
 
         finish_direct(1, group_hi(3, P, last[0], 147.125))
         store_turned(*TURNED[-1], turned[len(TURNED) - 1])
@@ -436,4 +444,5 @@ def tile_list_tsunami_edge_fluxes_kernel(
         store_direct(*DIRECT[0], 179)
         finish_direct(2, grouped_last)
         store_direct(*DIRECT[1], 182)
-        store_direct(*DIRECT[2], 46)
+        for b0 in (0, 2):
+            store_direct(*DIRECT[2], 46 + b0 / 2, b0, 2)

@@ -400,12 +400,14 @@ def tile_list_tsunami_edge_fluxes_kernel(
                 nc.scalar.copy(out=res[:, :, P * j : P * (j + 1)], in_=back[:])
             nc.sync.dma_start(out=out_v[:, :, m0 : m0 + width], in_=res[:])
 
-        def store_direct(m0, width, at, b0=0, count=4):
+        def store_direct(m0, width, at, acc, b0=0):
+            count = acc.shape[1]
             res = placed("res%d_%d" % (m0, b0), [P, count, width], F32, at)
             cols = slice(m0 - DIRECT[0][0], m0 - DIRECT[0][0] + width)
             factors = le_tail[:, cols].unsqueeze(1).to_broadcast([P, count, width])
-            nc.vector.tensor_tensor(out=res[:], in0=direct_acc[m0, b0][:], in1=factors, op=MULT)
-            nc.sync.dma_start(out=out_v[:, b0 : b0 + count, m0 : m0 + width], in_=res[:])
+            nc.vector.tensor_tensor(out=res[:], in0=acc, in1=factors, op=MULT)
+            queue = nc.scalar if b0 == 2 else nc.sync
+            queue.dma_start(out=out_v[:, b0 : b0 + count, m0 : m0 + width], in_=res[:])
 
         opened = open_turned(HALF)
         grouped = {}
@@ -441,8 +443,10 @@ def tile_list_tsunami_edge_fluxes_kernel(
         finish_direct(1, group_hi(3, P, last[0], 147.125))
         store_turned(*TURNED[-1], turned[len(TURNED) - 1])
         grouped_last = group_hi(4, P, last[1], 213)
-        store_direct(*DIRECT[0], 179)
+        store_direct(*DIRECT[0], 179, direct_acc[DIRECT[0][0], 0][:])
         finish_direct(2, grouped_last)
-        store_direct(*DIRECT[1], 182)
         for b0 in (0, 2):
-            store_direct(*DIRECT[2], 46 + b0 / 2, b0, 2)
+            store_direct(*DIRECT[1], 182 + b0 / 2, direct_acc[DIRECT[1][0], 0][:, b0 : b0 + 2, :], b0)
+        store_direct(*DIRECT[2], 46, direct_acc[DIRECT[2][0], 0][:], 0)
+        for b in (2, 3):
+            store_direct(*DIRECT[2], 46 + b / 2, direct_acc[DIRECT[2][0], 2][:, b - 2 : b - 1, :], b)

@@ -22,12 +22,12 @@ P = 128
 KIB = 1024
 HALF = 512
 QUARTER = 256
+PSUM_BANKS = 8
 STAGED = 96
 LAP = 0.0625
 FIRST_PIECES = ((0, QUARTER), (QUARTER, QUARTER), (HALF, HALF))
-TURNED = ((0, QUARTER), (QUARTER, QUARTER), (HALF, P))
-DIRECT = ((HALF + P, P), (HALF + 2 * P, P), (HALF + 3 * P, P))
-TURNED_EDGES = HALF + P
+TURNED_EDGES = 5 * P
+DIRECT_FIRST, DIRECT_SECOND, DIRECT_LAST = range(TURNED_EDGES, E, P)
 
 
 def tile_list_tsunami_edge_fluxes_kernel(
@@ -38,7 +38,7 @@ def tile_list_tsunami_edge_fluxes_kernel(
         lists = ctx.enter_context(tc.tile_pool(name="lists", bufs=1))
         keep = ctx.enter_context(tc.tile_pool(name="keep", bufs=1))
         shared = ctx.enter_context(tc.tile_pool(name="shared", bufs=1))
-        psum = ctx.enter_context(tc.psum_pool(name="psum", bufs=8))
+        psum = ctx.enter_context(tc.psum_pool(name="psum", bufs=PSUM_BANKS))
 
         def placed(name, shape, dtype, kib):
             return shared.tile(shape, dtype, name=name, align_bytes=64, offset=int(kib * KIB))
@@ -64,7 +64,7 @@ def tile_list_tsunami_edge_fluxes_kernel(
         pages = [placed("page%d" % i, [P, T2], F32, kib) for i, kib in enumerate((223, 0, 114 + LAP, 124 - LAP))]
         le_tail = placed("le_tail", [P, E - TURNED_EDGES], F32, 139.5 + LAP)
         w2_sc = placed("w2_sc", [P, 2, N], U8, 146 + LAP)
-        le_col = placed("le_col", [P, TURNED_EDGES // P], F32, 147 + 3 * LAP)
+        le_col = placed("le_col", [P, DIRECT_SECOND // P], F32, 147 + 3 * LAP)
         v_sc = keep.tile([P, S], U8, name="v_sc", align_bytes=64)
         bias_lo = keep.tile([P, 4], F32, name="bias_lo")
         bias_hi = placed("bias_hi", [P, 4], F32, 56.125)
@@ -87,8 +87,8 @@ def tile_list_tsunami_edge_fluxes_kernel(
             rows = bstep[QUARTER * c : QUARTER * (c + 1), :]
             nc.sync.dma_start(out=bstep_lo[c][:], in_=rows.rearrange("(i p) m -> p i m", p=P))
 
-        def list_cols(m0, width):
-            return slice(m0 // 16, (m0 + width) // 16)
+        def list_cols(first, count):
+            return slice(first // 16, (first + count) // 16)
 
         nc.vector.memset(tab_sc[0:STAGED, :].bitcast(I32), 0)
         nc.sync.dma_start(
@@ -227,10 +227,10 @@ def tile_list_tsunami_edge_fluxes_kernel(
         for q in range(4):
             nc.sync.dma_start(out=wgs_hi[32 * q : 32 * (q + 1)], in_=wgs.rearrange("(p t) j -> p t j", t=4))
 
-        grouped_second = cast_w1(1, 1, 122)
+        grouped_second = cast_w1(1, 1, grouped_at=122)
         add_bias(h_first[1][:], acc_first[-1], bias_lo[:, 0:1])
         scatter(pages[0], h_first[0][:], wgs_lo, 0, HALF)
-        w1_q = w1_q + quantise_w1(1, grouped_second, 141, 147)
+        w1_q = w1_q + quantise_w1(1, grouped_second, codes_at=141, scales_at=147)
         scatter(pages[0], h_first[1][:], wgs_lo, HALF, HALF)
         nc.sync.dma_start(out=bstep_hi[:], in_=bstep[HALF:H, :].rearrange("(p t) m -> p t m", t=4))
         nc.sync.dma_start(out=w2_w[:].bitcast(I32), in_=w2_words.rearrange("a p c -> p a c").bitcast(I32))
@@ -243,14 +243,14 @@ def tile_list_tsunami_edge_fluxes_kernel(
         nc.gpsimd.memset(w2_sc[:].rearrange("p a c -> p (a c)").bitcast(I32), 0)
         nc.sync.dma_start(out=le_tail[:], in_=le[TURNED_EDGES:E].partition_broadcast(P))
         with nc.allow_non_contiguous_dma(reason="one length factor a partition"):
-            nc.sync.dma_start(out=le_col[:], in_=le[0:TURNED_EDGES].rearrange("(c p) -> p c", p=P))
+            nc.sync.dma_start(out=le_col[:], in_=le[0:DIRECT_SECOND].rearrange("(c p) -> p c", p=P))
         for q in range(4):
             nc.sync.dma_start(
                 out=w2_sc[32 * q : 32 * q + 4].bitcast(I32),
                 in_=w2_scales[:, 4 * q : 4 * q + 4, :].rearrange("a r c -> r a c").bitcast(I32),
             )
 
-        w1_q = w1_q + quantise_w1(2, cast_w1(2, 2, 142 - LAP), 147.5, 149.5)
+        w1_q = w1_q + quantise_w1(2, cast_w1(2, 2, grouped_at=142 - LAP), codes_at=147.5, scales_at=149.5)
         for i in range(2, 4):
             h[i] = make_h(i, w1_q[i], bias_lo[:, i : i + 1])
 
@@ -298,16 +298,16 @@ def tile_list_tsunami_edge_fluxes_kernel(
                 func=IDENT,
             )
 
-        z_codes = [placed("z_codes%d" % a, [P, E], U32, 195) for a in range(1)]
-        z_scales = [placed("z_scales%d" % a, [P, E], U8, 199) for a in range(1)]
+        codes_lo = placed("z_codes0", [P, E], U32, 195)
+        scales_lo = placed("z_scales0", [P, E], U8, 199)
 
         def quantise_z(grouped, codes, scales):
             nc.vector.quantize_mx(out=codes.bitcast(FP8X4), scales=scales, in_=grouped[:].rearrange("p m t -> p (m t)"))
 
         for c, m0 in enumerate(range(0, E, HALF)):
-            grouped = placed("zg_lo%d" % c, [P, HALF, 4], BF16, 32 + 4 * c)
-            interleave_z(z_lo[:, :, m0 : m0 + HALF], grouped)
-            quantise_z(grouped, z_codes[0][:, m0 : m0 + HALF], z_scales[0][:, m0 : m0 + HALF])
+            grouped_lo = placed("zg_lo%d" % c, [P, HALF, 4], BF16, 32 + 4 * c)
+            interleave_z(z_lo[:, :, m0 : m0 + HALF], grouped_lo)
+            quantise_z(grouped_lo, codes_lo[:, m0 : m0 + HALF], scales_lo[:, m0 : m0 + HALF])
 
         out_v = out.rearrange("(b p) m -> p b m", p=P)
 
@@ -324,20 +324,19 @@ def tile_list_tsunami_edge_fluxes_kernel(
                     stop=(a == 1 and b == b0 + count - 1),
                 )
 
-        direct_acc = {}
-
         def open_direct(m0, b0, count):
             acc = psum.tile([P, count, P], F32, name="acc_direct", tag="bank")
-            direct_pass(acc, 0, z_codes[0][:, m0 : m0 + P], z_scales[0][:, m0 : m0 + P], b0)
-            direct_acc[m0, b0] = acc
+            direct_pass(acc, 0, codes_lo[:, m0 : m0 + P], scales_lo[:, m0 : m0 + P], b0)
+            return acc
 
-        for (m0, width), count in zip(DIRECT, (4, 4, 2)):
-            open_direct(m0, 0, count)
+        acc_direct_first = open_direct(DIRECT_FIRST, 2, 2)
+        acc_direct_second = open_direct(DIRECT_SECOND, 0, 4)
+        acc_last_low = open_direct(DIRECT_LAST, 0, 2)
 
-        def gather_left(m0, width, planes=range(4), at=16):
-            y = [placed("y_hi%d_%d" % (m0, t), [P, width], F32, at + t) for t in planes]
-            for t, part in zip(planes, y):
-                gather_minus(part[:], pages_hi[t], idx3, m0, width, bstep_hi[:, t, m0 : m0 + width])
+        def gather_left(m0, tiles, at=16):
+            y = [placed("y_hi%d_%d" % (m0, t), [P, QUARTER], F32, at + t) for t in tiles]
+            for t, part in zip(tiles, y):
+                gather_minus(part[:], pages_hi[t], idx3, m0, QUARTER, bstep_hi[:, t, m0 : m0 + QUARTER])
             return y
 
         def gather_right(m0, width, y, z_at):
@@ -346,39 +345,44 @@ def tile_list_tsunami_edge_fluxes_kernel(
                 gather_minus(z_hi[:, t, :], pages_hi[t], idx4, m0, width, y[t])
             return z_hi
 
-        def group_hi(c, width, z_hi, at=None):
-            grouped = placed("zg_hi%d" % c, [P, width, 4], BF16, 209 + 2 * (c % 2) if at is None else at)
+        def group_hi(c, z_hi, at):
+            grouped = placed("zg_hi%d" % c, [P, z_hi.shape[2], 4], BF16, at)
             interleave_z(z_hi[:], grouped)
             return grouped
 
-        def quantise_hi(m0, width, grouped):
+        def right_chunk(c, y):
+            return group_hi(c, gather_right(QUARTER * c, QUARTER, [part[:] for part in y], 179), 209 + 2 * (c % 2))
+
+        def quantise_hi(m0, grouped):
+            width = grouped.shape[1]
             codes = placed("zc_hi%d" % m0, [P, width], U32, 200 + m0 / 256)
             scales = placed("zs_hi%d" % m0, [P, width], U8, 221 + m0 / 1024)
             quantise_z(grouped, codes[:], scales[:])
             return codes, scales
 
         def turned_pass(acc, a, codes, scales):
+            columns = acc.shape[1]
             nc.tensor.matmul_mx(
                 out=acc[:],
                 lhsT=codes.bitcast(FP8X4),
                 lhsT_scale=scales,
-                rhs=w2_w[:, a, :].bitcast(FP4X4),
-                rhs_scale=w2_sc[:, a, :],
+                rhs=w2_w[:, a, 0 : 2 * columns].bitcast(FP4X4),
+                rhs_scale=w2_sc[:, a, 0:columns],
                 start=(a == 0),
                 stop=(a == 1),
             )
 
-        def open_turned(m0):
-            acc = psum.tile([P, N], F32, name="acc_turned", tag="bank")
-            turned_pass(acc, 0, z_codes[0][:, m0 : m0 + P], z_scales[0][:, m0 : m0 + P])
+        def open_turned(m0, columns=N):
+            acc = psum.tile([P, columns], F32, name="acc_turned", tag="bank")
+            turned_pass(acc, 0, codes_lo[:, m0 : m0 + P], scales_lo[:, m0 : m0 + P])
             return acc
 
-        def multiply_turned(m0, width, quantised, opened=None):
+        def multiply_chunk(m0, grouped):
+            codes, scales = quantise_hi(m0, grouped)
             banks = []
-            for j in range(width // P):
-                acc = open_turned(m0 + P * j) if opened is None else opened
-                hi = slice(P * j, P * (j + 1))
-                turned_pass(acc, 1, quantised[0][:, hi], quantised[1][:, hi])
+            for j in range(QUARTER // P):
+                acc = open_turned(m0 + P * j)
+                turned_pass(acc, 1, codes[:, P * j : P * (j + 1)], scales[:, P * j : P * (j + 1)])
                 banks.append(acc)
             return banks
 
@@ -386,67 +390,69 @@ def tile_list_tsunami_edge_fluxes_kernel(
             turned = []
             for j, acc in enumerate(banks):
                 block = m0 // P + j
-                scaled = placed("scaled%d" % block, [P, N], F32, 213 + 2 * (block % 4))
+                ranges = acc.shape[1] // P
+                scaled = placed("scaled%d" % block, [P, ranges * P], F32, 213 + 2 * (block % 4))
                 nc.scalar.activation(out=scaled[:], in_=acc[:], func=IDENT, scale=le_col[:, block : block + 1])
-                back = psum.tile([P, 4, P], F32, name="acc_back", tag="bank")
-                for b in range(4):
+                back = psum.tile([P, ranges, P], F32, name="acc_back", tag="bank")
+                for b in range(ranges):
                     nc.tensor.transpose(back[:, b, :], scaled[:, P * b : P * (b + 1)], ident[:])
                 turned.append(back)
             return turned
 
-        def store_turned(m0, width, turned):
-            res = placed("res%d" % m0, [P, 4, width], F32, (24, 28, 40)[m0 // QUARTER])
+        def store_turned(m0, turned, at):
+            width = P * len(turned)
+            ranges = turned[0].shape[1]
+            res = placed("res%d" % m0, [P, ranges, width], F32, at)
             for j, back in enumerate(turned):
                 nc.scalar.copy(out=res[:, :, P * j : P * (j + 1)], in_=back[:])
-            nc.sync.dma_start(out=out_v[:, :, m0 : m0 + width], in_=res[:])
+            nc.sync.dma_start(out=out_v[:, 0:ranges, m0 : m0 + width], in_=res[:])
 
-        def store_direct(m0, width, at, acc, b0=0):
+        def store_direct(m0, b0, acc, at, queue):
             count = acc.shape[1]
-            res = placed("res%d_%d" % (m0, b0), [P, count, width], F32, at)
-            cols = slice(m0 - DIRECT[0][0], m0 - DIRECT[0][0] + width)
-            factors = le_tail[:, cols].unsqueeze(1).to_broadcast([P, count, width])
+            res = placed("res%d_%d" % (m0, b0), [P, count, P], F32, at)
+            factors = le_tail[:, m0 - TURNED_EDGES : m0 - TURNED_EDGES + P].unsqueeze(1).to_broadcast([P, count, P])
             nc.vector.tensor_tensor(out=res[:], in0=acc, in1=factors, op=MULT)
-            queue = nc.scalar if b0 == 2 else nc.sync
-            queue.dma_start(out=out_v[:, b0 : b0 + count, m0 : m0 + width], in_=res[:])
+            queue.dma_start(out=out_v[:, b0 : b0 + count, m0 : m0 + P], in_=res[:])
 
-        opened = open_turned(HALF)
-        grouped = {}
-        turned = {}
-        for c in range(len(TURNED) + 1):
-            y = gather_left(QUARTER * c, QUARTER, range(4) if c < len(TURNED) else range(3))
-            if c >= 1:
-                m0, width = TURNED[c - 1]
-                quantised = quantise_hi(m0, QUARTER, grouped[c - 1])
-                banks = multiply_turned(m0, width, quantised, opened if width < QUARTER else None)
-                if width < QUARTER:
-                    direct_pass(direct_acc[m0 + width, 0], 1, quantised[0][:, width:], quantised[1][:, width:])
-            if c >= 2:
-                store_turned(*TURNED[c - 2], turned[c - 2])
-            if c >= 1:
-                turned[c - 1] = scale_and_turn(m0, banks)
-            if c < len(TURNED):
-                grouped[c] = group_hi(c, QUARTER, gather_right(QUARTER * c, QUARTER, [part[:] for part in y], 179))
-        open_direct(DIRECT[2][0], 2, 2)
-        y = y + gather_left(HALF + QUARTER, QUARTER, range(3, 4), 178)
-        last = [
-            gather_right(m0, width, [part[:, P * j : P * (j + 1)] for part in y], 179 + 3 * j)
-            for j, (m0, width) in enumerate(DIRECT[1:])
-        ]
+        acc_last_turned = open_turned(HALF)
+        grouped = right_chunk(0, gather_left(0, range(4)))
 
-        def finish_direct(j, grouped):
-            m0, width = DIRECT[j]
-            quantised = quantise_hi(m0, width, grouped)
-            for first, b0 in direct_acc:
-                if first == m0:
-                    direct_pass(direct_acc[m0, b0], 1, quantised[0][:], quantised[1][:], b0)
+        y = gather_left(QUARTER, range(4))
+        turned0 = scale_and_turn(0, multiply_chunk(0, grouped))
+        grouped = right_chunk(1, y)
 
-        finish_direct(1, group_hi(3, P, last[0], 147.125))
-        store_turned(*TURNED[-1], turned[len(TURNED) - 1])
-        grouped_last = group_hi(4, P, last[1], 213)
-        store_direct(*DIRECT[0], 179, direct_acc[DIRECT[0][0], 0][:])
-        finish_direct(2, grouped_last)
-        for b0 in (0, 2):
-            store_direct(*DIRECT[1], 182 + b0 / 2, direct_acc[DIRECT[1][0], 0][:, b0 : b0 + 2, :], b0)
-        store_direct(*DIRECT[2], 46, direct_acc[DIRECT[2][0], 0][:], 0)
-        for b in (2, 3):
-            store_direct(*DIRECT[2], 46 + b / 2, direct_acc[DIRECT[2][0], 2][:, b - 2 : b - 1, :], b)
+        y = gather_left(HALF, range(4))
+        banks = multiply_chunk(QUARTER, grouped)
+        store_turned(0, turned0, at=24)
+        turned1 = scale_and_turn(QUARTER, banks)
+        grouped = right_chunk(2, y)
+
+        y = gather_left(DIRECT_SECOND, range(3))
+        codes, scales = quantise_hi(HALF, grouped)
+        turned_pass(acc_last_turned, 1, codes[:, 0:P], scales[:, 0:P])
+        store_turned(QUARTER, turned1, at=28)
+        acc_half_turned = open_turned(DIRECT_FIRST, QUARTER)
+        turned_pass(acc_half_turned, 1, codes[:, P:], scales[:, P:])
+        direct_pass(acc_direct_first, 1, codes[:, P:], scales[:, P:], 2)
+        turned2 = scale_and_turn(HALF, [acc_last_turned])
+        turned3 = scale_and_turn(DIRECT_FIRST, [acc_half_turned])
+        acc_last_high = open_direct(DIRECT_LAST, 2, 2)
+        y = y + gather_left(DIRECT_SECOND, range(3, 4), at=178)
+
+        z_second = gather_right(DIRECT_SECOND, P, [part[:, 0:P] for part in y], 179)
+        z_last = gather_right(DIRECT_LAST, P, [part[:, P : 2 * P] for part in y], 182)
+
+        codes, scales = quantise_hi(DIRECT_SECOND, group_hi(3, z_second, 147.125))
+        direct_pass(acc_direct_second, 1, codes[:], scales[:])
+        store_turned(HALF, turned2, at=40)
+        grouped = group_hi(4, z_last, 213)
+        store_direct(DIRECT_FIRST, 2, acc_direct_first[:], 179, nc.sync)
+        store_turned(DIRECT_FIRST, turned3, at=42)
+        codes, scales = quantise_hi(DIRECT_LAST, grouped)
+        direct_pass(acc_last_low, 1, codes[:], scales[:], 0)
+        direct_pass(acc_last_high, 1, codes[:], scales[:], 2)
+        store_direct(DIRECT_SECOND, 0, acc_direct_second[:, 0:2, :], 182, nc.sync)
+        store_direct(DIRECT_SECOND, 2, acc_direct_second[:, 2:4, :], 183, nc.scalar)
+        store_direct(DIRECT_LAST, 0, acc_last_low[:], 46, nc.sync)
+        store_direct(DIRECT_LAST, 2, acc_last_high[:, 0:1, :], 47, nc.scalar)
+        store_direct(DIRECT_LAST, 3, acc_last_high[:, 1:2, :], 47.5, nc.sync)

@@ -24,6 +24,7 @@ HALF = 512
 QUARTER = 256
 PSUM_BANKS = 8
 STAGED = 96
+SCALE_ROW = (12, 0)
 LAP = 0.0625
 FIRST_PIECES = ((0, QUARTER), (QUARTER, QUARTER), (HALF, HALF))
 TURNED_EDGES = 5 * P
@@ -102,17 +103,17 @@ def tile_list_tsunami_edge_fluxes_kernel(
         bias_turned = psum.tile([P, P], F32, name="bias_turned", tag="bank")
         nc.tensor.transpose(bias_turned[:], bias_rows[:], ident[:])
         nc.scalar.activation(out=bias_lo[:], in_=bias_turned[:, 0:4], func=IDENT)
-        nc.vector.memset(v_sc[:].bitcast(I32), 0)
-        for c0 in range(0, T2, HALF):
-            nc.gpsimd.memset(pages[0][:, c0 : c0 + HALF], 0.0)
+        nc.vector.memset(v_sc[0:STAGED, :].bitcast(I32), 0)
+        nc.vector.memset(pages[0][:], 0.0)
         nc.vector.tensor_copy(out=picked_sc[:], in_=tab_sc[:].indirect(idx[:]))
-        for a, queue in enumerate((nc.scalar, nc.gpsimd)):
-            for q in range(4):
-                row = STAGED + 16 * a + 4 * q
-                queue.dma_start(
-                    out=v_sc[32 * q + 4 * a : 32 * q + 4 * a + 4, :].bitcast(I32),
-                    in_=picked_sc[row : row + 4, :].bitcast(I32),
-                )
+        nc.vector.tensor_copy(out=v_sc[STAGED:P, :].bitcast(I32), in_=picked_sc[STAGED:P, :].bitcast(I32))
+        for a, q in [(0, 0), (0, 1), (0, 2), (1, 0), (1, 1), (1, 2), (1, 3)]:
+            row = STAGED + 16 * a + 4 * q
+            queue = nc.gpsimd if a == 0 else nc.scalar
+            queue.dma_start(
+                out=v_sc[32 * q + SCALE_ROW[a] : 32 * q + SCALE_ROW[a] + 4, :].bitcast(I32),
+                in_=picked_sc[row : row + 4, :].bitcast(I32),
+            )
         nc.gpsimd.dma_start(out=bias_hi[:], in_=b1[HALF:H].rearrange("(p t) -> p t", t=4))
 
         load_tab(0)
@@ -170,7 +171,7 @@ def tile_list_tsunami_edge_fluxes_kernel(
                 lhsT=codes.bitcast(FP8X4),
                 lhsT_scale=scales,
                 rhs=words.bitcast(FP8X4),
-                rhs_scale=v_sc[4 * a : P, cols],
+                rhs_scale=v_sc[SCALE_ROW[a] : P, cols],
                 start=(a == 0),
                 stop=(a == 1),
             )

@@ -116,8 +116,8 @@ def tile_list_tsunami_edge_fluxes_kernel(
             )
         nc.gpsimd.dma_start(out=bias_hi[:], in_=b1[HALF:H].rearrange("(p t) -> p t", t=4))
 
-        load_tab(0)
         load_w1_first(0)
+        load_tab(0)
         load_tab(1)
         load_w1_first(1)
         nc.sync.dma_start(idx3[:], offs3)
@@ -156,7 +156,7 @@ def tile_list_tsunami_edge_fluxes_kernel(
                 func=IDENT,
             )
             codes = placed("first_codes%d" % a, [P, P], U32, 75.625 - 0.5 * a)
-            scales = placed("first_scales%d" % a, [P, P], U8, 123 + 0.125 * a)
+            scales = placed("first_scales%d" % a, [P, P], U8, (123, LAP)[a])
             nc.vector.quantize_mx(
                 out=codes[:].bitcast(FP8X4), scales=scales[:], in_=grouped[:].rearrange("p c j -> p (c j)")
             )
@@ -200,7 +200,6 @@ def tile_list_tsunami_edge_fluxes_kernel(
         for s0 in range(0, S, HALF):
             nc.sync.dma_start(out=wgs_lo[:, s0 : s0 + HALF], in_=wgs[:, s0 : s0 + HALF])
         load_w1_nat(1)
-        nc.vector.memset(pages[1][:], 0.0)
         w1_q = [[quantise_first(a) for a in range(2)]]
         acc_first = []
         for s0, width in FIRST_PIECES:
@@ -217,6 +216,12 @@ def tile_list_tsunami_edge_fluxes_kernel(
             h_pass(acc, w1_q[0], 1, s0, width)
             if s0 < HALF:
                 add_bias(h_first[0][:, s0 : s0 + width], acc, bias_lo[:, 0:1])
+
+        def clear_page(i):
+            for c0 in range(0, T2, HALF):
+                nc.gpsimd.memset(pages[i][:, c0 : c0 + HALF], 0.0)
+
+        clear_page(1)
 
         load_w1_nat(2)
         load_w1_nat(3)
@@ -239,8 +244,7 @@ def tile_list_tsunami_edge_fluxes_kernel(
         scatter(pages[1], h[1][:], wgs_lo, 0, S)
 
         for i in range(2, 4):
-            for c0 in range(0, T2, HALF):
-                nc.gpsimd.memset(pages[i][:, c0 : c0 + HALF], 0.0)
+            clear_page(i)
         nc.gpsimd.memset(w2_sc[:].rearrange("p a c -> p (a c)").bitcast(I32), 0)
         nc.sync.dma_start(out=le_tail[:], in_=le[TURNED_EDGES:E].partition_broadcast(P))
         with nc.allow_non_contiguous_dma(reason="one length factor a partition"):

@@ -51,12 +51,11 @@ def tile_list_tsunami_edge_fluxes_kernel(
 
         tab = [placed("tab%d" % a, [P, T], I32, 16 * a + LAP) for a in range(2)]
         bstep_lo = [placed("bstep_lo%d" % c, [P, 2, E], F32, kib) for c, kib in enumerate((24, 67 + 3 * LAP))]
-        w1_first = [placed("w1_first%d" % a, [P, 4, P], F32, kib) for a, kib in enumerate((57.125, 50))]
+        w1_first = [placed("w1_first%d" % a, [P, 4, P], F32, kib) for a, kib in enumerate((57.125, 59.125))]
         w1_nat = {i: placed("w1_nat%d" % i, [P, 2, 4, P], F32, kib) for i, kib in ((1, 12), (2, 16), (3, 20))}
         w1_hi = placed("w1_hi", [P, 2, 4, HALF], F32, 32)
         wgs_lo = placed("wgs_lo", [P, S], F32, 8)
-        v_words0 = placed("v_words0", [P, S], U32, 132)
-        v_words1 = [placed("v_words1_%d" % c, [P, HALF], U32, 48 + 2 * c) for c in range(2)]
+        v_words = [placed("v_words%d" % a, [P, S], U32, kib) for a, kib in enumerate((132, 48))]
         tab_sc = placed("tab_sc", [P, T], U8, 52.125)
         picked_sc = placed("picked_sc", [P, S], U8, 56.125)
         wgs_hi = placed("wgs_hi", [P, 4, S], F32, 76 + LAP)
@@ -66,7 +65,7 @@ def tile_list_tsunami_edge_fluxes_kernel(
         le_tail = placed("le_tail", [P, E - TURNED_EDGES], F32, 139.5 + LAP)
         w2_sc = placed("w2_sc", [P, 2, N], U8, 146 + LAP)
         le_col = placed("le_col", [P, DIRECT_SECOND // P], F32, 147 + 3 * LAP)
-        v_sc = keep.tile([P, S], U8, name="v_sc", align_bytes=64)
+        v_sc = [keep.tile([P, S], U8, name="v_sc%d" % a, align_bytes=64) for a in range(2)]
         bias_lo = keep.tile([P, 4], F32, name="bias_lo")
         bias_hi = placed("bias_hi", [P, 4], F32, 56.125)
         bias_rows = keep.tile([P, P], F32, name="bias_rows")
@@ -103,23 +102,25 @@ def tile_list_tsunami_edge_fluxes_kernel(
         bias_turned = psum.tile([P, P], F32, name="bias_turned", tag="bank")
         nc.tensor.transpose(bias_turned[:], bias_rows[:], ident[:])
         nc.scalar.activation(out=bias_lo[:], in_=bias_turned[:, 0:4], func=IDENT)
-        nc.vector.memset(v_sc[0:STAGED, :].bitcast(I32), 0)
+        nc.vector.memset(v_sc[0][0:STAGED, :].bitcast(I32), 0)
+        nc.vector.memset(v_sc[1][:].bitcast(I32), 0)
         nc.vector.memset(pages[0][:], 0.0)
         nc.vector.tensor_copy(out=picked_sc[:], in_=tab_sc[:].indirect(idx[:]))
-        nc.vector.tensor_copy(out=v_sc[STAGED:P, :].bitcast(I32), in_=picked_sc[STAGED:P, :].bitcast(I32))
-        for a, q in [(0, 0), (0, 1), (0, 2), (1, 0), (1, 1), (1, 2), (1, 3)]:
-            row = STAGED + 16 * a + 4 * q
-            queue = nc.gpsimd if a == 0 else nc.scalar
-            queue.dma_start(
-                out=v_sc[32 * q + SCALE_ROW[a] : 32 * q + SCALE_ROW[a] + 4, :].bitcast(I32),
-                in_=picked_sc[row : row + 4, :].bitcast(I32),
-            )
+        nc.vector.tensor_copy(out=v_sc[0][STAGED:P, :].bitcast(I32), in_=picked_sc[STAGED:P, :].bitcast(I32))
+        for a, quadrants in enumerate((3, 4)):
+            for q in range(quadrants):
+                row = STAGED + 16 * a + 4 * q
+                queue = nc.scalar if q < 2 else nc.gpsimd
+                queue.dma_start(
+                    out=v_sc[a][32 * q + SCALE_ROW[a] : 32 * q + SCALE_ROW[a] + 4, :].bitcast(I32),
+                    in_=picked_sc[row : row + 4, :].bitcast(I32),
+                )
         nc.gpsimd.dma_start(out=bias_hi[:], in_=b1[HALF:H].rearrange("(p t) -> p t", t=4))
 
-        load_w1_first(0)
         load_tab(0)
+        for a in range(2):
+            load_w1_first(a)
         load_tab(1)
-        load_w1_first(1)
         nc.sync.dma_start(idx3[:], offs3)
         nc.sync.dma_start(idx4[:], offs4)
 
@@ -165,13 +166,12 @@ def tile_list_tsunami_edge_fluxes_kernel(
         def h_pass(acc, quantised, a, s0, width):
             codes, scales = quantised[a]
             cols = slice(s0, s0 + width)
-            words = v_words0[:, cols] if a == 0 else v_words1[s0 // HALF][:, s0 % HALF : s0 % HALF + width]
             nc.tensor.matmul_mx(
                 out=acc[:],
                 lhsT=codes.bitcast(FP8X4),
                 lhsT_scale=scales,
-                rhs=words.bitcast(FP8X4),
-                rhs_scale=v_sc[SCALE_ROW[a] : P, cols],
+                rhs=v_words[a][:, cols].bitcast(FP8X4),
+                rhs_scale=v_sc[a][SCALE_ROW[a] : P, cols],
                 start=(a == 0),
                 stop=(a == 1),
             )
@@ -196,7 +196,7 @@ def tile_list_tsunami_edge_fluxes_kernel(
         def gather_minus(dst, page, which, m0, width, other):
             nc.vector.tensor_tensor(out=dst, in0=page[:].indirect(which[:, list_cols(m0, width)]), in1=other, op=SUB)
 
-        nc.vector.tensor_copy(out=v_words0[:], in_=tab[0][:].bitcast(U32).indirect(idx[:]))
+        nc.vector.tensor_copy(out=v_words[0][:], in_=tab[0][:].bitcast(U32).indirect(idx[:]))
         for s0 in range(0, S, HALF):
             nc.sync.dma_start(out=wgs_lo[:, s0 : s0 + HALF], in_=wgs[:, s0 : s0 + HALF])
         load_w1_nat(1)
@@ -208,11 +208,9 @@ def tile_list_tsunami_edge_fluxes_kernel(
             acc_first.append(acc)
         h_first = [placed("h_first%d" % c, [P, HALF], F32, kib) for c, kib in enumerate((110, 12))]
         for (s0, width), acc in zip(FIRST_PIECES, acc_first):
-            if s0 % HALF == 0:
-                nc.vector.tensor_copy(
-                    out=v_words1[s0 // HALF][:],
-                    in_=tab[1][:].bitcast(U32).indirect(idx[:, list_cols(s0, HALF)]),
-                )
+            nc.vector.tensor_copy(
+                out=v_words[1][:, s0 : s0 + width], in_=tab[1][:].bitcast(U32).indirect(idx[:, list_cols(s0, width)])
+            )
             h_pass(acc, w1_q[0], 1, s0, width)
             if s0 < HALF:
                 add_bias(h_first[0][:, s0 : s0 + width], acc, bias_lo[:, 0:1])

@@ -52,16 +52,16 @@ def tile_list_tsunami_edge_fluxes_kernel(
         tab = [placed("tab%d" % a, [P, T], I32, 16 * a + LAP) for a in range(2)]
         bstep_lo = [placed("bstep_lo%d" % c, [P, 2, E], F32, kib) for c, kib in enumerate((24, 67 + 3 * LAP))]
         w1_first = [placed("w1_first%d" % a, [P, 4, P], F32, kib) for a, kib in enumerate((57.125, 59.125))]
-        w1_nat = {i: placed("w1_nat%d" % i, [P, 2, 4, P], F32, kib) for i, kib in ((1, 12), (2, 16), (3, 20))}
+        w1_nat = {i: placed("w1_nat%d" % i, [P, 2, 4, P], F32, kib) for i, kib in ((1, 4), (2, 16), (3, 20))}
         w1_hi = placed("w1_hi", [P, 2, 4, HALF], F32, 32)
         wgs_lo = placed("wgs_lo", [P, S], F32, 8)
         v_words = [placed("v_words%d" % a, [P, S], U32, kib) for a, kib in enumerate((132, 48))]
         tab_sc = placed("tab_sc", [P, T], U8, 52.125)
         picked_sc = placed("picked_sc", [P, S], U8, 56.125)
-        wgs_hi = placed("wgs_hi", [P, 4, S], F32, 76 + LAP)
+        wgs_hi = placed("wgs_hi", [P, 4, S], F32, 75.625 - LAP)
         bstep_hi = placed("bstep_hi", [P, 4, E], F32, 94 + LAP)
         w2_w = placed("w2_w", [P, 2, 2 * N], U8, 112 - LAP)
-        pages = [placed("page%d" % i, [P, T2], F32, kib) for i, kib in enumerate((223, 0, 114 + LAP, 124 - LAP))]
+        pages = [placed("page%d" % i, [P, T2], F32, kib) for i, kib in enumerate((223, 114 + LAP, 0, 124 - LAP))]
         le_tail = placed("le_tail", [P, E - TURNED_EDGES], F32, 139.5 + LAP)
         w2_sc = placed("w2_sc", [P, 2, N], U8, 146 + LAP)
         le_col = placed("le_col", [P, DIRECT_SECOND // P], F32, 147 + 3 * LAP)
@@ -95,7 +95,6 @@ def tile_list_tsunami_edge_fluxes_kernel(
             out=tab_sc[STAGED:P, :].bitcast(I32), in_=tab_scales.rearrange("a q t -> (a q) t").bitcast(I32)
         )
         nc.sync.dma_start(idx[:], offs)
-        nc.sync.dma_start(idx2[:], offs2)
         nc.gpsimd.memset(bias_rows[:], 0.0)
         nc.gpsimd.dma_start(out=bias_rows[0:4, :], in_=b1[0:HALF].rearrange("(i p) -> i p", p=P))
         make_identity(nc, ident[:])
@@ -110,17 +109,17 @@ def tile_list_tsunami_edge_fluxes_kernel(
         for a, quadrants in enumerate((3, 4)):
             for q in range(quadrants):
                 row = STAGED + 16 * a + 4 * q
-                queue = nc.scalar if q < 2 else nc.gpsimd
-                queue.dma_start(
+                nc.gpsimd.dma_start(
                     out=v_sc[a][32 * q + SCALE_ROW[a] : 32 * q + SCALE_ROW[a] + 4, :].bitcast(I32),
                     in_=picked_sc[row : row + 4, :].bitcast(I32),
                 )
         nc.gpsimd.dma_start(out=bias_hi[:], in_=b1[HALF:H].rearrange("(p t) -> p t", t=4))
 
-        load_tab(0)
         for a in range(2):
             load_w1_first(a)
-        load_tab(1)
+        for a in range(2):
+            load_tab(a)
+        nc.sync.dma_start(idx2[:], offs2)
         nc.sync.dma_start(idx3[:], offs3)
         nc.sync.dma_start(idx4[:], offs4)
 
@@ -156,8 +155,8 @@ def tile_list_tsunami_edge_fluxes_kernel(
                 in_=w1_first[a][:].rearrange("p j (c i) -> p c j i", i=4),
                 func=IDENT,
             )
-            codes = placed("first_codes%d" % a, [P, P], U32, 75.625 - 0.5 * a)
-            scales = placed("first_scales%d" % a, [P, P], U8, (123, LAP)[a])
+            codes = placed("first_codes%d" % a, [P, P], U32, (92, 75.125)[a])
+            scales = placed("first_scales%d" % a, [P, P], U8, 123 + 0.125 * a)
             nc.vector.quantize_mx(
                 out=codes[:].bitcast(FP8X4), scales=scales[:], in_=grouped[:].rearrange("p c j -> p (c j)")
             )
@@ -196,7 +195,13 @@ def tile_list_tsunami_edge_fluxes_kernel(
         def gather_minus(dst, page, which, m0, width, other):
             nc.vector.tensor_tensor(out=dst, in0=page[:].indirect(which[:, list_cols(m0, width)]), in1=other, op=SUB)
 
-        nc.vector.tensor_copy(out=v_words[0][:], in_=tab[0][:].bitcast(U32).indirect(idx[:]))
+        def gather_words(a, s0, width):
+            nc.vector.tensor_copy(
+                out=v_words[a][:, s0 : s0 + width], in_=tab[a][:].bitcast(U32).indirect(idx[:, list_cols(s0, width)])
+            )
+
+        for s0, width in FIRST_PIECES:
+            gather_words(0, s0, width)
         for s0 in range(0, S, HALF):
             nc.sync.dma_start(out=wgs_lo[:, s0 : s0 + HALF], in_=wgs[:, s0 : s0 + HALF])
         load_w1_nat(1)
@@ -206,11 +211,9 @@ def tile_list_tsunami_edge_fluxes_kernel(
             acc = psum.tile([P, width], F32, name="acc_first", tag="bank")
             h_pass(acc, w1_q[0], 0, s0, width)
             acc_first.append(acc)
-        h_first = [placed("h_first%d" % c, [P, HALF], F32, kib) for c, kib in enumerate((110, 12))]
+        h_first = [placed("h_first%d" % c, [P, HALF], F32, kib) for c, kib in enumerate((110, 4))]
         for (s0, width), acc in zip(FIRST_PIECES, acc_first):
-            nc.vector.tensor_copy(
-                out=v_words[1][:, s0 : s0 + width], in_=tab[1][:].bitcast(U32).indirect(idx[:, list_cols(s0, width)])
-            )
+            gather_words(1, s0, width)
             h_pass(acc, w1_q[0], 1, s0, width)
             if s0 < HALF:
                 add_bias(h_first[0][:, s0 : s0 + width], acc, bias_lo[:, 0:1])
@@ -218,8 +221,6 @@ def tile_list_tsunami_edge_fluxes_kernel(
         def clear_page(i):
             for c0 in range(0, T2, HALF):
                 nc.gpsimd.memset(pages[i][:, c0 : c0 + HALF], 0.0)
-
-        clear_page(1)
 
         load_w1_nat(2)
         load_w1_nat(3)
@@ -235,13 +236,14 @@ def tile_list_tsunami_edge_fluxes_kernel(
         add_bias(h_first[1][:], acc_first[-1], bias_lo[:, 0:1])
         scatter(pages[0], h_first[0][:], wgs_lo, 0, HALF)
         w1_q = w1_q + quantise_w1(1, grouped_second, codes_at=141, scales_at=147)
+        clear_page(1)
         scatter(pages[0], h_first[1][:], wgs_lo, HALF, HALF)
         nc.sync.dma_start(out=bstep_hi[:], in_=bstep[HALF:H, :].rearrange("(p t) m -> p t m", t=4))
         nc.sync.dma_start(out=w2_w[:].bitcast(I32), in_=w2_words.rearrange("a p c -> p a c").bitcast(I32))
         h = {1: make_h(1, w1_q[1], bias_lo[:, 1:2])}
         scatter(pages[1], h[1][:], wgs_lo, 0, S)
 
-        for i in range(2, 4):
+        for i in (3, 2):
             clear_page(i)
         nc.gpsimd.memset(w2_sc[:].rearrange("p a c -> p (a c)").bitcast(I32), 0)
         nc.sync.dma_start(out=le_tail[:], in_=le[TURNED_EDGES:E].partition_broadcast(P))

@@ -109,7 +109,8 @@ def tile_list_tsunami_edge_fluxes_kernel(
         for a, quadrants in enumerate((3, 4)):
             for q in range(quadrants):
                 row = STAGED + 16 * a + 4 * q
-                nc.gpsimd.dma_start(
+                queue = nc.scalar if (a, q) == (0, 0) else nc.gpsimd
+                queue.dma_start(
                     out=v_sc[a][32 * q + SCALE_ROW[a] : 32 * q + SCALE_ROW[a] + 4, :].bitcast(I32),
                     in_=picked_sc[row : row + 4, :].bitcast(I32),
                 )

from contextlib import ExitStack

import concourse.mybir as mybir
from concourse.masks import make_identity

K, T, S, T2, E, H, N = 1024, 4096, 1024, 2048, 1024, 1024, 512
FLOPS = 2 * K * H * S + 2 * H * N * E

F32 = mybir.dt.float32
BF16 = mybir.dt.bfloat16
I32 = mybir.dt.int32
U32 = mybir.dt.uint32
U16 = mybir.dt.uint16
U8 = mybir.dt.uint8
FP8X4 = mybir.dt.float8_e4m3fn_x4
FP4X4 = mybir.dt.float4_e2m1fn_x4
MULT = mybir.AluOpType.mult
SUB = mybir.AluOpType.subtract
IDENT = mybir.ActivationFunctionType.Identity

P = 128
KIB = 1024
HALF = 512
QUARTER = 256
PSUM_BANKS = 8
STAGED = 96
SCALE_ROW = (12, 0)
LAP = 0.0625
FIRST_PIECES = ((0, QUARTER), (QUARTER, QUARTER), (HALF, HALF))
TURNED_EDGES = 5 * P
DIRECT_FIRST, DIRECT_SECOND, DIRECT_LAST = range(TURNED_EDGES, E, P)


def tile_list_tsunami_edge_fluxes_kernel(
    tc, tab_words, tab_scales, offs, w1, b1, wgs, offs2, offs3, offs4, bstep, w2_words, w2_scales, le, out
):
    nc = tc.nc
    with ExitStack() as ctx:
        lists = ctx.enter_context(tc.tile_pool(name="lists", bufs=1))
        keep = ctx.enter_context(tc.tile_pool(name="keep", bufs=1))
        shared = ctx.enter_context(tc.tile_pool(name="shared", bufs=1))
        psum = ctx.enter_context(tc.psum_pool(name="psum", bufs=PSUM_BANKS))

        def placed(name, shape, dtype, kib):
            return shared.tile(shape, dtype, name=name, align_bytes=64, offset=int(kib * KIB))

        idx = lists.tile([P, S // 16], U16, name="idx")
        idx2 = lists.tile([P, S // 16], U16, name="idx2")
        idx3 = lists.tile([P, E // 16], U16, name="idx3")
        idx4 = lists.tile([P, E // 16], U16, name="idx4")

        tab = [placed("tab%d" % a, [P, T], I32, 16 * a + LAP) for a in range(2)]
        bstep_lo = [placed("bstep_lo%d" % c, [P, 2, E], F32, kib) for c, kib in enumerate((24, 67 + 3 * LAP))]
        w1_first = [placed("w1_first%d" % a, [P, 4, P], F32, kib) for a, kib in enumerate((57.125, 59.125))]
        w1_nat = {i: placed("w1_nat%d" % i, [P, 2, 4, P], F32, kib) for i, kib in ((1, 4), (2, 16), (3, 20))}
        w1_hi = placed("w1_hi", [P, 2, 4, HALF], F32, 32)
        wgs_lo = placed("wgs_lo", [P, S], F32, 8)
        v_words = [placed("v_words%d" % a, [P, S], U32, kib) for a, kib in enumerate((132, 48))]
        tab_sc = placed("tab_sc", [P, T], U8, 52.125)
        picked_sc = placed("picked_sc", [P, S], U8, 56.125)
        wgs_hi = placed("wgs_hi", [P, 4, S], F32, 75.625 - LAP)
        bstep_hi = placed("bstep_hi", [P, 4, E], F32, 94 + LAP)
        w2_w = placed("w2_w", [P, 2, 2 * N], U8, 112 - LAP)
        pages = [placed("page%d" % i, [P, T2], F32, kib) for i, kib in enumerate((223, 114 + LAP, 0, 124 - LAP))]
        le_tail = placed("le_tail", [P, E - TURNED_EDGES], F32, 139.5 + LAP)
        w2_sc = placed("w2_sc", [P, 2, N], U8, 146 + LAP)
        le_col = placed("le_col", [P, DIRECT_SECOND // P], F32, 147 + 3 * LAP)
        v_sc = [keep.tile([P, S], U8, name="v_sc%d" % a, align_bytes=64) for a in range(2)]
        bias_lo = keep.tile([P, 4], F32, name="bias_lo")
        bias_hi = placed("bias_hi", [P, 4], F32, 56.125)
        bias_rows = keep.tile([P, P], F32, name="bias_rows")
        ident = keep.tile([P, P], F32, name="ident")

        def load_w1_nat(i):
            for a in range(2):
                rows = w1[HALF * a : HALF * (a + 1), P * i : P * (i + 1)]
                nc.sync.dma_start(out=w1_nat[i][:, a], in_=rows.rearrange("(p j) c -> p j c", j=4))

        def load_w1_first(a):
            rows = w1[HALF * a : HALF * (a + 1), 0:P]
            nc.sync.dma_start(out=w1_first[a][:], in_=rows.rearrange("(p j) c -> p j c", j=4))

        def load_tab(a):
            nc.sync.dma_start(out=tab[a][:], in_=tab_words[a].rearrange("p t i -> p (t i)").bitcast(I32))

        def load_bstep_lo(c):
            rows = bstep[QUARTER * c : QUARTER * (c + 1), :]
            nc.sync.dma_start(out=bstep_lo[c][:], in_=rows.rearrange("(i p) m -> p i m", p=P))

        def list_cols(first, count):
            return slice(first // 16, (first + count) // 16)

        nc.vector.memset(tab_sc[0:STAGED, :].bitcast(I32), 0)
        nc.sync.dma_start(
            out=tab_sc[STAGED:P, :].bitcast(I32), in_=tab_scales.rearrange("a q t -> (a q) t").bitcast(I32)
        )
        nc.sync.dma_start(idx[:], offs)
        nc.gpsimd.memset(bias_rows[:], 0.0)
        nc.gpsimd.dma_start(out=bias_rows[0:4, :], in_=b1[0:HALF].rearrange("(i p) -> i p", p=P))
        make_identity(nc, ident[:])
        bias_turned = psum.tile([P, P], F32, name="bias_turned", tag="bank")
        nc.tensor.transpose(bias_turned[:], bias_rows[:], ident[:])
        nc.scalar.activation(out=bias_lo[:], in_=bias_turned[:, 0:4], func=IDENT)
        nc.vector.memset(v_sc[0][0:STAGED, :].bitcast(I32), 0)
        nc.vector.memset(v_sc[1][:].bitcast(I32), 0)
        nc.vector.memset(pages[0][:], 0.0)
        nc.vector.tensor_copy(out=picked_sc[:], in_=tab_sc[:].indirect(idx[:]))
        nc.vector.tensor_copy(out=v_sc[0][STAGED:P, :].bitcast(I32), in_=picked_sc[STAGED:P, :].bitcast(I32))
        for a, quadrants in enumerate((3, 4)):
            for q in range(quadrants):
                row = STAGED + 16 * a + 4 * q
                queue = nc.scalar if (a, q) == (0, 0) else nc.gpsimd
                queue.dma_start(
                    out=v_sc[a][32 * q + SCALE_ROW[a] : 32 * q + SCALE_ROW[a] + 4, :].bitcast(I32),
                    in_=picked_sc[row : row + 4, :].bitcast(I32),
                )
        nc.gpsimd.dma_start(out=bias_hi[:], in_=b1[HALF:H].rearrange("(p t) -> p t", t=4))

        for a in range(2):
            load_w1_first(a)
        for a in range(2):
            load_tab(a)
        nc.sync.dma_start(idx2[:], offs2)
        nc.sync.dma_start(idx3[:], offs3)
        nc.sync.dma_start(idx4[:], offs4)

        def cast_w1(first, count, grouped_at):
            grouped = placed("w1_grouped%d" % first, [P, count, 2, P, 4], BF16, grouped_at)
            for i in range(count):
                for a in range(2):
                    nc.scalar.activation(
                        out=grouped[:, i, a].rearrange("p (c i) j -> p c j i", i=4),
                        in_=w1_nat[first + i][:, a].rearrange("p j (c i) -> p c j i", i=4),
                        func=IDENT,
                    )
            return grouped

        def by_pass(codes, scales):
            return [(codes[:, P * a : P * (a + 1)], scales[:, P * a : P * (a + 1)]) for a in range(2)]

        def quantise_w1(first, grouped, codes_at, scales_at):
            count = grouped.shape[1]
            codes = placed("w1_codes%d" % first, [P, count, 2 * P], U32, codes_at)
            scales = placed("w1_scales%d" % first, [P, count, 2 * P], U8, scales_at)
            nc.vector.quantize_mx(
                out=codes[:].rearrange("p i c -> p (i c)").bitcast(FP8X4),
                scales=scales[:].rearrange("p i c -> p (i c)"),
                in_=grouped[:].rearrange("p i a c j -> p (i a c j)"),
            )
            return [by_pass(codes[:, i], scales[:, i]) for i in range(count)]

        def quantise_first(a):
            grouped = placed("first_grouped%d" % a, [P, P, 4], BF16, 65.125 + a)
            nc.scalar.activation(
                out=grouped[:].rearrange("p (c i) j -> p c j i", i=4),
                in_=w1_first[a][:].rearrange("p j (c i) -> p c j i", i=4),
                func=IDENT,
            )
            codes = placed("first_codes%d" % a, [P, P], U32, (92, 75.125)[a])
            scales = placed("first_scales%d" % a, [P, P], U8, 123 + 0.125 * a)
            nc.vector.quantize_mx(
                out=codes[:].bitcast(FP8X4), scales=scales[:], in_=grouped[:].rearrange("p c j -> p (c j)")
            )
            return codes[:], scales[:]

        def h_pass(acc, quantised, a, s0, width):
            codes, scales = quantised[a]
            cols = slice(s0, s0 + width)
            nc.tensor.matmul_mx(
                out=acc[:],
                lhsT=codes.bitcast(FP8X4),
                lhsT_scale=scales,
                rhs=v_words[a][:, cols].bitcast(FP8X4),
                rhs_scale=v_sc[a][SCALE_ROW[a] : P, cols],
                start=(a == 0),
                stop=(a == 1),
            )

        def add_bias(dst, acc, bias):
            nc.scalar.activation(out=dst, in_=acc[:], func=IDENT, bias=bias)

        def make_h(i, quantised, bias):
            h = placed("h%d" % i, [P, S], F32, (204.5, 52.125, 57.125, 61.125)[i % 4])
            for s0 in range(0, S, HALF):
                acc = psum.tile([P, HALF], F32, name="acc_h", tag="bank")
                for a in range(2):
                    h_pass(acc, quantised, a, s0, HALF)
                add_bias(h[:, s0 : s0 + HALF], acc, bias)
            return h

        def scatter(page, h, weights, s0, width):
            nc.vector.tensor_tensor(
                out=page[:].indirect(idx2[:, list_cols(s0, width)]), in0=h, in1=weights[:, s0 : s0 + width], op=MULT
            )

        def gather_minus(dst, page, which, m0, width, other):
            nc.vector.tensor_tensor(out=dst, in0=page[:].indirect(which[:, list_cols(m0, width)]), in1=other, op=SUB)

        def gather_words(a, s0, width):
            nc.vector.tensor_copy(
                out=v_words[a][:, s0 : s0 + width], in_=tab[a][:].bitcast(U32).indirect(idx[:, list_cols(s0, width)])
            )

        for s0, width in FIRST_PIECES:
            gather_words(0, s0, width)
        for s0 in range(0, S, HALF):
            nc.sync.dma_start(out=wgs_lo[:, s0 : s0 + HALF], in_=wgs[:, s0 : s0 + HALF])
        load_w1_nat(1)
        w1_q = [[quantise_first(a) for a in range(2)]]
        acc_first = []
        for s0, width in FIRST_PIECES:
            acc = psum.tile([P, width], F32, name="acc_first", tag="bank")
            h_pass(acc, w1_q[0], 0, s0, width)
            acc_first.append(acc)
        h_first = [placed("h_first%d" % c, [P, HALF], F32, kib) for c, kib in enumerate((110, 4))]
        for (s0, width), acc in zip(FIRST_PIECES, acc_first):
            gather_words(1, s0, width)
            h_pass(acc, w1_q[0], 1, s0, width)
            if s0 < HALF:
                add_bias(h_first[0][:, s0 : s0 + width], acc, bias_lo[:, 0:1])

        def clear_page(i):
            for c0 in range(0, T2, HALF):
                nc.gpsimd.memset(pages[i][:, c0 : c0 + HALF], 0.0)

        load_w1_nat(2)
        load_w1_nat(3)
        load_bstep_lo(0)
        for a in range(2):
            rows = w1[HALF * a : HALF * (a + 1), HALF:H]
            nc.sync.dma_start(out=w1_hi[:, a], in_=rows.rearrange("(p j) c -> p j c", j=4))
        load_bstep_lo(1)
        for q in range(4):
            nc.sync.dma_start(out=wgs_hi[32 * q : 32 * (q + 1)], in_=wgs.rearrange("(p t) j -> p t j", t=4))

        grouped_second = cast_w1(1, 1, grouped_at=122)
        add_bias(h_first[1][:], acc_first[-1], bias_lo[:, 0:1])
        scatter(pages[0], h_first[0][:], wgs_lo, 0, HALF)
        w1_q = w1_q + quantise_w1(1, grouped_second, codes_at=141, scales_at=147)
        clear_page(1)
        scatter(pages[0], h_first[1][:], wgs_lo, HALF, HALF)
        nc.sync.dma_start(out=bstep_hi[:], in_=bstep[HALF:H, :].rearrange("(p t) m -> p t m", t=4))
        nc.sync.dma_start(out=w2_w[:].bitcast(I32), in_=w2_words.rearrange("a p c -> p a c").bitcast(I32))
        h = {1: make_h(1, w1_q[1], bias_lo[:, 1:2])}
        scatter(pages[1], h[1][:], wgs_lo, 0, S)

        for i in (3, 2):
            clear_page(i)
        nc.gpsimd.memset(w2_sc[:].rearrange("p a c -> p (a c)").bitcast(I32), 0)
        nc.sync.dma_start(out=le_tail[:], in_=le[TURNED_EDGES:E].partition_broadcast(P))
        with nc.allow_non_contiguous_dma(reason="one length factor a partition"):
            nc.sync.dma_start(out=le_col[:], in_=le[0:DIRECT_SECOND].rearrange("(c p) -> p c", p=P))
        for q in range(4):
            nc.sync.dma_start(
                out=w2_sc[32 * q : 32 * q + 4].bitcast(I32),
                in_=w2_scales[:, 4 * q : 4 * q + 4, :].rearrange("a r c -> r a c").bitcast(I32),
            )

        w1_q = w1_q + quantise_w1(2, cast_w1(2, 2, grouped_at=142 - LAP), codes_at=147.5, scales_at=149.5)
        for i in range(2, 4):
            h[i] = make_h(i, w1_q[i], bias_lo[:, i : i + 1])

        z_lo = placed("z_lo", [P, 4, E], F32, 179)

        def gather_lo(first):
            y = [placed("y_lo%d" % (first + c), [P, E], F32, 171 + 4 * c) for c in range(2)]
            for c in range(2):
                gather_minus(y[c][:], pages[c], idx3, 0, E, bstep_lo[first // 2][:, c, :])
            for c in range(2):
                i = first + c
                z_nat = placed("z_nat%d" % i, [P, E], F32, (142 - LAP, 158, 150, 162)[i])
                gather_minus(z_nat[:], pages[c], idx4, 0, E, y[c][:])
                for t in range(4):
                    nc.sync.dma_start(out=z_lo[32 * i : 32 * (i + 1), t, :], in_=z_nat[t:P:4, :])

        gather_lo(0)

        grouped_hi = placed("grouped_hi", [P, 4, 2, P, 4], BF16, 150)
        for a in range(2):
            nc.scalar.activation(
                out=grouped_hi[:].rearrange("p t a c j -> p a c t j")[:, a],
                in_=w1_hi[:, a].rearrange("p j (c t) -> p c t j", t=4),
                func=IDENT,
            )
        for c in range(2):
            scatter(pages[c], h[2 + c][:], wgs_lo, 0, S)
        codes_hi = placed("codes_hi", [P, 4, 2 * P], U32, 166)
        scales_hi = placed("scales_hi", [P, 4, 2 * P], U8, 170)
        nc.vector.quantize_mx(
            out=codes_hi[:].rearrange("p t c -> p (t c)").bitcast(FP8X4),
            scales=scales_hi[:].rearrange("p t c -> p (t c)"),
            in_=grouped_hi[:].rearrange("p t a c j -> p (t a c j)"),
        )
        h_hi = [make_h(4 + t, by_pass(codes_hi[:, t], scales_hi[:, t]), bias_hi[:, t : t + 1]) for t in range(4)]
        gather_lo(2)
        pages_hi = pages[2:] + pages[:2]
        for t in range(4):
            scatter(pages_hi[t], h_hi[t][:], wgs_hi[:, t, :], 0, S)

        def interleave_z(src, grouped):
            nc.scalar.activation(
                out=grouped[:].rearrange("p (c i) t -> p c t i", i=4),
                in_=src.rearrange("p t (c i) -> p c t i", i=4),
                func=IDENT,
            )

        codes_lo = placed("z_codes0", [P, E], U32, 195)
        scales_lo = placed("z_scales0", [P, E], U8, 199)

        def quantise_z(grouped, codes, scales):
            nc.vector.quantize_mx(out=codes.bitcast(FP8X4), scales=scales, in_=grouped[:].rearrange("p m t -> p (m t)"))

        for c, m0 in enumerate(range(0, E, HALF)):
            grouped_lo = placed("zg_lo%d" % c, [P, HALF, 4], BF16, 32 + 4 * c)
            interleave_z(z_lo[:, :, m0 : m0 + HALF], grouped_lo)
            quantise_z(grouped_lo, codes_lo[:, m0 : m0 + HALF], scales_lo[:, m0 : m0 + HALF])

        out_v = out.rearrange("(b p) m -> p b m", p=P)

        def direct_pass(acc, a, codes, scales, b0=0):
            count = acc.shape[1]
            for b in range(b0, b0 + count):
                nc.tensor.matmul_mx(
                    out=acc[:, b - b0, :],
                    lhsT=w2_w[:, a, 2 * P * b : 2 * P * (b + 1)].bitcast(FP4X4),
                    lhsT_scale=w2_sc[:, a, P * b : P * (b + 1)],
                    rhs=codes.bitcast(FP8X4),
                    rhs_scale=scales,
                    start=(a == 0 and b == b0),
                    stop=(a == 1 and b == b0 + count - 1),
                )

        def open_direct(m0, b0, count):
            acc = psum.tile([P, count, P], F32, name="acc_direct", tag="bank")
            direct_pass(acc, 0, codes_lo[:, m0 : m0 + P], scales_lo[:, m0 : m0 + P], b0)
            return acc

        acc_direct_first = open_direct(DIRECT_FIRST, 2, 2)
        acc_direct_second = open_direct(DIRECT_SECOND, 0, 4)
        acc_last_low = open_direct(DIRECT_LAST, 0, 2)

        def gather_left(m0, tiles, at=16):
            y = [placed("y_hi%d_%d" % (m0, t), [P, QUARTER], F32, at + t) for t in tiles]
            for t, part in zip(tiles, y):
                gather_minus(part[:], pages_hi[t], idx3, m0, QUARTER, bstep_hi[:, t, m0 : m0 + QUARTER])
            return y

        def gather_right(m0, width, y, z_at):
            z_hi = placed("z_hi%d" % m0, [P, 4, width], F32, z_at)
            for t in range(4):
                gather_minus(z_hi[:, t, :], pages_hi[t], idx4, m0, width, y[t])
            return z_hi

        def group_hi(c, z_hi, at):
            grouped = placed("zg_hi%d" % c, [P, z_hi.shape[2], 4], BF16, at)
            interleave_z(z_hi[:], grouped)
            return grouped

        def right_chunk(c, y):
            return group_hi(c, gather_right(QUARTER * c, QUARTER, [part[:] for part in y], 179), 209 + 2 * (c % 2))

        def quantise_hi(m0, grouped):
            width = grouped.shape[1]
            codes = placed("zc_hi%d" % m0, [P, width], U32, 200 + m0 / 256)
            scales = placed("zs_hi%d" % m0, [P, width], U8, 221 + m0 / 1024)
            quantise_z(grouped, codes[:], scales[:])
            return codes, scales

        def turned_pass(acc, a, codes, scales):
            columns = acc.shape[1]
            nc.tensor.matmul_mx(
                out=acc[:],
                lhsT=codes.bitcast(FP8X4),
                lhsT_scale=scales,
                rhs=w2_w[:, a, 0 : 2 * columns].bitcast(FP4X4),
                rhs_scale=w2_sc[:, a, 0:columns],
                start=(a == 0),
                stop=(a == 1),
            )

        def open_turned(m0, columns=N):
            acc = psum.tile([P, columns], F32, name="acc_turned", tag="bank")
            turned_pass(acc, 0, codes_lo[:, m0 : m0 + P], scales_lo[:, m0 : m0 + P])
            return acc

        def multiply_chunk(m0, grouped):
            codes, scales = quantise_hi(m0, grouped)
            banks = []
            for j in range(QUARTER // P):
                acc = open_turned(m0 + P * j)
                turned_pass(acc, 1, codes[:, P * j : P * (j + 1)], scales[:, P * j : P * (j + 1)])
                banks.append(acc)
            return banks

        def scale_and_turn(m0, banks):
            turned = []
            for j, acc in enumerate(banks):
                block = m0 // P + j
                ranges = acc.shape[1] // P
                scaled = placed("scaled%d" % block, [P, ranges * P], F32, 213 + 2 * (block % 4))
                nc.scalar.activation(out=scaled[:], in_=acc[:], func=IDENT, scale=le_col[:, block : block + 1])
                back = psum.tile([P, ranges, P], F32, name="acc_back", tag="bank")
                for b in range(ranges):
                    nc.tensor.transpose(back[:, b, :], scaled[:, P * b : P * (b + 1)], ident[:])
                turned.append(back)
            return turned

        def store_turned(m0, turned, at):
            width = P * len(turned)
            ranges = turned[0].shape[1]
            res = placed("res%d" % m0, [P, ranges, width], F32, at)
            for j, back in enumerate(turned):
                nc.scalar.copy(out=res[:, :, P * j : P * (j + 1)], in_=back[:])
            nc.sync.dma_start(out=out_v[:, 0:ranges, m0 : m0 + width], in_=res[:])

        def store_direct(m0, b0, acc, at, queue):
            count = acc.shape[1]
            res = placed("res%d_%d" % (m0, b0), [P, count, P], F32, at)
            factors = le_tail[:, m0 - TURNED_EDGES : m0 - TURNED_EDGES + P].unsqueeze(1).to_broadcast([P, count, P])
            nc.vector.tensor_tensor(out=res[:], in0=acc, in1=factors, op=MULT)
            queue.dma_start(out=out_v[:, b0 : b0 + count, m0 : m0 + P], in_=res[:])

        acc_last_turned = open_turned(HALF)
        grouped = right_chunk(0, gather_left(0, range(4)))

        y = gather_left(QUARTER, range(4))
        turned0 = scale_and_turn(0, multiply_chunk(0, grouped))
        grouped = right_chunk(1, y)

        y = gather_left(HALF, range(4))
        banks = multiply_chunk(QUARTER, grouped)
        store_turned(0, turned0, at=24)
        turned1 = scale_and_turn(QUARTER, banks)
        grouped = right_chunk(2, y)

        y = gather_left(DIRECT_SECOND, range(3))
        codes, scales = quantise_hi(HALF, grouped)
        turned_pass(acc_last_turned, 1, codes[:, 0:P], scales[:, 0:P])
        store_turned(QUARTER, turned1, at=28)
        acc_half_turned = open_turned(DIRECT_FIRST, QUARTER)
        turned_pass(acc_half_turned, 1, codes[:, P:], scales[:, P:])
        direct_pass(acc_direct_first, 1, codes[:, P:], scales[:, P:], 2)
        turned2 = scale_and_turn(HALF, [acc_last_turned])
        turned3 = scale_and_turn(DIRECT_FIRST, [acc_half_turned])
        acc_last_high = open_direct(DIRECT_LAST, 2, 2)
        y = y + gather_left(DIRECT_SECOND, range(3, 4), at=178)

        z_second = gather_right(DIRECT_SECOND, P, [part[:, 0:P] for part in y], 179)
        z_last = gather_right(DIRECT_LAST, P, [part[:, P : 2 * P] for part in y], 182)

        codes, scales = quantise_hi(DIRECT_SECOND, group_hi(3, z_second, 147.125))
        direct_pass(acc_direct_second, 1, codes[:], scales[:])
        store_turned(HALF, turned2, at=40)
        grouped = group_hi(4, z_last, 213)
        store_direct(DIRECT_FIRST, 2, acc_direct_first[:], 179, nc.sync)
        store_turned(DIRECT_FIRST, turned3, at=42)
        codes, scales = quantise_hi(DIRECT_LAST, grouped)
        direct_pass(acc_last_low, 1, codes[:], scales[:], 0)
        direct_pass(acc_last_high, 1, codes[:], scales[:], 2)
        store_direct(DIRECT_SECOND, 0, acc_direct_second[:, 0:2, :], 182, nc.sync)
        store_direct(DIRECT_SECOND, 2, acc_direct_second[:, 2:4, :], 183, nc.scalar)
        store_direct(DIRECT_LAST, 0, acc_last_low[:], 46, nc.sync)
        store_direct(DIRECT_LAST, 2, acc_last_high[:, 0:1, :], 47, nc.scalar)
        store_direct(DIRECT_LAST, 3, acc_last_high[:, 1:2, :], 47.5, nc.sync)
